import numpy as np
import ml_dtypes


def mxq(x, axis, fmt="e4m3"):
    dtype, down = {"e4m3": (ml_dtypes.float8_e4m3fn, 7), "e5m2": (ml_dtypes.float8_e5m2, 14)}[fmt]
    v = np.moveaxis(np.asarray(x, np.float32).astype(ml_dtypes.bfloat16).astype(np.float64), axis, -1)
    blocks = v.reshape(v.shape[:-1] + (-1, 32))
    amax = np.abs(blocks).max(-1, keepdims=True)
    byte = np.maximum(np.where(amax > 0, np.frexp(amax)[1] - 1 + 127, 0) - down, 1)
    scale = np.exp2(byte - 127.0)
    codes = (blocks / scale).astype(np.float32).astype(dtype).astype(np.float64)
    return np.moveaxis((codes * scale).reshape(v.shape), -1, axis)


WIDE = False


def mx_kscale(k):
    if not WIDE:
        return np.ones(k)
    levels = np.array([10, -10, 5, -5, 0])
    if k % 512:
        return np.exp2(np.random.permutation(np.resize(levels, k // 32))).repeat(32)
    a = np.empty((k // 512, 16))
    for p in range(k // 512):
        a[p, :8] = np.random.permutation(np.resize(levels, 8))
        for g in range(8):
            far = levels[np.abs(levels - a[p, g]) >= 10]
            a[p, g + 8] = far[np.random.randint(len(far))]
    return np.exp2(a.ravel()).repeat(32)


def f64(x):
    return np.asarray(x).astype(np.float64)


def striped(idx):
    return np.tile(idx.reshape(-1, 16).T, (8, 1)).astype(np.uint16)


def unstriped(offs):
    return offs[:16].T.reshape(-1).astype(np.int64)


E2M1 = np.array([0.0, 0.5, 1.0, 1.5, 2.0, 3.0, 4.0, 6.0, -0.0, -0.5, -1.0, -1.5, -2.0, -3.0, -4.0, -6.0])


def pack_weight(w, fmt):
    k, n = w.shape
    w = f64(np.asarray(w, np.float32).astype(ml_dtypes.bfloat16)).reshape(k // 32, 32, n)
    amax = np.abs(w).max(1)
    if fmt == "e4m3":
        byte = np.frexp(amax)[1] - 1 + 127 - 7
    else:
        mant, ex = np.frexp(amax / 6.0)
        byte = np.where(mant > 0.5, ex, ex - 1) + 127
    byte = np.clip(np.where(amax > 0, byte, 1), 1, 254)
    scaled = (w * np.exp2(127.0 - byte)[:, None, :]).reshape(k, n).astype(np.float32)
    by_word = np.ascontiguousarray(scaled.reshape(k // 512, 128, 4, n).transpose(0, 1, 3, 2))
    if fmt == "e4m3":
        words = by_word.astype(ml_dtypes.float8_e4m3fn).view(np.uint8)
    else:
        c = by_word.astype(ml_dtypes.float4_e2m1fn).view(np.uint8) & 0xF
        words = (c[..., 0::2] | (c[..., 1::2] << 4)).reshape(k // 512, 128, 2 * n)
    return np.ascontiguousarray(words), np.ascontiguousarray(byte.astype(np.uint8).reshape(k // 512, 16, n))


def unpack_weight(words, scales, fmt):
    g, _, n = scales.shape
    words = np.ascontiguousarray(words).reshape(g, 128, n, -1)
    if fmt == "e4m3":
        vals = words.view(ml_dtypes.float8_e4m3fn).astype(np.float64)
    else:
        nib = np.empty((g, 128, n, 4), np.uint8)
        nib[..., 0::2] = words & 0xF
        nib[..., 1::2] = words >> 4
        vals = E2M1[nib]
    vals = vals * np.repeat(np.exp2(scales.astype(np.float64) - 127.0), 8, axis=1)[..., None]
    return vals.transpose(0, 1, 3, 2).reshape(g * 512, n)


def silu(v):
    return v / (1.0 + np.exp(-np.maximum(v, -700.0)))


K, T, G, C1, E, C2, H = 1024, 1024, 2, 512, 8, 128, 512
N = 128


def by_expert(wq, xq, E, C):
    return np.concatenate([wq[e].T @ xq[:, e * C:(e + 1) * C] for e in range(E)], axis=1)


def setup_inputs():
    n = np.random.standard_normal
    s = mx_kscale(K)
    u = mx_kscale(H)
    slots1 = np.random.permutation(T)
    slots2 = np.concatenate([q * C1 + np.random.permutation(C1) for q in range(G)])
    x = pack_weight(n((K, T)) * s[:, None], "e4m3")
    wg = [pack_weight(m, "e2m1") for m in n((G, K, H)) / np.sqrt(K) / s[None, :, None] * u]
    we = [pack_weight(m, "e4m3") for m in n((E, H, N)) / np.sqrt(H) / u[None, :, None]]
    return {
        "x_words": x[0],
        "x_scales": x[1],
        "wg_words": np.stack([m[0] for m in wg]),
        "wg_scales": np.stack([m[1] for m in wg]),
        "we_words": np.stack([m[0] for m in we]),
        "we_scales": np.stack([m[1] for m in we]),
        "gate": (np.tile(np.random.uniform(0.2, 1.0, T), (128, 1))).astype(np.float32),
        "offs": striped(slots1),
        "offs2": striped(slots2),
        "dst": striped(slots1[slots2]),
    }


def reference(x_words, x_scales, wg_words, wg_scales, we_words, we_scales, gate, offs, offs2, dst):
    wg = np.stack([unpack_weight(wg_words[e], wg_scales[e], "e2m1") for e in range(G)])
    we = np.stack([unpack_weight(we_words[e], we_scales[e], "e4m3") for e in range(E)])
    idx, idx2 = unstriped(offs), unstriped(offs2)
    xq = unpack_weight(x_words, x_scales, "e4m3")[:, idx]
    a = silu(by_expert(wg, xq, G, C1))
    y = by_expert(we, mxq(a[:, idx2], 0, "e4m3"), E, C2)
    out = np.zeros((N, T))
    out[:, unstriped(dst)] = f64(gate[:1]) * y
    return out

@@ -1,0 +1,201 @@
+from contextlib import ExitStack
+
+import concourse.mybir as mybir
+from concourse.masks import make_identity
+
+K, T, G, C1, E, C2, H, N = 1024, 1024, 2, 512, 8, 128, 512, 128
+FLOPS = 2 * K * H * T + 2 * H * N * T
+
+F32 = mybir.dt.float32
+BF16 = mybir.dt.bfloat16
+I32 = mybir.dt.int32
+U32 = mybir.dt.uint32
+U16 = mybir.dt.uint16
+U8 = mybir.dt.uint8
+FP8X4 = mybir.dt.float8_e4m3fn_x4
+FP4X4 = mybir.dt.float4_e2m1fn_x4
+SILU = mybir.ActivationFunctionType.Silu
+MULT = mybir.AluOpType.mult
+
+P = 128
+PASSES = K // 512
+PIECE = 256
+PIECES = T // PIECE
+LANES = 16
+
+
+def entries(offsets, first, count):
+    return offsets[:, first // LANES : (first + count) // LANES]
+
+
+def tile_moe_hie_silu_kernel(
+    tc, x_words, x_scales, wg_words, wg_scales, we_words, we_scales, gate, offs, offs2, dst, out
+):
+    nc = tc.nc
+    with ExitStack() as ctx:
+        lists = ctx.enter_context(tc.tile_pool(name="lists", bufs=1))
+        keep = ctx.enter_context(tc.tile_pool(name="keep", bufs=1))
+        ring = ctx.enter_context(tc.tile_pool(name="ring", bufs=4))
+        psum = ctx.enter_context(tc.psum_pool(name="psum", bufs=1))
+
+        token_of = lists.tile([P, T // LANES], U16, name="token_of")
+        slot_of = lists.tile([P, T // LANES], U16, name="slot_of")
+        column_of = lists.tile([P, T // LANES], U16, name="column_of")
+
+        xs = keep.tile([P, PASSES * T], U8, name="xs", align_bytes=64)
+        wgs = keep.tile([P, G * PASSES * H], U8, name="wgs", align_bytes=64)
+        wes = keep.tile([P, E * N], U8, name="wes", align_bytes=64)
+        nc.gpsimd.memset(xs[:].bitcast(I32), 0)
+        nc.vector.memset(wgs[:].bitcast(I32), 0)
+        nc.vector.memset(wes[:].bitcast(I32), 0)
+
+        nc.sync.dma_start(slot_of[:], offs2)
+        nc.sync.dma_start(column_of[:], dst)
+        for q in range(4):
+            nc.sync.dma_start(
+                xs[32 * q : 32 * q + 4, :].bitcast(I32).rearrange("r (s t) -> r s t", s=PASSES),
+                x_scales[:, 4 * q : 4 * q + 4, :].bitcast(I32).rearrange("s r t -> r s t"),
+            )
+        nc.sync.dma_start(token_of[:], offs)
+        xw = keep.tile([P, PASSES * T], I32, name="xw", align_bytes=64)
+        nc.scalar.dma_start(
+            xw[:].rearrange("p (s t) -> p s t", s=PASSES),
+            x_words.rearrange("s p t d -> p s (t d)").bitcast(I32),
+        )
+        wgw = []
+        for f in range(G):
+            words = keep.tile([P, PASSES * 2 * H], U8, name=f"wgw{f}", align_bytes=64)
+            nc.sync.dma_start(
+                words[:].bitcast(I32).rearrange("p (s b) -> p s b", s=PASSES),
+                wg_words[f].bitcast(I32).rearrange("s p b -> p s b"),
+            )
+            wgw.append(words)
+            if f == 0:
+                for q in range(4):
+                    nc.sync.dma_start(
+                        wgs[32 * q : 32 * q + 4, :].bitcast(I32).rearrange("r (c i) -> r c i", c=G * PASSES),
+                        wg_scales[:, :, 4 * q : 4 * q + 4, :].bitcast(I32).rearrange("f s r i -> r (f s) i"),
+                    )
+        for q in range(4):
+            nc.sync.dma_start(
+                wes[32 * q : 32 * q + 4, :].bitcast(I32).rearrange("r (e n) -> r e n", e=E),
+                we_scales[:, 0, 4 * q : 4 * q + 4, :].bitcast(I32).rearrange("e r n -> r e n"),
+            )
+
+        identity = keep.tile([P, P], F32, name="identity")
+        make_identity(nc, identity[:])
+
+        pairs = keep.tile([P, G * 2 * C1], F32, name="pairs", align_bytes=64)
+        slot_words, slot_scales = {}, {}
+
+        def gather_scales(f):
+            for s in range(PASSES):
+                t = keep.tile([P, C1], U8, name=f"slot_scales{f}{s}", align_bytes=64)
+                nc.vector.tensor_copy(t[:], xs[:, s * T : (s + 1) * T].indirect(entries(token_of, f * C1, C1)))
+                slot_scales[f, s] = t
+
+        def gather_words(c):
+            for s in range(PASSES):
+                t = keep.tile([P, PIECE], U32, name=f"slot_words{c}{s}", align_bytes=64)
+                nc.vector.tensor_copy(t[:], xw[:, s * T : (s + 1) * T].bitcast(U32).indirect(entries(token_of, c * PIECE, PIECE)))
+                slot_words[c, s] = t
+
+        hidden = {}
+
+        def group_layer(c):
+            f = c * PIECE // C1
+            for b in range(PIECE // P):
+                acc = psum.tile([P, H], F32, name="acc", tag=f"bank{2 * c + b}")
+                first = c * PIECE % C1 + b * P
+                for s in range(PASSES):
+                    nc.tensor.matmul_mx(
+                        acc[:],
+                        lhsT=slot_words[c, s][:, b * P : (b + 1) * P].bitcast(FP8X4),
+                        lhsT_scale=slot_scales[f, s][:, first : first + P],
+                        rhs=wgw[f][:, s * 2 * H : (s + 1) * 2 * H].bitcast(FP4X4),
+                        rhs_scale=wgs[:, (f * PASSES + s) * H : (f * PASSES + s + 1) * H],
+                        start=(s == 0),
+                        stop=(s == PASSES - 1),
+                    )
+                h = ring.tile([P, H], BF16, name="h", align_bytes=64)
+                nc.scalar.activation(
+                    h[:].rearrange("j (u p e) -> j u p e", u=2, e=2),
+                    acc[:].rearrange("j (p u e) -> j u p e", u=2, e=2),
+                    SILU,
+                )
+                hidden[c, b] = h
+
+        def turn(f):
+            for u in range(2):
+                plane = pairs[:, (2 * f + u) * C1 : (2 * f + u + 1) * C1].rearrange("p (c b j) -> p c b j", c=2, b=2)
+                for b in range(2):
+                    turned = psum.tile([P, 2, P], F32, name="turned", tag=f"bank{(4 * (f + 1) + 2 * u + b) % 8}")
+                    for c in range(2):
+                        nc.tensor.transpose(
+                            turned[:, c, :],
+                            hidden[2 * f + c, b][:].bitcast(F32)[:, u * P : (u + 1) * P],
+                            identity[:],
+                        )
+                    nc.scalar.copy(plane[:, :, b, :], turned[:])
+
+        for f in range(G):
+            gather_scales(f)
+            for c in range(2 * f, 2 * f + 2):
+                gather_words(c)
+                group_layer(c)
+            turn(f)
+
+        wew = keep.tile([P, E * N], I32, name="wew", align_bytes=64)
+        nc.sync.dma_start(
+            wew[:].rearrange("p (e n) -> p e n", e=E),
+            we_words.rearrange("e s p n d -> p (e s) (n d)").bitcast(I32),
+        )
+        weight = keep.tile([P, T], F32, name="weight", align_bytes=64)
+        nc.sync.dma_start(weight[:], gate)
+
+        grouped, results = {}, {}
+
+        def gather_hidden(c):
+            f = c * PIECE // C1
+            t = keep.tile([P, 2 * PIECE], U32, name=f"grouped{c}", align_bytes=64)
+            for u in range(2):
+                start = (2 * f + u) * C1 - f * C1
+                window = pairs[:, start : start + (f + 1) * C1].bitcast(U32)
+                nc.vector.tensor_copy(t[:, u::2], window.indirect(entries(slot_of, c * PIECE, PIECE)))
+            grouped[c] = t
+
+        def expert_layer(c):
+            codes = keep.tile([P, PIECE], U32, name=f"codes{c}", align_bytes=64)
+            scales = keep.tile([P, PIECE], U8, name=f"scales{c}", align_bytes=64)
+            nc.vector.quantize_mx(codes[:].bitcast(FP8X4), scales[:], grouped[c][:].bitcast(BF16))
+            y = psum.tile([P, PIECE], F32, name="y", tag=f"bank{(7 + 2 * c) % 8}")
+            for b in range(PIECE // C2):
+                e = c * PIECE // C2 + b
+                nc.tensor.matmul_mx(
+                    y[:, b * C2 : (b + 1) * C2],
+                    lhsT=wew[:, e * N : (e + 1) * N].bitcast(FP8X4),
+                    lhsT_scale=wes[:, e * N : (e + 1) * N],
+                    rhs=codes[:, b * C2 : (b + 1) * C2].bitcast(FP8X4),
+                    rhs_scale=scales[:, b * C2 : (b + 1) * C2],
+                    start=True,
+                    stop=True,
+                )
+            r = keep.tile([P, PIECE], F32, name=f"result{c}")
+            nc.scalar.copy(r[:], y[:])
+            results[c] = r
+
+        for c in range(PIECES):
+            gather_hidden(c)
+            if c > 0:
+                expert_layer(c - 1)
+        expert_layer(PIECES - 1)
+
+        placed = keep.tile([P, T], F32, name="placed")
+        for c in range(PIECES):
+            nc.vector.tensor_tensor(
+                placed[:].indirect(entries(column_of, c * PIECE, PIECE)),
+                results[c][:],
+                weight[:, c * PIECE : (c + 1) * PIECE],
+                MULT,
+            )
+        nc.sync.dma_start(out, placed[:])

@@ -22,6 +22,7 @@ PASSES = K // 512
 PIECE = 256
 PIECES = T // PIECE
 LANES = 16
+SPARE = 192
 
 
 def entries(offsets, first, count):
@@ -35,7 +36,6 @@ def tile_moe_hie_silu_kernel(
     with ExitStack() as ctx:
         lists = ctx.enter_context(tc.tile_pool(name="lists", bufs=1))
         keep = ctx.enter_context(tc.tile_pool(name="keep", bufs=1))
-        ring = ctx.enter_context(tc.tile_pool(name="ring", bufs=4))
         psum = ctx.enter_context(tc.psum_pool(name="psum", bufs=1))
 
         token_of = lists.tile([P, T // LANES], U16, name="token_of")
@@ -49,102 +49,34 @@ def tile_moe_hie_silu_kernel(
         nc.vector.memset(wgs[:].bitcast(I32), 0)
         nc.vector.memset(wes[:].bitcast(I32), 0)
 
-        nc.sync.dma_start(slot_of[:], offs2)
-        nc.sync.dma_start(column_of[:], dst)
-        for q in range(4):
-            nc.sync.dma_start(
-                xs[32 * q : 32 * q + 4, :].bitcast(I32).rearrange("r (s t) -> r s t", s=PASSES),
-                x_scales[:, 4 * q : 4 * q + 4, :].bitcast(I32).rearrange("s r t -> r s t"),
-            )
-        nc.sync.dma_start(token_of[:], offs)
-        xw = keep.tile([P, PASSES * T], I32, name="xw", align_bytes=64)
-        nc.scalar.dma_start(
-            xw[:].rearrange("p (s t) -> p s t", s=PASSES),
-            x_words.rearrange("s p t d -> p s (t d)").bitcast(I32),
-        )
-        wgw = []
-        for f in range(G):
+        def load_scale_rows(plane, rows, count):
+            for q in range(4):
+                nc.sync.dma_start(
+                    plane[32 * q : 32 * q + 4, :].bitcast(I32).rearrange("r (c w) -> r c w", c=count),
+                    rows[:, 4 * q : 4 * q + 4, :].bitcast(I32).rearrange("c r w -> r c w"),
+                )
+
+        def load_group_words(f):
             words = keep.tile([P, PASSES * 2 * H], U8, name=f"wgw{f}", align_bytes=64)
             nc.sync.dma_start(
                 words[:].bitcast(I32).rearrange("p (s b) -> p s b", s=PASSES),
                 wg_words[f].bitcast(I32).rearrange("s p b -> p s b"),
             )
-            wgw.append(words)
-            if f == 0:
-                for q in range(4):
-                    nc.sync.dma_start(
-                        wgs[32 * q : 32 * q + 4, :].bitcast(I32).rearrange("r (c i) -> r c i", c=G * PASSES),
-                        wg_scales[:, :, 4 * q : 4 * q + 4, :].bitcast(I32).rearrange("f s r i -> r (f s) i"),
-                    )
-        for q in range(4):
-            nc.sync.dma_start(
-                wes[32 * q : 32 * q + 4, :].bitcast(I32).rearrange("r (e n) -> r e n", e=E),
-                we_scales[:, 0, 4 * q : 4 * q + 4, :].bitcast(I32).rearrange("e r n -> r e n"),
-            )
+            return words
 
-        identity = keep.tile([P, P], F32, name="identity")
-        make_identity(nc, identity[:])
-
-        pairs = keep.tile([P, G * 2 * C1], F32, name="pairs", align_bytes=64)
-        slot_words, slot_scales = {}, {}
-
-        def gather_scales(f):
-            for s in range(PASSES):
-                t = keep.tile([P, C1], U8, name=f"slot_scales{f}{s}", align_bytes=64)
-                nc.vector.tensor_copy(t[:], xs[:, s * T : (s + 1) * T].indirect(entries(token_of, f * C1, C1)))
-                slot_scales[f, s] = t
-
-        def gather_words(c):
-            for s in range(PASSES):
-                t = keep.tile([P, PIECE], U32, name=f"slot_words{c}{s}", align_bytes=64)
-                nc.vector.tensor_copy(t[:], xw[:, s * T : (s + 1) * T].bitcast(U32).indirect(entries(token_of, c * PIECE, PIECE)))
-                slot_words[c, s] = t
-
-        hidden = {}
-
-        def group_layer(c):
-            f = c * PIECE // C1
-            for b in range(PIECE // P):
-                acc = psum.tile([P, H], F32, name="acc", tag=f"bank{2 * c + b}")
-                first = c * PIECE % C1 + b * P
-                for s in range(PASSES):
-                    nc.tensor.matmul_mx(
-                        acc[:],
-                        lhsT=slot_words[c, s][:, b * P : (b + 1) * P].bitcast(FP8X4),
-                        lhsT_scale=slot_scales[f, s][:, first : first + P],
-                        rhs=wgw[f][:, s * 2 * H : (s + 1) * 2 * H].bitcast(FP4X4),
-                        rhs_scale=wgs[:, (f * PASSES + s) * H : (f * PASSES + s + 1) * H],
-                        start=(s == 0),
-                        stop=(s == PASSES - 1),
-                    )
-                h = ring.tile([P, H], BF16, name="h", align_bytes=64)
-                nc.scalar.activation(
-                    h[:].rearrange("j (u p e) -> j u p e", u=2, e=2),
-                    acc[:].rearrange("j (p u e) -> j u p e", u=2, e=2),
-                    SILU,
-                )
-                hidden[c, b] = h
-
-        def turn(f):
-            for u in range(2):
-                plane = pairs[:, (2 * f + u) * C1 : (2 * f + u + 1) * C1].rearrange("p (c b j) -> p c b j", c=2, b=2)
-                for b in range(2):
-                    turned = psum.tile([P, 2, P], F32, name="turned", tag=f"bank{(4 * (f + 1) + 2 * u + b) % 8}")
-                    for c in range(2):
-                        nc.tensor.transpose(
-                            turned[:, c, :],
-                            hidden[2 * f + c, b][:].bitcast(F32)[:, u * P : (u + 1) * P],
-                            identity[:],
-                        )
-                    nc.scalar.copy(plane[:, :, b, :], turned[:])
-
-        for f in range(G):
-            gather_scales(f)
-            for c in range(2 * f, 2 * f + 2):
-                gather_words(c)
-                group_layer(c)
-            turn(f)
-
+        nc.sync.dma_start(token_of[:], offs)
+        nc.sync.dma_start(slot_of[:], offs2)
+        load_scale_rows(xs, x_scales, PASSES)
+        xw = keep.tile([P, PASSES * T], I32, name="xw", align_bytes=64)
+        nc.sync.dma_start(
+            xw[:].rearrange("p (s t) -> p s t", s=PASSES),
+            x_words.rearrange("s p t d -> p s (t d)").bitcast(I32),
+        )
+        wgw = [load_group_words(0)]
+        load_scale_rows(wgs, wg_scales.rearrange("f s r i -> (f s) r i"), G * PASSES)
+        wgw.append(load_group_words(1))
+        nc.sync.dma_start(column_of[:], dst)
+        load_scale_rows(wes, we_scales.rearrange("e s r n -> (e s) r n"), E)
         wew = keep.tile([P, E * N], I32, name="wew", align_bytes=64)
         nc.sync.dma_start(
             wew[:].rearrange("p (e n) -> p e n", e=E),
@@ -153,49 +85,122 @@ def tile_moe_hie_silu_kernel(
         weight = keep.tile([P, T], F32, name="weight", align_bytes=64)
         nc.sync.dma_start(weight[:], gate)
 
-        grouped, results = {}, {}
+        identity = keep.tile([P, P], F32, name="identity")
+        make_identity(nc, identity[:])
 
-        def gather_hidden(c):
-            f = c * PIECE // C1
-            t = keep.tile([P, 2 * PIECE], U32, name=f"grouped{c}", align_bytes=64)
-            for u in range(2):
-                start = (2 * f + u) * C1 - f * C1
-                window = pairs[:, start : start + (f + 1) * C1].bitcast(U32)
-                nc.vector.tensor_copy(t[:, u::2], window.indirect(entries(slot_of, c * PIECE, PIECE)))
-            grouped[c] = t
+        pairs = keep.tile([P, G * 2 * C1 + SPARE], F32, name="pairs", align_bytes=64)
+        nc.gpsimd.memset(pairs[:, 2 * C1 : 2 * C1 + SPARE], 0.0)
 
-        def expert_layer(c):
-            codes = keep.tile([P, PIECE], U32, name=f"codes{c}", align_bytes=64)
-            scales = keep.tile([P, PIECE], U8, name=f"scales{c}", align_bytes=64)
-            nc.vector.quantize_mx(codes[:].bitcast(FP8X4), scales[:], grouped[c][:].bitcast(BF16))
-            y = psum.tile([P, PIECE], F32, name="y", tag=f"bank{(7 + 2 * c) % 8}")
-            for b in range(PIECE // C2):
-                e = c * PIECE // C2 + b
-                nc.tensor.matmul_mx(
-                    y[:, b * C2 : (b + 1) * C2],
-                    lhsT=wew[:, e * N : (e + 1) * N].bitcast(FP8X4),
-                    lhsT_scale=wes[:, e * N : (e + 1) * N],
-                    rhs=codes[:, b * C2 : (b + 1) * C2].bitcast(FP8X4),
-                    rhs_scale=scales[:, b * C2 : (b + 1) * C2],
-                    start=True,
-                    stop=True,
+        def plane_start(f, u):
+            return (2 * f + u) * C1 + f * SPARE
+
+        def gather_tokens(into, table, s, f, first, width):
+            nc.vector.tensor_copy(
+                into[:, first : first + width],
+                table[:, s * T : (s + 1) * T].indirect(entries(token_of, f * C1 + first, width)),
+            )
+
+        slot_words, slot_scales, hidden = {}, {}, {}
+
+        def gather_group(f):
+            for s in range(PASSES):
+                slot_words[f, s] = keep.tile([P, C1], U32, name=f"slot_words{f}{s}", align_bytes=64)
+                tag = f"slot_words0{s}" if f else f"slot_scales{s}"
+                slot_scales[f, s] = keep.tile([P, C1], U8, name="slot_scales", tag=tag, align_bytes=64)
+            steps = [(slot_scales, xs[:]), (slot_words, xw[:].bitcast(U32))]
+            (early, early_table), (late, late_table) = steps[::-1] if f else steps
+            for s in range(PASSES):
+                gather_tokens(early[f, s], early_table, s, f, 0, C1)
+            for first in range(0, C1, PIECE):
+                for s in range(PASSES):
+                    gather_tokens(late[f, s], late_table, s, f, first, PIECE)
+
+        def group_layer(c):
+            f, first = divmod(c * PIECE, C1)
+            for b in range(PIECE // P):
+                acc = psum.tile([P, H], F32, name="acc", tag=f"bank{(0, 1, 2, 3, 3, 4, 5, 3)[2 * c + b]}")
+                cols = slice(first + b * P, first + (b + 1) * P)
+                for s in range(PASSES):
+                    nc.tensor.matmul_mx(
+                        acc[:],
+                        lhsT=slot_words[f, s][:, cols].bitcast(FP8X4),
+                        lhsT_scale=slot_scales[f, s][:, cols],
+                        rhs=wgw[f][:, s * 2 * H : (s + 1) * 2 * H].bitcast(FP4X4),
+                        rhs_scale=wgs[:, (f * PASSES + s) * H : (f * PASSES + s + 1) * H],
+                        start=(s == 0),
+                        stop=(s == PASSES - 1),
+                    )
+                h = keep.tile([P, H], BF16, name="h", bufs=4, align_bytes=64)
+                nc.scalar.activation(
+                    h[:].rearrange("j (u p e) -> j u p e", u=2, e=2),
+                    acc[:].rearrange("j (p u e) -> j u p e", u=2, e=2),
+                    SILU,
                 )
-            r = keep.tile([P, PIECE], F32, name=f"result{c}")
-            nc.scalar.copy(r[:], y[:])
-            results[c] = r
+                hidden[c, b] = h
 
-        for c in range(PIECES):
-            gather_hidden(c)
-            if c > 0:
-                expert_layer(c - 1)
-        expert_layer(PIECES - 1)
+        def turn(f):
+            turned = [psum.tile([P, C1], F32, name="turned", tag=f"bank{(4, 0)[f] + u}") for u in range(2)]
+            for n in range(C1 // P):
+                for u in range(2):
+                    nc.tensor.transpose(
+                        turned[u][:, n * P : (n + 1) * P],
+                        hidden[2 * f + n // 2, n % 2][:].bitcast(F32)[:, u * P : (u + 1) * P],
+                        identity[:],
+                    )
+            for u in range(2):
+                nc.scalar.copy(pairs[:, plane_start(f, u) : plane_start(f, u) + C1], turned[u][:])
+
+        for f in range(G):
+            gather_group(f)
+            for c in range(2 * f, 2 * f + 2):
+                group_layer(c)
+            turn(f)
+        results = {}
+        for f in range(G):
+            picked = keep.tile([P, 2, C1], U32, name=f"picked{f}", align_bytes=64)
+            for u in range(2):
+                start = plane_start(f, u) - f * C1
+                width = T if f or not u else C1 + SPARE
+                window = pairs[:, start : start + width].bitcast(U32)
+                nc.vector.tensor_copy(picked[:, u, :], window.indirect(entries(slot_of, f * C1, C1)))
+            grouped = keep.tile([P, 2 * C1], U32, name=f"grouped{f}", align_bytes=64)
+            woven = grouped[:].rearrange("p (j u) -> p j u", u=2)
+            planes = picked[:].rearrange("p u j -> p j u")
+            if f == 0:
+                nc.vector.tensor_copy(woven.bitcast(I32), planes.bitcast(I32))
+            else:
+                nc.scalar.copy(woven, planes)
+            codes = keep.tile([P, C1], U32, name=f"codes{f}", align_bytes=64)
+            scales = keep.tile([P, C1], U8, name=f"scales{f}", align_bytes=64)
+            nc.vector.quantize_mx(codes[:].bitcast(FP8X4), scales[:], grouped[:].bitcast(BF16))
+            for c in range(2 * f, 2 * f + 2):
+                y = psum.tile([P, PIECE], F32, name="y", tag=f"bank{(3, 1, 2, 6)[c]}")
+                for b in range(PIECE // C2):
+                    e = c * PIECE // C2 + b
+                    cols = slice(e * C2 - f * C1, (e + 1) * C2 - f * C1)
+                    nc.tensor.matmul_mx(
+                        y[:, b * C2 : (b + 1) * C2],
+                        lhsT=wew[:, e * N : (e + 1) * N].bitcast(FP8X4),
+                        lhsT_scale=wes[:, e * N : (e + 1) * N],
+                        rhs=codes[:, cols].bitcast(FP8X4),
+                        rhs_scale=scales[:, cols],
+                        start=True,
+                        stop=True,
+                    )
+                results[c] = y
 
         placed = keep.tile([P, T], F32, name="placed")
-        for c in range(PIECES):
+
+        def place(pieces, tag):
+            first, width = pieces[0] * PIECE, len(pieces) * PIECE
+            staged = keep.tile([P, width], F32, name="staged", tag=tag, align_bytes=64)
+            for n, c in enumerate(pieces):
+                nc.scalar.copy(staged[:, n * PIECE : (n + 1) * PIECE], results[c][:])
             nc.vector.tensor_tensor(
-                placed[:].indirect(entries(column_of, c * PIECE, PIECE)),
-                results[c][:],
-                weight[:, c * PIECE : (c + 1) * PIECE],
-                MULT,
+                placed[:].indirect(entries(column_of, first, width)), staged[:], weight[:, first : first + width], MULT
             )
+
+        place([0], "staged0")
+        place([1], "picked1")
+        place([2, 3], "picked0")
         nc.sync.dma_start(out, placed[:])

@@ -42,11 +42,13 @@ def tile_moe_hie_silu_kernel(
         slot_of = lists.tile([P, T // LANES], U16, name="slot_of")
         column_of = lists.tile([P, T // LANES], U16, name="column_of")
 
-        xs = keep.tile([P, PASSES * T], U8, name="xs", align_bytes=64)
+        xs = keep.tile([P, T], U8, name="xs", align_bytes=64)
+        lowered = keep.tile([P, T], U8, name="lowered", align_bytes=64)
         wgs = keep.tile([P, G * PASSES * H], U8, name="wgs", align_bytes=64)
         wes = keep.tile([P, E * N], U8, name="wes", align_bytes=64)
         nc.gpsimd.memset(xs[:].bitcast(I32), 0)
         nc.vector.memset(wgs[:].bitcast(I32), 0)
+        nc.vector.memset(lowered[:].bitcast(I32), 0)
         nc.vector.memset(wes[:].bitcast(I32), 0)
 
         def load_scale_rows(plane, rows, count):
@@ -65,8 +67,9 @@ def tile_moe_hie_silu_kernel(
             return words
 
         nc.sync.dma_start(token_of[:], offs)
-        nc.sync.dma_start(slot_of[:], offs2)
-        load_scale_rows(xs, x_scales, PASSES)
+        for q in range(4):
+            queue = nc.sync if q % 2 else nc.scalar
+            queue.dma_start(xs[32 * q : 32 * q + 8, :].bitcast(I32), x_scales[:, 4 * q : 4 * q + 4, :].bitcast(I32))
         xw = keep.tile([P, PASSES * T], I32, name="xw", align_bytes=64)
         nc.sync.dma_start(
             xw[:].rearrange("p (s t) -> p s t", s=PASSES),
@@ -74,7 +77,15 @@ def tile_moe_hie_silu_kernel(
         )
         wgw = [load_group_words(0)]
         load_scale_rows(wgs, wg_scales.rearrange("f s r i -> (f s) r i"), G * PASSES)
+        slot_words, slot_scales, hidden = {}, {}, {}
+        for f in range(G):
+            both = keep.tile([P, C1], U8, name=f"slot_scales{f}", align_bytes=64)
+            nc.vector.tensor_copy(both[:], xs[:].indirect(entries(token_of, f * C1, C1)))
+            second = lowered[:, f * C1 : (f + 1) * C1]
+            nc.sync.dma_start(second[0:100, :].bitcast(I32), both[4:104, :].bitcast(I32))
+            slot_scales[f, 0], slot_scales[f, 1] = both[:], second
         wgw.append(load_group_words(1))
+        nc.sync.dma_start(slot_of[:], offs2)
         nc.sync.dma_start(column_of[:], dst)
         load_scale_rows(wes, we_scales.rearrange("e s r n -> (e s) r n"), E)
         wew = keep.tile([P, E * N], I32, name="wew", align_bytes=64)
@@ -94,31 +105,22 @@ def tile_moe_hie_silu_kernel(
         def plane_start(f, u):
             return (2 * f + u) * C1 + f * SPARE
 
-        def gather_tokens(into, table, s, f, first, width):
-            nc.vector.tensor_copy(
-                into[:, first : first + width],
-                table[:, s * T : (s + 1) * T].indirect(entries(token_of, f * C1 + first, width)),
-            )
-
-        slot_words, slot_scales, hidden = {}, {}, {}
-
         def gather_group(f):
             for s in range(PASSES):
                 slot_words[f, s] = keep.tile([P, C1], U32, name=f"slot_words{f}{s}", align_bytes=64)
-                tag = f"slot_words0{s}" if f else f"slot_scales{s}"
-                slot_scales[f, s] = keep.tile([P, C1], U8, name="slot_scales", tag=tag, align_bytes=64)
-            steps = [(slot_scales, xs[:]), (slot_words, xw[:].bitcast(U32))]
-            (early, early_table), (late, late_table) = steps[::-1] if f else steps
-            for s in range(PASSES):
-                gather_tokens(early[f, s], early_table, s, f, 0, C1)
-            for first in range(0, C1, PIECE):
-                for s in range(PASSES):
-                    gather_tokens(late[f, s], late_table, s, f, first, PIECE)
+            cuts = [(s, first, PIECE) for first in range(0, C1, PIECE) for s in range(PASSES)]
+            if f:
+                cuts = [(0, 0, C1)] + [cut for cut in cuts if cut[0]]
+            for s, first, width in cuts:
+                nc.vector.tensor_copy(
+                    slot_words[f, s][:, first : first + width],
+                    xw[:, s * T : (s + 1) * T].bitcast(U32).indirect(entries(token_of, f * C1 + first, width)),
+                )
 
         def group_layer(c):
             f, first = divmod(c * PIECE, C1)
             for b in range(PIECE // P):
-                acc = psum.tile([P, H], F32, name="acc", tag=f"bank{(0, 1, 2, 3, 3, 4, 5, 3)[2 * c + b]}")
+                acc = psum.tile([P, H], F32, name="acc", tag=f"bank{(0, 1, 2, 3, 1, 2, 3, 1)[2 * c + b]}")
                 cols = slice(first + b * P, first + (b + 1) * P)
                 for s in range(PASSES):
                     nc.tensor.matmul_mx(
@@ -130,7 +132,7 @@ def tile_moe_hie_silu_kernel(
                         start=(s == 0),
                         stop=(s == PASSES - 1),
                     )
-                h = keep.tile([P, H], BF16, name="h", bufs=4, align_bytes=64)
+                h = keep.tile([P, H], BF16, name="h", bufs=8, align_bytes=64)
                 nc.scalar.activation(
                     h[:].rearrange("j (u p e) -> j u p e", u=2, e=2),
                     acc[:].rearrange("j (p u e) -> j u p e", u=2, e=2),
@@ -138,23 +140,29 @@ def tile_moe_hie_silu_kernel(
                 )
                 hidden[c, b] = h
 
-        def turn(f):
-            turned = [psum.tile([P, C1], F32, name="turned", tag=f"bank{(4, 0)[f] + u}") for u in range(2)]
-            for n in range(C1 // P):
+        def turn(f, blocks, bank, copy):
+            turned = psum.tile([P, 2, len(blocks) * P], F32, name="turned", tag=f"bank{bank}")
+            for n, block in enumerate(blocks):
                 for u in range(2):
                     nc.tensor.transpose(
-                        turned[u][:, n * P : (n + 1) * P],
-                        hidden[2 * f + n // 2, n % 2][:].bitcast(F32)[:, u * P : (u + 1) * P],
+                        turned[:, u, n * P : (n + 1) * P],
+                        hidden[2 * f + block // 2, block % 2][:].bitcast(F32)[:, u * P : (u + 1) * P],
                         identity[:],
                     )
-            for u in range(2):
-                nc.scalar.copy(pairs[:, plane_start(f, u) : plane_start(f, u) + C1], turned[u][:])
+            planes = pairs[:, plane_start(f, 0) : plane_start(f, 2)].rearrange("p (u j) -> p u j", u=2)
+            copy(planes[:, :, blocks[0] * P : (blocks[-1] + 1) * P], turned[:])
 
-        for f in range(G):
-            gather_group(f)
-            for c in range(2 * f, 2 * f + 2):
-                group_layer(c)
-            turn(f)
+        gather_group(0)
+        gather_group(1)
+        group_layer(0)
+        turn(0, [0, 1], 4, nc.vector.tensor_copy)
+        group_layer(1)
+        turn(0, [2], 5, nc.vector.tensor_copy)
+        turn(0, [3], 6, nc.vector.tensor_copy)
+        group_layer(2)
+        turn(1, [0, 1], 0, nc.scalar.copy)
+        group_layer(3)
+        turn(1, [2, 3], 7, nc.scalar.copy)
         results = {}
         for f in range(G):
             picked = keep.tile([P, 2, C1], U32, name=f"picked{f}", align_bytes=64)
@@ -174,7 +182,7 @@ def tile_moe_hie_silu_kernel(
             scales = keep.tile([P, C1], U8, name=f"scales{f}", align_bytes=64)
             nc.vector.quantize_mx(codes[:].bitcast(FP8X4), scales[:], grouped[:].bitcast(BF16))
             for c in range(2 * f, 2 * f + 2):
-                y = psum.tile([P, PIECE], F32, name="y", tag=f"bank{(3, 1, 2, 6)[c]}")
+                y = psum.tile([P, PIECE], F32, name="y", tag=f"bank{(1, 7, 4, 5)[c]}")
                 for b in range(PIECE // C2):
                     e = c * PIECE // C2 + b
                     cols = slice(e * C2 - f * C1, (e + 1) * C2 - f * C1)

@@ -82,7 +82,8 @@ def tile_moe_hie_silu_kernel(
             both = keep.tile([P, C1], U8, name=f"slot_scales{f}", align_bytes=64)
             nc.vector.tensor_copy(both[:], xs[:].indirect(entries(token_of, f * C1, C1)))
             second = lowered[:, f * C1 : (f + 1) * C1]
-            nc.sync.dma_start(second[0:100, :].bitcast(I32), both[4:104, :].bitcast(I32))
+            queue = nc.sync if f else nc.scalar
+            queue.dma_start(second[0:100, :].bitcast(I32), both[4:104, :].bitcast(I32))
             slot_scales[f, 0], slot_scales[f, 1] = both[:], second
         wgw.append(load_group_words(1))
         nc.sync.dma_start(slot_of[:], offs2)
@@ -119,10 +120,13 @@ def tile_moe_hie_silu_kernel(
 
         def group_layer(c):
             f, first = divmod(c * PIECE, C1)
-            for b in range(PIECE // P):
-                acc = psum.tile([P, H], F32, name="acc", tag=f"bank{(0, 1, 2, 3, 1, 2, 3, 1)[2 * c + b]}")
-                cols = slice(first + b * P, first + (b + 1) * P)
-                for s in range(PASSES):
+            sums = [
+                psum.tile([P, H], F32, name="acc", tag=f"bank{(0, 1, 2, 3, 1, 3, 6, 1)[2 * c + b]}")
+                for b in range(PIECE // P)
+            ]
+            for s in range(PASSES):
+                for b, acc in enumerate(sums):
+                    cols = slice(first + b * P, first + (b + 1) * P)
                     nc.tensor.matmul_mx(
                         acc[:],
                         lhsT=slot_words[f, s][:, cols].bitcast(FP8X4),
@@ -132,6 +136,7 @@ def tile_moe_hie_silu_kernel(
                         start=(s == 0),
                         stop=(s == PASSES - 1),
                     )
+            for b, acc in enumerate(sums):
                 h = keep.tile([P, H], BF16, name="h", bufs=8, align_bytes=64)
                 nc.scalar.activation(
                     h[:].rearrange("j (u p e) -> j u p e", u=2, e=2),
@@ -140,29 +145,34 @@ def tile_moe_hie_silu_kernel(
                 )
                 hidden[c, b] = h
 
-        def turn(f, blocks, bank, copy):
+        def turn(into, block, u):
+            nc.tensor.transpose(
+                into, hidden[block // 2, block % 2][:].bitcast(F32)[:, u * P : (u + 1) * P], identity[:]
+            )
+
+        def turn_blocks(blocks, bank, copy):
             turned = psum.tile([P, 2, len(blocks) * P], F32, name="turned", tag=f"bank{bank}")
             for n, block in enumerate(blocks):
                 for u in range(2):
-                    nc.tensor.transpose(
-                        turned[:, u, n * P : (n + 1) * P],
-                        hidden[2 * f + block // 2, block % 2][:].bitcast(F32)[:, u * P : (u + 1) * P],
-                        identity[:],
-                    )
-            planes = pairs[:, plane_start(f, 0) : plane_start(f, 2)].rearrange("p (u j) -> p u j", u=2)
+                    turn(turned[:, u, n * P : (n + 1) * P], block, u)
+            planes = pairs[:, plane_start(0, 0) : plane_start(0, 2)].rearrange("p (u j) -> p u j", u=2)
             copy(planes[:, :, blocks[0] * P : (blocks[-1] + 1) * P], turned[:])
 
         gather_group(0)
         gather_group(1)
         group_layer(0)
-        turn(0, [0, 1], 4, nc.vector.tensor_copy)
+        turn_blocks([0, 1], 4, nc.scalar.copy)
         group_layer(1)
-        turn(0, [2], 5, nc.vector.tensor_copy)
-        turn(0, [3], 6, nc.vector.tensor_copy)
+        turn_blocks([2], 5, nc.vector.tensor_copy)
+        turn_blocks([3], 6, nc.vector.tensor_copy)
         group_layer(2)
-        turn(1, [0, 1], 0, nc.scalar.copy)
         group_layer(3)
-        turn(1, [2, 3], 7, nc.scalar.copy)
+        turned = [psum.tile([P, C1], F32, name="turned", tag=f"bank{7 * u}") for u in range(2)]
+        for n in range(C1 // P):
+            for u in range(2):
+                turn(turned[u][:, n * P : (n + 1) * P], C1 // P + n, u)
+        for u in range(2):
+            nc.scalar.copy(pairs[:, plane_start(1, u) : plane_start(1, u) + C1], turned[u][:])
         results = {}
         for f in range(G):
             picked = keep.tile([P, 2, C1], U32, name=f"picked{f}", align_bytes=64)

@@ -161,8 +161,8 @@ def tile_moe_hie_silu_kernel(
         gather_group(0)
         gather_group(1)
         group_layer(0)
-        turn_blocks([0, 1], 4, nc.scalar.copy)
         group_layer(1)
+        turn_blocks([0, 1], 4, nc.scalar.copy)
         turn_blocks([2], 5, nc.vector.tensor_copy)
         turn_blocks([3], 6, nc.vector.tensor_copy)
         group_layer(2)

@@ -20,9 +20,9 @@ MULT = mybir.AluOpType.mult
 P = 128
 PASSES = K // 512
 PIECE = 256
-PIECES = T // PIECE
 LANES = 16
 SPARE = 192
+WARM_UP = 3
 
 
 def entries(offsets, first, count):
@@ -50,9 +50,11 @@ def tile_moe_hie_silu_kernel(
         nc.vector.memset(wgs[:].bitcast(I32), 0)
         nc.vector.memset(lowered[:].bitcast(I32), 0)
         nc.vector.memset(wes[:].bitcast(I32), 0)
+        codes0 = keep.tile([P, C1], U32, name="codes0", align_bytes=64)
+        nc.vector.memset(codes0[:].bitcast(I32), 0)
 
-        def load_scale_rows(plane, rows, count):
-            for q in range(4):
+        def load_scale_rows(plane, rows, count, quadrants):
+            for q in quadrants:
                 nc.sync.dma_start(
                     plane[32 * q : 32 * q + 4, :].bitcast(I32).rearrange("r (c w) -> r c w", c=count),
                     rows[:, 4 * q : 4 * q + 4, :].bitcast(I32).rearrange("c r w -> r c w"),
@@ -70,25 +72,30 @@ def tile_moe_hie_silu_kernel(
         for q in range(4):
             queue = nc.sync if q % 2 else nc.scalar
             queue.dma_start(xs[32 * q : 32 * q + 8, :].bitcast(I32), x_scales[:, 4 * q : 4 * q + 4, :].bitcast(I32))
+        group_rows = wg_scales.rearrange("f s r i -> (f s) r i")
+        load_scale_rows(wgs, group_rows, G * PASSES, range(1))
         xw = keep.tile([P, PASSES * T], I32, name="xw", align_bytes=64)
         nc.sync.dma_start(
             xw[:].rearrange("p (s t) -> p s t", s=PASSES),
             x_words.rearrange("s p t d -> p s (t d)").bitcast(I32),
         )
         wgw = [load_group_words(0)]
-        load_scale_rows(wgs, wg_scales.rearrange("f s r i -> (f s) r i"), G * PASSES)
+        load_scale_rows(wgs, group_rows, G * PASSES, range(1, 4))
         slot_words, slot_scales, hidden = {}, {}, {}
         for f in range(G):
             both = keep.tile([P, C1], U8, name=f"slot_scales{f}", align_bytes=64)
             nc.vector.tensor_copy(both[:], xs[:].indirect(entries(token_of, f * C1, C1)))
             second = lowered[:, f * C1 : (f + 1) * C1]
             queue = nc.sync if f else nc.scalar
-            queue.dma_start(second[0:100, :].bitcast(I32), both[4:104, :].bitcast(I32))
+            for first, count in ((0, 64), (64, 32), (96, 4)):
+                queue.dma_start(
+                    second[first : first + count, :].bitcast(I32), both[first + 4 : first + 4 + count, :].bitcast(I32)
+                )
             slot_scales[f, 0], slot_scales[f, 1] = both[:], second
         wgw.append(load_group_words(1))
         nc.sync.dma_start(slot_of[:], offs2)
         nc.sync.dma_start(column_of[:], dst)
-        load_scale_rows(wes, we_scales.rearrange("e s r n -> (e s) r n"), E)
+        load_scale_rows(wes, we_scales.rearrange("e s r n -> (e s) r n"), E, range(4))
         wew = keep.tile([P, E * N], I32, name="wew", align_bytes=64)
         nc.sync.dma_start(
             wew[:].rearrange("p (e n) -> p e n", e=E),
@@ -100,33 +107,25 @@ def tile_moe_hie_silu_kernel(
         identity = keep.tile([P, P], F32, name="identity")
         make_identity(nc, identity[:])
 
-        pairs = keep.tile([P, G * 2 * C1 + SPARE], F32, name="pairs", align_bytes=64)
-        nc.gpsimd.memset(pairs[:, 2 * C1 : 2 * C1 + SPARE], 0.0)
+        pair0, pair1, spare, pair2 = 0, C1, 2 * C1, 2 * C1 + SPARE
+        pair3 = pair2 + C1
+        planes = keep.tile([P, pair3 + C1], F32, name="planes", align_bytes=64)
+        nc.gpsimd.memset(planes[:, spare : spare + SPARE], 0.0)
 
-        def plane_start(f, u):
-            return (2 * f + u) * C1 + f * SPARE
-
-        def gather_group(f):
+        def gather_words(f, cuts):
             for s in range(PASSES):
                 slot_words[f, s] = keep.tile([P, C1], U32, name=f"slot_words{f}{s}", align_bytes=64)
-            cuts = [(s, first, PIECE) for first in range(0, C1, PIECE) for s in range(PASSES)]
-            if f:
-                cuts = [(0, 0, C1)] + [cut for cut in cuts if cut[0]]
             for s, first, width in cuts:
                 nc.vector.tensor_copy(
                     slot_words[f, s][:, first : first + width],
                     xw[:, s * T : (s + 1) * T].bitcast(U32).indirect(entries(token_of, f * C1 + first, width)),
                 )
 
-        def group_layer(c):
-            f, first = divmod(c * PIECE, C1)
-            sums = [
-                psum.tile([P, H], F32, name="acc", tag=f"bank{(0, 1, 2, 3, 1, 3, 6, 1)[2 * c + b]}")
-                for b in range(PIECE // P)
-            ]
-            for s in range(PASSES):
-                for b, acc in enumerate(sums):
-                    cols = slice(first + b * P, first + (b + 1) * P)
+        def group_layer(f, banks):
+            for b, bank in enumerate(banks):
+                acc = psum.tile([P, H], F32, name="acc", tag=f"bank{bank}")
+                cols = slice(b * P, (b + 1) * P)
+                for s in range(PASSES):
                     nc.tensor.matmul_mx(
                         acc[:],
                         lhsT=slot_words[f, s][:, cols].bitcast(FP8X4),
@@ -136,89 +135,108 @@ def tile_moe_hie_silu_kernel(
                         start=(s == 0),
                         stop=(s == PASSES - 1),
                     )
-            for b, acc in enumerate(sums):
                 h = keep.tile([P, H], BF16, name="h", bufs=8, align_bytes=64)
                 nc.scalar.activation(
                     h[:].rearrange("j (u p e) -> j u p e", u=2, e=2),
                     acc[:].rearrange("j (p u e) -> j u p e", u=2, e=2),
                     SILU,
                 )
-                hidden[c, b] = h
+                hidden[f, b] = h
 
-        def turn(into, block, u):
-            nc.tensor.transpose(
-                into, hidden[block // 2, block % 2][:].bitcast(F32)[:, u * P : (u + 1) * P], identity[:]
-            )
+        def turn_pairs(into, f, b, u):
+            nc.tensor.transpose(into, hidden[f, b][:].bitcast(F32)[:, u * P : (u + 1) * P], identity[:])
 
-        def turn_blocks(blocks, bank, copy):
-            turned = psum.tile([P, 2, len(blocks) * P], F32, name="turned", tag=f"bank{bank}")
-            for n, block in enumerate(blocks):
-                for u in range(2):
-                    turn(turned[:, u, n * P : (n + 1) * P], block, u)
-            planes = pairs[:, plane_start(0, 0) : plane_start(0, 2)].rearrange("p (u j) -> p u j", u=2)
-            copy(planes[:, :, blocks[0] * P : (blocks[-1] + 1) * P], turned[:])
+        def experts(y, first_expert, count, codes, scales):
+            for b in range(count):
+                e = first_expert + b
+                nc.tensor.matmul_mx(
+                    y[:, b * C2 : (b + 1) * C2],
+                    lhsT=wew[:, e * N : (e + 1) * N].bitcast(FP8X4),
+                    lhsT_scale=wes[:, e * N : (e + 1) * N],
+                    rhs=codes[:, b * C2 : (b + 1) * C2].bitcast(FP8X4),
+                    rhs_scale=scales[:, b * C2 : (b + 1) * C2],
+                    start=True,
+                    stop=True,
+                )
 
-        gather_group(0)
-        gather_group(1)
-        group_layer(0)
-        group_layer(1)
-        turn_blocks([0, 1], 4, nc.scalar.copy)
-        turn_blocks([2], 5, nc.vector.tensor_copy)
-        turn_blocks([3], 6, nc.vector.tensor_copy)
-        group_layer(2)
-        group_layer(3)
-        turned = [psum.tile([P, C1], F32, name="turned", tag=f"bank{7 * u}") for u in range(2)]
-        for n in range(C1 // P):
-            for u in range(2):
-                turn(turned[u][:, n * P : (n + 1) * P], C1 // P + n, u)
-        for u in range(2):
-            nc.scalar.copy(pairs[:, plane_start(1, u) : plane_start(1, u) + C1], turned[u][:])
-        results = {}
-        for f in range(G):
-            picked = keep.tile([P, 2, C1], U32, name=f"picked{f}", align_bytes=64)
-            for u in range(2):
-                start = plane_start(f, u) - f * C1
-                width = T if f or not u else C1 + SPARE
-                window = pairs[:, start : start + width].bitcast(U32)
-                nc.vector.tensor_copy(picked[:, u, :], window.indirect(entries(slot_of, f * C1, C1)))
-            grouped = keep.tile([P, 2 * C1], U32, name=f"grouped{f}", align_bytes=64)
-            woven = grouped[:].rearrange("p (j u) -> p j u", u=2)
-            planes = picked[:].rearrange("p u j -> p j u")
-            if f == 0:
-                nc.vector.tensor_copy(woven.bitcast(I32), planes.bitcast(I32))
-            else:
-                nc.scalar.copy(woven, planes)
-            codes = keep.tile([P, C1], U32, name=f"codes{f}", align_bytes=64)
-            scales = keep.tile([P, C1], U8, name=f"scales{f}", align_bytes=64)
+        def quantise(grouped, codes, width, name):
+            scales = keep.tile([P, width], U8, name=f"scales{name}", align_bytes=64)
             nc.vector.quantize_mx(codes[:].bitcast(FP8X4), scales[:], grouped[:].bitcast(BF16))
-            for c in range(2 * f, 2 * f + 2):
-                y = psum.tile([P, PIECE], F32, name="y", tag=f"bank{(1, 7, 4, 5)[c]}")
-                for b in range(PIECE // C2):
-                    e = c * PIECE // C2 + b
-                    cols = slice(e * C2 - f * C1, (e + 1) * C2 - f * C1)
-                    nc.tensor.matmul_mx(
-                        y[:, b * C2 : (b + 1) * C2],
-                        lhsT=wew[:, e * N : (e + 1) * N].bitcast(FP8X4),
-                        lhsT_scale=wes[:, e * N : (e + 1) * N],
-                        rhs=codes[:, cols].bitcast(FP8X4),
-                        rhs_scale=scales[:, cols],
-                        start=True,
-                        stop=True,
-                    )
-                results[c] = y
+            return scales
 
         placed = keep.tile([P, T], F32, name="placed")
 
-        def place(pieces, tag):
-            first, width = pieces[0] * PIECE, len(pieces) * PIECE
-            staged = keep.tile([P, width], F32, name="staged", tag=tag, align_bytes=64)
-            for n, c in enumerate(pieces):
-                nc.scalar.copy(staged[:, n * PIECE : (n + 1) * PIECE], results[c][:])
+        def place(first, width, staged):
             nc.vector.tensor_tensor(
-                placed[:].indirect(entries(column_of, first, width)), staged[:], weight[:, first : first + width], MULT
+                placed[:].indirect(entries(column_of, first, width)), staged, weight[:, first : first + width], MULT
             )
 
-        place([0], "staged0")
-        place([1], "picked1")
-        place([2, 3], "picked0")
+        gather_words(0, [(0, 0, PIECE), (1, 0, P), (1, P, P), (0, PIECE, PIECE), (1, 2 * P, P), (1, 3 * P, P)])
+        gather_words(1, [(0, 0, C1), (1, 0, PIECE), (1, PIECE, PIECE)])
+        warm = psum.tile([P, H], F32, name="warm", tag="bank7")
+        for n in range(WARM_UP):
+            nc.tensor.matmul_mx(
+                warm[:],
+                lhsT=codes0[:, 0:P].bitcast(FP8X4),
+                lhsT_scale=slot_scales[0, 0][:, 0:P],
+                rhs=codes0[:].bitcast(FP8X4),
+                rhs_scale=slot_scales[0, 0],
+                start=True,
+                stop=True,
+            )
+        group_layer(0, (0, 1, 2, 3))
+        both_pairs = planes[:, pair0:spare].rearrange("p (u j) -> p u j", u=2)
+        for half, bank in enumerate((2, 0)):
+            turned = psum.tile([P, 2, PIECE], F32, name="turned", tag=f"bank{bank}")
+            for n in range(2):
+                for u in range(2):
+                    turn_pairs(turned[:, u, n * P : (n + 1) * P], 0, 2 * half + n, u)
+            copy = nc.vector.tensor_copy if half else nc.scalar.copy
+            copy(both_pairs[:, :, half * PIECE : (half + 1) * PIECE], turned[:])
+        group_layer(1, (3, 2, 0, 3))
+
+        picked0 = keep.tile([P, 2, C1], U32, name="picked0", align_bytes=64)
+        for u, (start, width) in enumerate(((pair0, T), (pair1, C1 + SPARE))):
+            window = planes[:, start : start + width].bitcast(U32)
+            nc.vector.tensor_copy(picked0[:, u, :], window.indirect(entries(slot_of, 0, C1)))
+        grouped0 = keep.tile([P, 2 * C1], U32, name="grouped0", align_bytes=64)
+        nc.vector.tensor_copy(
+            grouped0[:].rearrange("p (j u) -> p j u", u=2).bitcast(I32),
+            picked0[:].rearrange("p u j -> p j u").bitcast(I32),
+        )
+        scales0 = quantise(grouped0, codes0, C1, "0")
+
+        for start, u, bank in ((pair2, 0, 1), (pair3, 1, 4)):
+            turned = psum.tile([P, C1], F32, name="turned", tag=f"bank{bank}")
+            for b in range(C1 // P):
+                turn_pairs(turned[:, b * P : (b + 1) * P], 1, b, u)
+            nc.scalar.copy(planes[:, start : start + C1], turned[:])
+
+        y0 = psum.tile([P, C1], F32, name="y0", tag="bank4")
+        experts(y0, 0, 4, codes0, scales0)
+
+        picked1 = keep.tile([P, 2 * C1], F32, name="picked1", align_bytes=64)
+        for u, start in enumerate((pair2, pair3)):
+            window = planes[:, start - C1 : start + C1].bitcast(U32)
+            nc.vector.tensor_copy(
+                picked1[:, u * C1 : (u + 1) * C1].bitcast(U32), window.indirect(entries(slot_of, C1, C1))
+            )
+        staged = keep.tile([P, PIECE], F32, name="staged", align_bytes=64)
+        nc.scalar.copy(staged[:], y0[:, 0:PIECE])
+        place(0, PIECE, staged[:])
+        grouped1 = keep.tile([P, 2 * C1], U32, name="grouped1", align_bytes=64)
+        nc.scalar.copy(
+            grouped1[:].rearrange("p (j u) -> p j u", u=2),
+            picked1[:].bitcast(U32).rearrange("p (u j) -> p j u", u=2),
+        )
+        codes1 = keep.tile([P, C1], U32, name="codes1", align_bytes=64)
+        scales1 = quantise(grouped1, codes1, C1, "1")
+        y1 = psum.tile([P, C1], F32, name="y1", tag="bank5")
+        experts(y1, 4, 4, codes1, scales1)
+        staged = picked1[:, 0:PIECE]
+        nc.scalar.copy(staged, y0[:, PIECE:C1])
+        place(PIECE, PIECE, staged)
+        last = keep.tile([P, C1], F32, name="last", align_bytes=64)
+        nc.scalar.copy(last[:], y1[:])
+        place(C1, C1, last[:])
         nc.sync.dma_start(out, placed[:])

@@ -22,7 +22,8 @@ PASSES = K // 512
 PIECE = 256
 LANES = 16
 SPARE = 192
-WARM_UP = 3
+WARM_UP = 4
+EARLY = 384
 
 
 def entries(offsets, first, count):
@@ -51,7 +52,9 @@ def tile_moe_hie_silu_kernel(
         nc.vector.memset(lowered[:].bitcast(I32), 0)
         nc.vector.memset(wes[:].bitcast(I32), 0)
         codes0 = keep.tile([P, C1], U32, name="codes0", align_bytes=64)
+        scales0 = keep.tile([P, C1], U8, name="scales0", align_bytes=64)
         nc.vector.memset(codes0[:].bitcast(I32), 0)
+        nc.vector.memset(scales0[:].bitcast(I32), 0)
 
         def load_scale_rows(plane, rows, count, quadrants):
             for q in quadrants:
@@ -81,17 +84,17 @@ def tile_moe_hie_silu_kernel(
         )
         wgw = [load_group_words(0)]
         load_scale_rows(wgs, group_rows, G * PASSES, range(1, 4))
-        slot_words, slot_scales, hidden = {}, {}, {}
-        for f in range(G):
-            both = keep.tile([P, C1], U8, name=f"slot_scales{f}", align_bytes=64)
-            nc.vector.tensor_copy(both[:], xs[:].indirect(entries(token_of, f * C1, C1)))
-            second = lowered[:, f * C1 : (f + 1) * C1]
-            queue = nc.sync if f else nc.scalar
-            for first, count in ((0, 64), (64, 32), (96, 4)):
+        slot_words, hidden = {}, {}
+        in_place = keep.tile([P, T], U8, name="in_place", align_bytes=64)
+        for first, width, queue in ((0, EARLY, nc.scalar), (EARLY, T - EARLY, nc.sync)):
+            cols = slice(first, first + width)
+            nc.vector.tensor_copy(in_place[:, cols], xs[:].indirect(entries(token_of, first, width)))
+            for row, count in ((0, 64), (64, 32), (96, 4)):
                 queue.dma_start(
-                    second[first : first + count, :].bitcast(I32), both[first + 4 : first + 4 + count, :].bitcast(I32)
+                    lowered[row : row + count, cols].bitcast(I32),
+                    in_place[row + 4 : row + 4 + count, cols].bitcast(I32),
                 )
-            slot_scales[f, 0], slot_scales[f, 1] = both[:], second
+        slot_scales = (in_place, lowered)
         wgw.append(load_group_words(1))
         nc.sync.dma_start(slot_of[:], offs2)
         nc.sync.dma_start(column_of[:], dst)
@@ -114,34 +117,36 @@ def tile_moe_hie_silu_kernel(
 
         def gather_words(f, cuts):
             for s in range(PASSES):
-                slot_words[f, s] = keep.tile([P, C1], U32, name=f"slot_words{f}{s}", align_bytes=64)
+                slot_words[f, s] = keep.tile([P, C1], U32, name="words", tag=f"slot_words{f}{s}", align_bytes=64)
             for s, first, width in cuts:
                 nc.vector.tensor_copy(
                     slot_words[f, s][:, first : first + width],
                     xw[:, s * T : (s + 1) * T].bitcast(U32).indirect(entries(token_of, f * C1 + first, width)),
                 )
 
-        def group_layer(f, banks):
-            for b, bank in enumerate(banks):
-                acc = psum.tile([P, H], F32, name="acc", tag=f"bank{bank}")
-                cols = slice(b * P, (b + 1) * P)
-                for s in range(PASSES):
-                    nc.tensor.matmul_mx(
-                        acc[:],
-                        lhsT=slot_words[f, s][:, cols].bitcast(FP8X4),
-                        lhsT_scale=slot_scales[f, s][:, cols],
-                        rhs=wgw[f][:, s * 2 * H : (s + 1) * 2 * H].bitcast(FP4X4),
-                        rhs_scale=wgs[:, (f * PASSES + s) * H : (f * PASSES + s + 1) * H],
-                        start=(s == 0),
-                        stop=(s == PASSES - 1),
-                    )
-                h = keep.tile([P, H], BF16, name="h", bufs=8, align_bytes=64)
-                nc.scalar.activation(
-                    h[:].rearrange("j (u p e) -> j u p e", u=2, e=2),
-                    acc[:].rearrange("j (p u e) -> j u p e", u=2, e=2),
-                    SILU,
+        def block_sums(f, b, bank):
+            acc = psum.tile([P, H], F32, name="acc", tag=f"bank{bank}")
+            cols = slice(b * P, (b + 1) * P)
+            for s in range(PASSES):
+                nc.tensor.matmul_mx(
+                    acc[:],
+                    lhsT=slot_words[f, s][:, cols].bitcast(FP8X4),
+                    lhsT_scale=slot_scales[s][:, f * C1 + b * P : f * C1 + (b + 1) * P],
+                    rhs=wgw[f][:, s * 2 * H : (s + 1) * 2 * H].bitcast(FP4X4),
+                    rhs_scale=wgs[:, (f * PASSES + s) * H : (f * PASSES + s + 1) * H],
+                    start=(s == 0),
+                    stop=(s == PASSES - 1),
                 )
-                hidden[f, b] = h
+            return acc
+
+        def activate(f, b, acc):
+            h = keep.tile([P, H], BF16, name="h", tag=f"hidden{f}{b}", align_bytes=64)
+            nc.scalar.activation(
+                h[:].rearrange("j (u p e) -> j u p e", u=2, e=2),
+                acc[:].rearrange("j (p u e) -> j u p e", u=2, e=2),
+                SILU,
+            )
+            hidden[f, b] = h
 
         def turn_pairs(into, f, b, u):
             nc.tensor.transpose(into, hidden[f, b][:].bitcast(F32)[:, u * P : (u + 1) * P], identity[:])
@@ -159,10 +164,20 @@ def tile_moe_hie_silu_kernel(
                     stop=True,
                 )
 
-        def quantise(grouped, codes, width, name):
-            scales = keep.tile([P, width], U8, name=f"scales{name}", align_bytes=64)
-            nc.vector.quantize_mx(codes[:].bitcast(FP8X4), scales[:], grouped[:].bitcast(BF16))
-            return scales
+        def weave(parts, tag):
+            grouped = keep.tile([P, 2 * PIECE], U32, name="grouped", tag=tag, align_bytes=64)
+            nc.scalar.copy(grouped[:].rearrange("p (j u) -> p j u", u=2), parts.rearrange("p u j -> p j u"))
+            return grouped
+
+        def quantise(grouped, half):
+            cols = slice(half * PIECE, (half + 1) * PIECE)
+            nc.vector.quantize_mx(codes0[:, cols].bitcast(FP8X4), scales0[:, cols], grouped[:].bitcast(BF16))
+
+        def expert_pair(half, bank):
+            cols = slice(half * PIECE, (half + 1) * PIECE)
+            y = psum.tile([P, PIECE], F32, name="y", tag=f"bank{bank}")
+            experts(y, 2 * half, 2, codes0[:, cols], scales0[:, cols])
+            return y
 
         placed = keep.tile([P, T], F32, name="placed")
 
@@ -171,58 +186,64 @@ def tile_moe_hie_silu_kernel(
                 placed[:].indirect(entries(column_of, first, width)), staged, weight[:, first : first + width], MULT
             )
 
-        gather_words(0, [(0, 0, PIECE), (1, 0, P), (1, P, P), (0, PIECE, PIECE), (1, 2 * P, P), (1, 3 * P, P)])
-        gather_words(1, [(0, 0, C1), (1, 0, PIECE), (1, PIECE, PIECE)])
+        gather_words(0, [(0, 0, P), (1, 0, P), (0, P, P), (1, P, P), (0, PIECE, PIECE), (1, 2 * P, P), (1, 3 * P, P)])
+        gather_words(1, [(0, 0, PIECE), (1, 0, PIECE), (0, PIECE, PIECE), (1, PIECE, PIECE)])
         warm = psum.tile([P, H], F32, name="warm", tag="bank7")
         for n in range(WARM_UP):
             nc.tensor.matmul_mx(
                 warm[:],
                 lhsT=codes0[:, 0:P].bitcast(FP8X4),
-                lhsT_scale=slot_scales[0, 0][:, 0:P],
+                lhsT_scale=in_place[:, 0:P],
                 rhs=codes0[:].bitcast(FP8X4),
-                rhs_scale=slot_scales[0, 0],
+                rhs_scale=scales0[:],
                 start=True,
                 stop=True,
             )
-        group_layer(0, (0, 1, 2, 3))
+        for b in range(C1 // P):
+            activate(0, b, block_sums(0, b, b))
         both_pairs = planes[:, pair0:spare].rearrange("p (u j) -> p u j", u=2)
-        for half, bank in enumerate((2, 0)):
-            turned = psum.tile([P, 2, PIECE], F32, name="turned", tag=f"bank{bank}")
-            for n in range(2):
+        for blocks, bank, copy in (((0, 1), 5, nc.scalar.copy), ((2,), 6, nc.scalar.copy), ((3,), 7, nc.vector.tensor_copy)):
+            turned = psum.tile([P, 2, len(blocks) * P], F32, name="turned", tag=f"bank{bank}")
+            for n, b in enumerate(blocks):
                 for u in range(2):
-                    turn_pairs(turned[:, u, n * P : (n + 1) * P], 0, 2 * half + n, u)
-            copy = nc.vector.tensor_copy if half else nc.scalar.copy
-            copy(both_pairs[:, :, half * PIECE : (half + 1) * PIECE], turned[:])
-        group_layer(1, (3, 2, 0, 3))
+                    turn_pairs(turned[:, u, n * P : (n + 1) * P], 0, b, u)
+            copy(both_pairs[:, :, blocks[0] * P : (blocks[-1] + 1) * P], turned[:])
 
-        picked0 = keep.tile([P, 2, C1], U32, name="picked0", align_bytes=64)
-        for u, (start, width) in enumerate(((pair0, T), (pair1, C1 + SPARE))):
-            window = planes[:, start : start + width].bitcast(U32)
-            nc.vector.tensor_copy(picked0[:, u, :], window.indirect(entries(slot_of, 0, C1)))
-        grouped0 = keep.tile([P, 2 * C1], U32, name="grouped0", align_bytes=64)
-        nc.vector.tensor_copy(
-            grouped0[:].rearrange("p (j u) -> p j u", u=2).bitcast(I32),
-            picked0[:].rearrange("p u j -> p j u").bitcast(I32),
-        )
-        scales0 = quantise(grouped0, codes0, C1, "0")
+        picked0 = []
+        for half in range(2):
+            picked = keep.tile([P, 2, PIECE], U32, name=f"picked0{half}", align_bytes=64)
+            for u, (start, width) in enumerate(((pair0, T), (pair1, C1 + SPARE))):
+                window = planes[:, start : start + width].bitcast(U32)
+                nc.vector.tensor_copy(picked[:, u, :], window.indirect(entries(slot_of, half * PIECE, PIECE)))
+            picked0.append(picked)
+        for b, bank in enumerate((2, 3, 5)):
+            activate(1, b, block_sums(1, b, bank))
+        activate(1, 3, block_sums(1, 3, 2))
 
-        for start, u, bank in ((pair2, 0, 1), (pair3, 1, 4)):
+        def turn_plane(start, u, bank):
             turned = psum.tile([P, C1], F32, name="turned", tag=f"bank{bank}")
             for b in range(C1 // P):
                 turn_pairs(turned[:, b * P : (b + 1) * P], 1, b, u)
             nc.scalar.copy(planes[:, start : start + C1], turned[:])
 
-        y0 = psum.tile([P, C1], F32, name="y0", tag="bank4")
-        experts(y0, 0, 4, codes0, scales0)
-
         picked1 = keep.tile([P, 2 * C1], F32, name="picked1", align_bytes=64)
-        for u, start in enumerate((pair2, pair3)):
+
+        def pick(start, u):
             window = planes[:, start - C1 : start + C1].bitcast(U32)
             nc.vector.tensor_copy(
                 picked1[:, u * C1 : (u + 1) * C1].bitcast(U32), window.indirect(entries(slot_of, C1, C1))
             )
+
+        quantise(weave(picked0[0][:], "hidden12"), 0)
+        turn_plane(pair2, 0, 1)
+        pick(pair2, 0)
+        quantise(weave(picked0[1][:], "hidden13"), 1)
+        y1 = expert_pair(1, 0)
+        turn_plane(pair3, 1, 4)
+        pick(pair3, 1)
+        y0 = expert_pair(0, 4)
         staged = keep.tile([P, PIECE], F32, name="staged", align_bytes=64)
-        nc.scalar.copy(staged[:], y0[:, 0:PIECE])
+        nc.scalar.copy(staged[:], y0[:])
         place(0, PIECE, staged[:])
         grouped1 = keep.tile([P, 2 * C1], U32, name="grouped1", align_bytes=64)
         nc.scalar.copy(
@@ -230,13 +251,13 @@ def tile_moe_hie_silu_kernel(
             picked1[:].bitcast(U32).rearrange("p (u j) -> p j u", u=2),
         )
         codes1 = keep.tile([P, C1], U32, name="codes1", align_bytes=64)
-        scales1 = quantise(grouped1, codes1, C1, "1")
-        y1 = psum.tile([P, C1], F32, name="y1", tag="bank5")
-        experts(y1, 4, 4, codes1, scales1)
-        staged = picked1[:, 0:PIECE]
-        nc.scalar.copy(staged, y0[:, PIECE:C1])
-        place(PIECE, PIECE, staged)
+        scales1 = keep.tile([P, C1], U8, name="scales1b", align_bytes=64)
+        nc.vector.quantize_mx(codes1[:].bitcast(FP8X4), scales1[:], grouped1[:].bitcast(BF16))
+        y2 = psum.tile([P, C1], F32, name="y2", tag="bank7")
+        experts(y2, 4, 4, codes1, scales1)
+        nc.scalar.copy(picked1[:, 0:PIECE], y1[:])
+        place(PIECE, PIECE, picked1[:, 0:PIECE])
         last = keep.tile([P, C1], F32, name="last", align_bytes=64)
-        nc.scalar.copy(last[:], y1[:])
+        nc.scalar.copy(last[:], y2[:])
         place(C1, C1, last[:])
         nc.sync.dma_start(out, placed[:])

@@ -164,15 +164,6 @@ def tile_moe_hie_silu_kernel(
                     stop=True,
                 )
 
-        def weave(parts, tag):
-            grouped = keep.tile([P, 2 * PIECE], U32, name="grouped", tag=tag, align_bytes=64)
-            nc.scalar.copy(grouped[:].rearrange("p (j u) -> p j u", u=2), parts.rearrange("p u j -> p j u"))
-            return grouped
-
-        def quantise(grouped, half):
-            cols = slice(half * PIECE, (half + 1) * PIECE)
-            nc.vector.quantize_mx(codes0[:, cols].bitcast(FP8X4), scales0[:, cols], grouped[:].bitcast(BF16))
-
         def expert_pair(half, bank):
             cols = slice(half * PIECE, (half + 1) * PIECE)
             y = psum.tile([P, PIECE], F32, name="y", tag=f"bank{bank}")
@@ -209,13 +200,10 @@ def tile_moe_hie_silu_kernel(
                     turn_pairs(turned[:, u, n * P : (n + 1) * P], 0, b, u)
             copy(both_pairs[:, :, blocks[0] * P : (blocks[-1] + 1) * P], turned[:])
 
-        picked0 = []
-        for half in range(2):
-            picked = keep.tile([P, 2, PIECE], U32, name=f"picked0{half}", align_bytes=64)
-            for u, (start, width) in enumerate(((pair0, T), (pair1, C1 + SPARE))):
-                window = planes[:, start : start + width].bitcast(U32)
-                nc.vector.tensor_copy(picked[:, u, :], window.indirect(entries(slot_of, half * PIECE, PIECE)))
-            picked0.append(picked)
+        picked0 = keep.tile([P, 2, C1], U32, name="picked0", align_bytes=64)
+        for u, (start, width) in enumerate(((pair0, T), (pair1, C1 + SPARE))):
+            window = planes[:, start : start + width].bitcast(U32)
+            nc.vector.tensor_copy(picked0[:, u, :], window.indirect(entries(slot_of, 0, C1)))
         for b, bank in enumerate((2, 3, 5)):
             activate(1, b, block_sums(1, b, bank))
         activate(1, 3, block_sums(1, 3, 2))
@@ -234,14 +222,18 @@ def tile_moe_hie_silu_kernel(
                 picked1[:, u * C1 : (u + 1) * C1].bitcast(U32), window.indirect(entries(slot_of, C1, C1))
             )
 
-        quantise(weave(picked0[0][:], "hidden12"), 0)
+        grouped0 = keep.tile([P, 2 * C1], U32, name="grouped0", align_bytes=64)
+        nc.vector.tensor_copy(
+            grouped0[:].rearrange("p (j u) -> p j u", u=2).bitcast(I32),
+            picked0[:].rearrange("p u j -> p j u").bitcast(I32),
+        )
+        nc.vector.quantize_mx(codes0[:].bitcast(FP8X4), scales0[:], grouped0[:].bitcast(BF16))
         turn_plane(pair2, 0, 1)
         pick(pair2, 0)
-        quantise(weave(picked0[1][:], "hidden13"), 1)
-        y1 = expert_pair(1, 0)
         turn_plane(pair3, 1, 4)
         pick(pair3, 1)
         y0 = expert_pair(0, 4)
+        y1 = expert_pair(1, 0)
         staged = keep.tile([P, PIECE], F32, name="staged", align_bytes=64)
         nc.scalar.copy(staged[:], y0[:])
         place(0, PIECE, staged[:])

@@ -24,6 +24,7 @@ LANES = 16
 SPARE = 192
 WARM_UP = 4
 EARLY = 384
+DROP = 16
 
 
 def entries(offsets, first, count):
@@ -51,10 +52,10 @@ def tile_moe_hie_silu_kernel(
         nc.vector.memset(wgs[:].bitcast(I32), 0)
         nc.vector.memset(lowered[:].bitcast(I32), 0)
         nc.vector.memset(wes[:].bitcast(I32), 0)
-        codes0 = keep.tile([P, C1], U32, name="codes0", align_bytes=64)
-        scales0 = keep.tile([P, C1], U8, name="scales0", align_bytes=64)
-        nc.vector.memset(codes0[:].bitcast(I32), 0)
-        nc.vector.memset(scales0[:].bitcast(I32), 0)
+        codes1 = keep.tile([P, C1], U32, name="codes1", align_bytes=64)
+        scales1 = keep.tile([P, C1], U8, name="scales1", align_bytes=64)
+        nc.vector.memset(codes1[:].bitcast(I32), 0)
+        nc.vector.memset(scales1[:].bitcast(I32), 0)
 
         def load_scale_rows(plane, rows, count, quadrants):
             for q in quadrants:
@@ -72,9 +73,10 @@ def tile_moe_hie_silu_kernel(
             return words
 
         nc.sync.dma_start(token_of[:], offs)
-        for q in range(4):
-            queue = nc.sync if q % 2 else nc.scalar
-            queue.dma_start(xs[32 * q : 32 * q + 8, :].bitcast(I32), x_scales[:, 4 * q : 4 * q + 4, :].bitcast(I32))
+        token_rows = x_scales.bitcast(I32).rearrange("s (q r) w -> r q s w", r=4)
+        for r in range(4):
+            queue = nc.sync if r % 2 else nc.scalar
+            queue.dma_start(xs[r:P:DROP, :].bitcast(I32), token_rows[r])
         group_rows = wg_scales.rearrange("f s r i -> (f s) r i")
         load_scale_rows(wgs, group_rows, G * PASSES, range(1))
         xw = keep.tile([P, PASSES * T], I32, name="xw", align_bytes=64)
@@ -92,7 +94,7 @@ def tile_moe_hie_silu_kernel(
             for row, count in ((0, 64), (64, 32), (96, 4)):
                 queue.dma_start(
                     lowered[row : row + count, cols].bitcast(I32),
-                    in_place[row + 4 : row + 4 + count, cols].bitcast(I32),
+                    in_place[row + DROP : row + DROP + count, cols].bitcast(I32),
                 )
         slot_scales = (in_place, lowered)
         wgw.append(load_group_words(1))
@@ -110,10 +112,11 @@ def tile_moe_hie_silu_kernel(
         identity = keep.tile([P, P], F32, name="identity")
         make_identity(nc, identity[:])
 
-        pair0, pair1, spare, pair2 = 0, C1, 2 * C1, 2 * C1 + SPARE
+        pair0, pair1, pair2 = 0, C1 + SPARE, 2 * (C1 + SPARE)
         pair3 = pair2 + C1
         planes = keep.tile([P, pair3 + C1], F32, name="planes", align_bytes=64)
-        nc.gpsimd.memset(planes[:, spare : spare + SPARE], 0.0)
+        for start in (pair0, pair1):
+            nc.gpsimd.memset(planes[:, start + C1 : start + C1 + SPARE], 0.0)
 
         def gather_words(f, cuts):
             for s in range(PASSES):
@@ -178,41 +181,36 @@ def tile_moe_hie_silu_kernel(
             )
 
         gather_words(0, [(0, 0, P), (1, 0, P), (0, P, P), (1, P, P), (0, PIECE, PIECE), (1, 2 * P, P), (1, 3 * P, P)])
-        gather_words(1, [(0, 0, PIECE), (1, 0, PIECE), (0, PIECE, PIECE), (1, PIECE, PIECE)])
+        gather_words(1, [(0, 0, PIECE), (1, 0, P), (1, P, P), (0, PIECE, PIECE), (1, PIECE, PIECE)])
         warm = psum.tile([P, H], F32, name="warm", tag="bank7")
         for n in range(WARM_UP):
             nc.tensor.matmul_mx(
                 warm[:],
-                lhsT=codes0[:, 0:P].bitcast(FP8X4),
+                lhsT=codes1[:, 0:P].bitcast(FP8X4),
                 lhsT_scale=in_place[:, 0:P],
-                rhs=codes0[:].bitcast(FP8X4),
-                rhs_scale=scales0[:],
+                rhs=codes1[:].bitcast(FP8X4),
+                rhs_scale=scales1[:],
                 start=True,
                 stop=True,
             )
         for b in range(C1 // P):
             activate(0, b, block_sums(0, b, b))
-        both_pairs = planes[:, pair0:spare].rearrange("p (u j) -> p u j", u=2)
-        for blocks, bank, copy in (((0, 1), 5, nc.scalar.copy), ((2,), 6, nc.scalar.copy), ((3,), 7, nc.vector.tensor_copy)):
-            turned = psum.tile([P, 2, len(blocks) * P], F32, name="turned", tag=f"bank{bank}")
+
+        def turn_plane(f, start, u, blocks, bank):
+            turned = psum.tile([P, len(blocks) * P], F32, name="turned", tag=f"bank{bank}")
             for n, b in enumerate(blocks):
-                for u in range(2):
-                    turn_pairs(turned[:, u, n * P : (n + 1) * P], 0, b, u)
-            copy(both_pairs[:, :, blocks[0] * P : (blocks[-1] + 1) * P], turned[:])
+                turn_pairs(turned[:, n * P : (n + 1) * P], f, b, u)
+            nc.scalar.copy(planes[:, start + blocks[0] * P : start + (blocks[-1] + 1) * P], turned[:])
 
+        activate(1, 0, block_sums(1, 0, 6))
+        turn_plane(0, pair0, 0, range(4), 2)
+        turn_plane(0, pair1, 1, range(4), 3)
         picked0 = keep.tile([P, 2, C1], U32, name="picked0", align_bytes=64)
-        for u, (start, width) in enumerate(((pair0, T), (pair1, C1 + SPARE))):
-            window = planes[:, start : start + width].bitcast(U32)
-            nc.vector.tensor_copy(picked0[:, u, :], window.indirect(entries(slot_of, 0, C1)))
-        for b, bank in enumerate((2, 3, 5)):
+        for u, start, first, width in ((0, pair0, 0, C1), (1, pair1, 0, PIECE), (1, pair1, PIECE, PIECE)):
+            window = planes[:, start : start + C1 + SPARE].bitcast(U32)
+            nc.vector.tensor_copy(picked0[:, u, first : first + width], window.indirect(entries(slot_of, first, width)))
+        for b, bank in ((1, 6), (2, 2), (3, 3)):
             activate(1, b, block_sums(1, b, bank))
-        activate(1, 3, block_sums(1, 3, 2))
-
-        def turn_plane(start, u, bank):
-            turned = psum.tile([P, C1], F32, name="turned", tag=f"bank{bank}")
-            for b in range(C1 // P):
-                turn_pairs(turned[:, b * P : (b + 1) * P], 1, b, u)
-            nc.scalar.copy(planes[:, start : start + C1], turned[:])
 
         picked1 = keep.tile([P, 2 * C1], F32, name="picked1", align_bytes=64)
 
@@ -223,27 +221,33 @@ def tile_moe_hie_silu_kernel(
             )
 
         grouped0 = keep.tile([P, 2 * C1], U32, name="grouped0", align_bytes=64)
-        nc.vector.tensor_copy(
-            grouped0[:].rearrange("p (j u) -> p j u", u=2).bitcast(I32),
-            picked0[:].rearrange("p u j -> p j u").bitcast(I32),
-        )
-        nc.vector.quantize_mx(codes0[:].bitcast(FP8X4), scales0[:], grouped0[:].bitcast(BF16))
-        turn_plane(pair2, 0, 1)
+        for first in (0, PIECE):
+            nc.vector.tensor_copy(
+                grouped0[:, 2 * first : 2 * (first + PIECE)].rearrange("p (j u) -> p j u", u=2).bitcast(I32),
+                picked0[:, :, first : first + PIECE].rearrange("p u j -> p j u").bitcast(I32),
+            )
+        codes0 = keep.tile([P, C1], U32, name="codes0", align_bytes=64)
+        scales0 = keep.tile([P, C1], U8, name="scales0", align_bytes=64)
+        for first in (0, PIECE):
+            cols = slice(first, first + PIECE)
+            nc.vector.quantize_mx(
+                codes0[:, cols].bitcast(FP8X4), scales0[:, cols], grouped0[:, 2 * first : 2 * (first + PIECE)].bitcast(BF16)
+            )
+        turn_plane(1, pair2, 0, range(3), 2)
+        turn_plane(1, pair2, 0, range(3, 4), 4)
         pick(pair2, 0)
-        turn_plane(pair3, 1, 4)
+        turn_plane(1, pair3, 1, range(4), 3)
         pick(pair3, 1)
-        y0 = expert_pair(0, 4)
-        y1 = expert_pair(1, 0)
+        y0 = expert_pair(0, 3)
+        y1 = expert_pair(1, 4)
         staged = keep.tile([P, PIECE], F32, name="staged", align_bytes=64)
         nc.scalar.copy(staged[:], y0[:])
         place(0, PIECE, staged[:])
-        grouped1 = keep.tile([P, 2 * C1], U32, name="grouped1", align_bytes=64)
+        grouped1 = keep.tile([P, 2 * C1], U32, name="grouped1", tag="codes0", align_bytes=64)
         nc.scalar.copy(
             grouped1[:].rearrange("p (j u) -> p j u", u=2),
             picked1[:].bitcast(U32).rearrange("p (u j) -> p j u", u=2),
         )
-        codes1 = keep.tile([P, C1], U32, name="codes1", align_bytes=64)
-        scales1 = keep.tile([P, C1], U8, name="scales1b", align_bytes=64)
         nc.vector.quantize_mx(codes1[:].bitcast(FP8X4), scales1[:], grouped1[:].bitcast(BF16))
         y2 = psum.tile([P, C1], F32, name="y2", tag="bank7")
         experts(y2, 4, 4, codes1, scales1)

@@ -149,10 +149,20 @@ def tile_moe_hie_silu_kernel(
                 acc[:].rearrange("j (p u e) -> j u p e", u=2, e=2),
                 SILU,
             )
-            hidden[f, b] = h
+            for u in range(2):
+                hidden[f, b, u] = h[:].bitcast(F32)[:, u * P : (u + 1) * P]
+
+        def activate_plane(f, b, u, acc):
+            h = keep.tile([P, H // 2], BF16, name="h", tag=f"hidden{f}{b}{u}", align_bytes=64)
+            nc.scalar.activation(
+                h[:].rearrange("j (p e) -> j p e", e=2),
+                acc[:].rearrange("j (p u e) -> j u p e", u=2, e=2)[:, u],
+                SILU,
+            )
+            hidden[f, b, u] = h[:].bitcast(F32)
 
         def turn_pairs(into, f, b, u):
-            nc.tensor.transpose(into, hidden[f, b][:].bitcast(F32)[:, u * P : (u + 1) * P], identity[:])
+            nc.tensor.transpose(into, hidden[f, b, u], identity[:])
 
         def experts(y, first_expert, count, codes, scales):
             for b in range(count):
@@ -181,7 +191,7 @@ def tile_moe_hie_silu_kernel(
             )
 
         gather_words(0, [(0, 0, P), (1, 0, P), (0, P, P), (1, P, P), (0, PIECE, PIECE), (1, 2 * P, P), (1, 3 * P, P)])
-        gather_words(1, [(0, 0, PIECE), (1, 0, P), (1, P, P), (0, PIECE, PIECE), (1, PIECE, PIECE)])
+        gather_words(1, [(0, 0, PIECE), (1, 0, PIECE), (0, PIECE, PIECE), (1, PIECE, PIECE)])
         warm = psum.tile([P, H], F32, name="warm", tag="bank7")
         for n in range(WARM_UP):
             nc.tensor.matmul_mx(
@@ -193,8 +203,11 @@ def tile_moe_hie_silu_kernel(
                 start=True,
                 stop=True,
             )
-        for b in range(C1 // P):
+        for b in range(3):
             activate(0, b, block_sums(0, b, b))
+        last_sums = block_sums(0, 3, 3)
+        for u in range(2):
+            activate_plane(0, 3, u, last_sums)
 
         def turn_plane(f, start, u, blocks, bank):
             turned = psum.tile([P, len(blocks) * P], F32, name="turned", tag=f"bank{bank}")
@@ -202,15 +215,19 @@ def tile_moe_hie_silu_kernel(
                 turn_pairs(turned[:, n * P : (n + 1) * P], f, b, u)
             nc.scalar.copy(planes[:, start + blocks[0] * P : start + (blocks[-1] + 1) * P], turned[:])
 
-        activate(1, 0, block_sums(1, 0, 6))
-        turn_plane(0, pair0, 0, range(4), 2)
-        turn_plane(0, pair1, 1, range(4), 3)
+        turn_plane(0, pair0, 0, range(4), 1)
+        turn_plane(0, pair1, 1, range(4), 2)
+        activate(1, 0, block_sums(1, 0, 3))
         picked0 = keep.tile([P, 2, C1], U32, name="picked0", align_bytes=64)
         for u, start, first, width in ((0, pair0, 0, C1), (1, pair1, 0, PIECE), (1, pair1, PIECE, PIECE)):
             window = planes[:, start : start + C1 + SPARE].bitcast(U32)
             nc.vector.tensor_copy(picked0[:, u, first : first + width], window.indirect(entries(slot_of, first, width)))
-        for b, bank in ((1, 6), (2, 2), (3, 3)):
+        for b, bank in ((1, 1), (2, 2)):
             activate(1, b, block_sums(1, b, bank))
+        last_sums = block_sums(1, 3, 3)
+        activate_plane(1, 3, 0, last_sums)
+        turn_plane(1, pair2, 0, range(3), 1)
+        activate_plane(1, 3, 1, last_sums)
 
         picked1 = keep.tile([P, 2 * C1], F32, name="picked1", align_bytes=64)
 
@@ -233,12 +250,11 @@ def tile_moe_hie_silu_kernel(
             nc.vector.quantize_mx(
                 codes0[:, cols].bitcast(FP8X4), scales0[:, cols], grouped0[:, 2 * first : 2 * (first + PIECE)].bitcast(BF16)
             )
-        turn_plane(1, pair2, 0, range(3), 2)
         turn_plane(1, pair2, 0, range(3, 4), 4)
         pick(pair2, 0)
-        turn_plane(1, pair3, 1, range(4), 3)
+        turn_plane(1, pair3, 1, range(4), 2)
         pick(pair3, 1)
-        y0 = expert_pair(0, 3)
+        y0 = expert_pair(0, 2)
         y1 = expert_pair(1, 4)
         staged = keep.tile([P, PIECE], F32, name="staged", align_bytes=64)
         nc.scalar.copy(staged[:], y0[:])

@@ -73,6 +73,7 @@ def tile_moe_hie_silu_kernel(
             return words
 
         nc.sync.dma_start(token_of[:], offs)
+        wgw = [load_group_words(0)]
         token_rows = x_scales.bitcast(I32).rearrange("s (q r) w -> r q s w", r=4)
         for r in range(4):
             queue = nc.sync if r % 2 else nc.scalar
@@ -84,7 +85,6 @@ def tile_moe_hie_silu_kernel(
             xw[:].rearrange("p (s t) -> p s t", s=PASSES),
             x_words.rearrange("s p t d -> p s (t d)").bitcast(I32),
         )
-        wgw = [load_group_words(0)]
         load_scale_rows(wgs, group_rows, G * PASSES, range(1, 4))
         slot_words, hidden = {}, {}
         in_place = keep.tile([P, T], U8, name="in_place", align_bytes=64)

@@ -23,6 +23,7 @@ PIECE = 256
 LANES = 16
 SPARE = 192
 WARM_UP = 4
+FIRST = 192
 EARLY = 384
 DROP = 16
 
@@ -72,8 +73,8 @@ def tile_moe_hie_silu_kernel(
             )
             return words
 
-        nc.sync.dma_start(token_of[:], offs)
         wgw = [load_group_words(0)]
+        nc.sync.dma_start(token_of[:], offs)
         token_rows = x_scales.bitcast(I32).rearrange("s (q r) w -> r q s w", r=4)
         for r in range(4):
             queue = nc.sync if r % 2 else nc.scalar
@@ -177,12 +178,6 @@ def tile_moe_hie_silu_kernel(
                     stop=True,
                 )
 
-        def expert_pair(half, bank):
-            cols = slice(half * PIECE, (half + 1) * PIECE)
-            y = psum.tile([P, PIECE], F32, name="y", tag=f"bank{bank}")
-            experts(y, 2 * half, 2, codes0[:, cols], scales0[:, cols])
-            return y
-
         placed = keep.tile([P, T], F32, name="placed")
 
         def place(first, width, staged):
@@ -231,10 +226,11 @@ def tile_moe_hie_silu_kernel(
 
         picked1 = keep.tile([P, 2 * C1], F32, name="picked1", align_bytes=64)
 
-        def pick(start, u):
+        def pick(start, u, first, width):
             window = planes[:, start - C1 : start + C1].bitcast(U32)
             nc.vector.tensor_copy(
-                picked1[:, u * C1 : (u + 1) * C1].bitcast(U32), window.indirect(entries(slot_of, C1, C1))
+                picked1[:, u * C1 + first : u * C1 + first + width].bitcast(U32),
+                window.indirect(entries(slot_of, C1 + first, width)),
             )
 
         grouped0 = keep.tile([P, 2 * C1], U32, name="grouped0", align_bytes=64)
@@ -251,24 +247,26 @@ def tile_moe_hie_silu_kernel(
                 codes0[:, cols].bitcast(FP8X4), scales0[:, cols], grouped0[:, 2 * first : 2 * (first + PIECE)].bitcast(BF16)
             )
         turn_plane(1, pair2, 0, range(3, 4), 4)
-        pick(pair2, 0)
+        pick(pair2, 0, 0, C1)
         turn_plane(1, pair3, 1, range(4), 2)
-        pick(pair3, 1)
-        y0 = expert_pair(0, 2)
-        y1 = expert_pair(1, 4)
-        staged = keep.tile([P, PIECE], F32, name="staged", align_bytes=64)
-        nc.scalar.copy(staged[:], y0[:])
-        place(0, PIECE, staged[:])
+        pick(pair3, 1, 0, PIECE)
+        pick(pair3, 1, PIECE, PIECE)
+        y0 = psum.tile([P, C1], F32, name="y0", tag="bank2")
+        experts(y0, 0, 4, codes0, scales0)
+        staged = keep.tile([P, FIRST], F32, name="staged", align_bytes=64)
+        nc.scalar.copy(staged[:], y0[:, 0:FIRST])
+        place(0, FIRST, staged[:])
         grouped1 = keep.tile([P, 2 * C1], U32, name="grouped1", tag="codes0", align_bytes=64)
-        nc.scalar.copy(
-            grouped1[:].rearrange("p (j u) -> p j u", u=2),
-            picked1[:].bitcast(U32).rearrange("p (u j) -> p j u", u=2),
-        )
+        for first in (0, PIECE):
+            nc.scalar.copy(
+                grouped1[:, 2 * first : 2 * (first + PIECE)].rearrange("p (j u) -> p j u", u=2),
+                picked1[:].bitcast(U32).rearrange("p (u j) -> p j u", u=2)[:, first : first + PIECE, :],
+            )
         nc.vector.quantize_mx(codes1[:].bitcast(FP8X4), scales1[:], grouped1[:].bitcast(BF16))
         y2 = psum.tile([P, C1], F32, name="y2", tag="bank7")
         experts(y2, 4, 4, codes1, scales1)
-        nc.scalar.copy(picked1[:, 0:PIECE], y1[:])
-        place(PIECE, PIECE, picked1[:, 0:PIECE])
+        nc.scalar.copy(picked1[:, FIRST:C1], y0[:, FIRST:C1])
+        place(FIRST, C1 - FIRST, picked1[:, FIRST:C1])
         last = keep.tile([P, C1], F32, name="last", align_bytes=64)
         nc.scalar.copy(last[:], y2[:])
         place(C1, C1, last[:])

@@ -186,7 +186,7 @@ def tile_moe_hie_silu_kernel(
             )
 
         gather_words(0, [(0, 0, P), (1, 0, P), (0, P, P), (1, P, P), (0, PIECE, PIECE), (1, 2 * P, P), (1, 3 * P, P)])
-        gather_words(1, [(0, 0, PIECE), (1, 0, PIECE), (0, PIECE, PIECE), (1, PIECE, PIECE)])
+        gather_words(1, [(0, 0, C1), (1, 0, PIECE), (1, PIECE, PIECE)])
         warm = psum.tile([P, H], F32, name="warm", tag="bank7")
         for n in range(WARM_UP):
             nc.tensor.matmul_mx(
@@ -210,7 +210,8 @@ def tile_moe_hie_silu_kernel(
                 turn_pairs(turned[:, n * P : (n + 1) * P], f, b, u)
             nc.scalar.copy(planes[:, start + blocks[0] * P : start + (blocks[-1] + 1) * P], turned[:])
 
-        turn_plane(0, pair0, 0, range(4), 1)
+        turn_plane(0, pair0, 0, range(3), 1)
+        turn_plane(0, pair0, 0, range(3, 4), 5)
         turn_plane(0, pair1, 1, range(4), 2)
         activate(1, 0, block_sums(1, 0, 3))
         picked0 = keep.tile([P, 2, C1], U32, name="picked0", align_bytes=64)

@@ -91,7 +91,8 @@ def tile_moe_hie_silu_kernel(
         in_place = keep.tile([P, T], U8, name="in_place", align_bytes=64)
         for first, width, queue in ((0, EARLY, nc.scalar), (EARLY, T - EARLY, nc.sync)):
             cols = slice(first, first + width)
-            nc.vector.tensor_copy(in_place[:, cols], xs[:].indirect(entries(token_of, first, width)))
+            for start, count in ((0, P), (P, EARLY - P)) if first == 0 else ((first, width),):
+                nc.vector.tensor_copy(in_place[:, start : start + count], xs[:].indirect(entries(token_of, start, count)))
             for row, count in ((0, 64), (64, 32), (96, 4)):
                 queue.dma_start(
                     lowered[row : row + count, cols].bitcast(I32),

@@ -15,6 +15,7 @@ U8 = mybir.dt.uint8
 FP8X4 = mybir.dt.float8_e4m3fn_x4
 FP4X4 = mybir.dt.float4_e2m1fn_x4
 SILU = mybir.ActivationFunctionType.Silu
+COPY = mybir.ActivationFunctionType.Copy
 MULT = mybir.AluOpType.mult
 
 P = 128
@@ -22,8 +23,6 @@ PASSES = K // 512
 PIECE = 256
 LANES = 16
 SPARE = 192
-WARM_UP = 4
-FIRST = 192
 EARLY = 384
 DROP = 16
 
@@ -53,10 +52,6 @@ def tile_moe_hie_silu_kernel(
         nc.vector.memset(wgs[:].bitcast(I32), 0)
         nc.vector.memset(lowered[:].bitcast(I32), 0)
         nc.vector.memset(wes[:].bitcast(I32), 0)
-        codes1 = keep.tile([P, C1], U32, name="codes1", align_bytes=64)
-        scales1 = keep.tile([P, C1], U8, name="scales1", align_bytes=64)
-        nc.vector.memset(codes1[:].bitcast(I32), 0)
-        nc.vector.memset(scales1[:].bitcast(I32), 0)
 
         def load_scale_rows(plane, rows, count, quadrants):
             for q in quadrants:
@@ -88,28 +83,23 @@ def tile_moe_hie_silu_kernel(
         )
         load_scale_rows(wgs, group_rows, G * PASSES, range(1, 4))
         slot_words, hidden = {}, {}
-        in_place = keep.tile([P, T], U8, name="in_place", align_bytes=64)
-        for first, width, queue in ((0, EARLY, nc.scalar), (EARLY, T - EARLY, nc.sync)):
-            cols = slice(first, first + width)
-            for start, count in ((0, P), (P, EARLY - P)) if first == 0 else ((first, width),):
-                nc.vector.tensor_copy(in_place[:, start : start + count], xs[:].indirect(entries(token_of, start, count)))
+        in_place = {}
+
+        def gather_scales(first, width, tag, queue):
+            tile = keep.tile([P, width], U8, name="in_place", tag=tag, align_bytes=64)
+            nc.vector.tensor_copy(tile[:], xs[:].indirect(entries(token_of, first, width)))
             for row, count in ((0, 64), (64, 32), (96, 4)):
                 queue.dma_start(
-                    lowered[row : row + count, cols].bitcast(I32),
-                    in_place[row + DROP : row + DROP + count, cols].bitcast(I32),
+                    lowered[row : row + count, first : first + width].bitcast(I32),
+                    tile[row + DROP : row + DROP + count, :].bitcast(I32),
                 )
-        slot_scales = (in_place, lowered)
+            for start in range(0, width, P):
+                in_place[first + start] = tile[:, start : start + P]
+
+        gather_scales(0, EARLY, "first_scales", nc.scalar)
+        gather_scales(EARLY, EARLY, "middle_scales", nc.sync)
         wgw.append(load_group_words(1))
         nc.sync.dma_start(slot_of[:], offs2)
-        nc.sync.dma_start(column_of[:], dst)
-        load_scale_rows(wes, we_scales.rearrange("e s r n -> (e s) r n"), E, range(4))
-        wew = keep.tile([P, E * N], I32, name="wew", align_bytes=64)
-        nc.sync.dma_start(
-            wew[:].rearrange("p (e n) -> p e n", e=E),
-            we_words.rearrange("e s p n d -> p (e s) (n d)").bitcast(I32),
-        )
-        weight = keep.tile([P, T], F32, name="weight", align_bytes=64)
-        nc.sync.dma_start(weight[:], gate)
 
         identity = keep.tile([P, P], F32, name="identity")
         make_identity(nc, identity[:])
@@ -121,22 +111,22 @@ def tile_moe_hie_silu_kernel(
             nc.gpsimd.memset(planes[:, start + C1 : start + C1 + SPARE], 0.0)
 
         def gather_words(f, cuts):
-            for s in range(PASSES):
-                slot_words[f, s] = keep.tile([P, C1], U32, name="words", tag=f"slot_words{f}{s}", align_bytes=64)
-            for s, first, width in cuts:
+            for s, first, width, tag in cuts:
+                words = keep.tile([P, width], U32, name="words", tag=tag, align_bytes=64)
                 nc.vector.tensor_copy(
-                    slot_words[f, s][:, first : first + width],
-                    xw[:, s * T : (s + 1) * T].bitcast(U32).indirect(entries(token_of, f * C1 + first, width)),
+                    words[:], xw[:, s * T : (s + 1) * T].bitcast(U32).indirect(entries(token_of, f * C1 + first, width))
                 )
+                for start in range(0, width, P):
+                    slot_words[f, s, (first + start) // P] = words[:, start : start + P]
 
         def block_sums(f, b, bank):
             acc = psum.tile([P, H], F32, name="acc", tag=f"bank{bank}")
-            cols = slice(b * P, (b + 1) * P)
+            first = f * C1 + b * P
             for s in range(PASSES):
                 nc.tensor.matmul_mx(
                     acc[:],
-                    lhsT=slot_words[f, s][:, cols].bitcast(FP8X4),
-                    lhsT_scale=slot_scales[s][:, f * C1 + b * P : f * C1 + (b + 1) * P],
+                    lhsT=slot_words[f, s, b].bitcast(FP8X4),
+                    lhsT_scale=lowered[:, first : first + P] if s else in_place[first],
                     rhs=wgw[f][:, s * 2 * H : (s + 1) * 2 * H].bitcast(FP4X4),
                     rhs_scale=wgs[:, (f * PASSES + s) * H : (f * PASSES + s + 1) * H],
                     start=(s == 0),
@@ -179,28 +169,22 @@ def tile_moe_hie_silu_kernel(
                     stop=True,
                 )
 
-        placed = keep.tile([P, T], F32, name="placed")
 
-        def place(first, width, staged):
-            nc.vector.tensor_tensor(
-                placed[:].indirect(entries(column_of, first, width)), staged, weight[:, first : first + width], MULT
-            )
-
-        gather_words(0, [(0, 0, P), (1, 0, P), (0, P, P), (1, P, P), (0, PIECE, PIECE), (1, 2 * P, P), (1, 3 * P, P)])
-        gather_words(1, [(0, 0, C1), (1, 0, PIECE), (1, PIECE, PIECE)])
-        warm = psum.tile([P, H], F32, name="warm", tag="bank7")
-        for n in range(WARM_UP):
-            nc.tensor.matmul_mx(
-                warm[:],
-                lhsT=codes1[:, 0:P].bitcast(FP8X4),
-                lhsT_scale=in_place[:, 0:P],
-                rhs=codes1[:].bitcast(FP8X4),
-                rhs_scale=scales1[:],
-                start=True,
-                stop=True,
-            )
+        cuts = [(0, 0, P), (1, 0, P), (0, P, P), (1, P, P), (0, PIECE, PIECE), (1, 2 * P, P), (1, 3 * P, P)]
+        gather_words(0, [(s, first, width, f"words{s}{first}") for s, first, width in cuts])
         for b in range(3):
             activate(0, b, block_sums(0, b, b))
+        gather_scales(2 * EARLY, T - 2 * EARLY, "words00", nc.sync)
+        weight = keep.tile([P, T], F32, name="weight", align_bytes=64)
+        nc.sync.dma_start(weight[:], gate)
+        load_scale_rows(wes, we_scales.rearrange("e s r n -> (e s) r n"), E, range(4))
+        wew = keep.tile([P, E * N], I32, name="wew", align_bytes=64)
+        nc.sync.dma_start(
+            wew[:].rearrange("p (e n) -> p e n", e=E),
+            we_words.rearrange("e s p n d -> p (e s) (n d)").bitcast(I32),
+        )
+        nc.sync.dma_start(column_of[:], dst)
+        gather_words(1, [(0, 0, C1, "words10"), (1, 0, PIECE, "words0128"), (1, PIECE, PIECE, "words1128")])
         last_sums = block_sums(0, 3, 3)
         for u in range(2):
             activate_plane(0, 3, u, last_sums)
@@ -215,6 +199,22 @@ def tile_moe_hie_silu_kernel(
         turn_plane(0, pair0, 0, range(3, 4), 5)
         turn_plane(0, pair1, 1, range(4), 2)
         activate(1, 0, block_sums(1, 0, 3))
+
+        def weave(first, width, pairs, tag):
+            grouped = keep.tile([P, width, 2], U32, name="grouped", tag=tag, align_bytes=64)
+            nc.vector.tensor_copy(
+                grouped[:].bitcast(I32), pairs[:, :, first : first + width].rearrange("p u j -> p j u").bitcast(I32)
+            )
+            return grouped
+
+        def quantise(grouped, codes, scales):
+            nc.vector.quantize_mx(codes.bitcast(FP8X4), scales, grouped.rearrange("p j u -> p (j u)").bitcast(BF16))
+
+        def place(first, width, staged):
+            nc.vector.tensor_tensor(
+                placed[:].indirect(entries(column_of, first, width)), staged, weight[:, first : first + width], MULT
+            )
+
         picked0 = keep.tile([P, 2, C1], U32, name="picked0", align_bytes=64)
         for u, start, first, width in ((0, pair0, 0, C1), (1, pair1, 0, PIECE), (1, pair1, PIECE, PIECE)):
             window = planes[:, start : start + C1 + SPARE].bitcast(U32)
@@ -226,50 +226,60 @@ def tile_moe_hie_silu_kernel(
         turn_plane(1, pair2, 0, range(3), 1)
         activate_plane(1, 3, 1, last_sums)
 
-        picked1 = keep.tile([P, 2 * C1], F32, name="picked1", align_bytes=64)
-
-        def pick(start, u, first, width):
-            window = planes[:, start - C1 : start + C1].bitcast(U32)
-            nc.vector.tensor_copy(
-                picked1[:, u * C1 + first : u * C1 + first + width].bitcast(U32),
-                window.indirect(entries(slot_of, C1 + first, width)),
-            )
-
-        grouped0 = keep.tile([P, 2 * C1], U32, name="grouped0", align_bytes=64)
-        for first in (0, PIECE):
-            nc.vector.tensor_copy(
-                grouped0[:, 2 * first : 2 * (first + PIECE)].rearrange("p (j u) -> p j u", u=2).bitcast(I32),
-                picked0[:, :, first : first + PIECE].rearrange("p u j -> p j u").bitcast(I32),
-            )
-        codes0 = keep.tile([P, C1], U32, name="codes0", align_bytes=64)
-        scales0 = keep.tile([P, C1], U8, name="scales0", align_bytes=64)
-        for first in (0, PIECE):
-            cols = slice(first, first + PIECE)
-            nc.vector.quantize_mx(
-                codes0[:, cols].bitcast(FP8X4), scales0[:, cols], grouped0[:, 2 * first : 2 * (first + PIECE)].bitcast(BF16)
-            )
+        grouped0 = [weave(first, PIECE, picked0, f"grouped{first}") for first in (0, PIECE)]
+        codes0 = [keep.tile([P, PIECE], U32, name=f"codes0{h}", align_bytes=64) for h in range(2)]
+        scales0 = [keep.tile([P, PIECE], U8, name=f"scales0{h}", align_bytes=64) for h in range(2)]
+        for h in range(2):
+            quantise(grouped0[h][:], codes0[h][:], scales0[h][:])
         turn_plane(1, pair2, 0, range(3, 4), 4)
-        pick(pair2, 0, 0, C1)
         turn_plane(1, pair3, 1, range(4), 2)
-        pick(pair3, 1, 0, PIECE)
-        pick(pair3, 1, PIECE, PIECE)
-        y0 = psum.tile([P, C1], F32, name="y0", tag="bank2")
-        experts(y0, 0, 4, codes0, scales0)
-        staged = keep.tile([P, FIRST], F32, name="staged", align_bytes=64)
-        nc.scalar.copy(staged[:], y0[:, 0:FIRST])
-        place(0, FIRST, staged[:])
-        grouped1 = keep.tile([P, 2 * C1], U32, name="grouped1", tag="codes0", align_bytes=64)
-        for first in (0, PIECE):
-            nc.scalar.copy(
-                grouped1[:, 2 * first : 2 * (first + PIECE)].rearrange("p (j u) -> p j u", u=2),
-                picked1[:].bitcast(U32).rearrange("p (u j) -> p j u", u=2)[:, first : first + PIECE, :],
-            )
-        nc.vector.quantize_mx(codes1[:].bitcast(FP8X4), scales1[:], grouped1[:].bitcast(BF16))
-        y2 = psum.tile([P, C1], F32, name="y2", tag="bank7")
-        experts(y2, 4, 4, codes1, scales1)
-        nc.scalar.copy(picked1[:, FIRST:C1], y0[:, FIRST:C1])
-        place(FIRST, C1 - FIRST, picked1[:, FIRST:C1])
-        last = keep.tile([P, C1], F32, name="last", align_bytes=64)
-        nc.scalar.copy(last[:], y2[:])
-        place(C1, C1, last[:])
+        placed = keep.tile([P, T], F32, name="placed", tag="hidden131", align_bytes=64)
+
+        def results(first, quantised, bank):
+            y = psum.tile([P, PIECE], F32, name="y", tag=f"bank{bank}")
+            experts(y, first // C2, 2, *quantised)
+            return y
+
+        def stage(y, tag):
+            staged = keep.tile([P, PIECE], F32, name="staged", tag=tag, align_bytes=64)
+            nc.scalar.copy(staged[:], y[:])
+            return staged
+
+        def pick(picked, start, u, first):
+            window = planes[:, start - C1 : start + C1].bitcast(U32)
+            nc.vector.tensor_copy(picked[:, u, :], window.indirect(entries(slot_of, first, PIECE)))
+
+        def quantised(grouped, name):
+            codes = keep.tile([P, PIECE], U32, name=f"codes{name}", align_bytes=64)
+            scales = keep.tile([P, PIECE], U8, name=f"scales{name}", align_bytes=64)
+            quantise(grouped[:], codes[:], scales[:])
+            return codes, scales
+
+        def woven(picked, name):
+            grouped = keep.tile([P, PIECE, 2], U32, name=name, align_bytes=64)
+            nc.scalar.copy(grouped[:], picked[:].rearrange("p u j -> p j u"))
+            return grouped
+
+        gated = keep.tile([P, PIECE], F32, name="gated", align_bytes=64)
+        nc.vector.tensor_tensor(gated[:], results(0, (codes0[0], scales0[0]), 1)[:], weight[:, 0:PIECE], MULT)
+        waiting = results(PIECE, (codes0[1], scales0[1]), 2)
+        second = keep.tile([P, C2], F32, name="second", align_bytes=64)
+        nc.scalar.copy(second[:], waiting[:, 0:C2])
+        nc.scalar.activation(placed[:].indirect(entries(column_of, 0, PIECE)), gated[:], COPY)
+        early = keep.tile([P, 2, PIECE], U32, name="early", tag="codes00", align_bytes=64)
+        pick(early, pair2, 0, C1)
+        pick(early, pair3, 1, C1)
+        late = keep.tile([P, 2, PIECE], U32, name="late", tag="codes01", align_bytes=64)
+        pick(late, pair2, 0, C1 + PIECE)
+        pick(late, pair3, 1, C1 + PIECE)
+        grouped = [woven(early, "grouped10")]
+        held = keep.tile([P, C2], F32, name="held", tag="codes00", align_bytes=64)
+        nc.scalar.copy(held[:], waiting[:, C2:PIECE])
+        grouped.append(woven(late, "grouped11"))
+        place(PIECE, C2, second[:])
+        third = stage(results(C1, quantised(grouped[0], "10"), 7), "third")
+        place(PIECE + C2, C2, held[:])
+        fourth = stage(results(C1 + PIECE, quantised(grouped[1], "11"), 5), "fourth")
+        place(C1, PIECE, third[:])
+        place(C1 + PIECE, PIECE, fourth[:])
         nc.sync.dma_start(out, placed[:])

@@ -83,23 +83,27 @@ def tile_moe_hie_silu_kernel(
         )
         load_scale_rows(wgs, group_rows, G * PASSES, range(1, 4))
         slot_words, hidden = {}, {}
-        in_place = {}
-
-        def gather_scales(first, width, tag, queue):
-            tile = keep.tile([P, width], U8, name="in_place", tag=tag, align_bytes=64)
-            nc.vector.tensor_copy(tile[:], xs[:].indirect(entries(token_of, first, width)))
+        in_place = keep.tile([P, T], U8, name="in_place", align_bytes=64)
+        for first, width, queue in ((0, EARLY, nc.scalar), (EARLY, T - EARLY, nc.sync)):
+            cols = slice(first, first + width)
+            nc.vector.tensor_copy(in_place[:, cols], xs[:].indirect(entries(token_of, first, width)))
             for row, count in ((0, 64), (64, 32), (96, 4)):
                 queue.dma_start(
-                    lowered[row : row + count, first : first + width].bitcast(I32),
-                    tile[row + DROP : row + DROP + count, :].bitcast(I32),
+                    lowered[row : row + count, cols].bitcast(I32),
+                    in_place[row + DROP : row + DROP + count, cols].bitcast(I32),
                 )
-            for start in range(0, width, P):
-                in_place[first + start] = tile[:, start : start + P]
-
-        gather_scales(0, EARLY, "first_scales", nc.scalar)
-        gather_scales(EARLY, EARLY, "middle_scales", nc.sync)
+        slot_scales = (in_place, lowered)
         wgw.append(load_group_words(1))
         nc.sync.dma_start(slot_of[:], offs2)
+        nc.sync.dma_start(column_of[:], dst)
+        weight = keep.tile([P, T], F32, name="weight", align_bytes=64)
+        nc.sync.dma_start(weight[:], gate)
+        load_scale_rows(wes, we_scales.rearrange("e s r n -> (e s) r n"), E, range(4))
+        wew = keep.tile([P, E * N], I32, name="wew", align_bytes=64)
+        nc.sync.dma_start(
+            wew[:].rearrange("p (e n) -> p e n", e=E),
+            we_words.rearrange("e s p n d -> p (e s) (n d)").bitcast(I32),
+        )
 
         identity = keep.tile([P, P], F32, name="identity")
         make_identity(nc, identity[:])
@@ -111,22 +115,22 @@ def tile_moe_hie_silu_kernel(
             nc.gpsimd.memset(planes[:, start + C1 : start + C1 + SPARE], 0.0)
 
         def gather_words(f, cuts):
-            for s, first, width, tag in cuts:
-                words = keep.tile([P, width], U32, name="words", tag=tag, align_bytes=64)
+            for s in range(PASSES):
+                slot_words[f, s] = keep.tile([P, C1], U32, name="words", tag=f"slot_words{f}{s}", align_bytes=64)
+            for s, first, width in cuts:
                 nc.vector.tensor_copy(
-                    words[:], xw[:, s * T : (s + 1) * T].bitcast(U32).indirect(entries(token_of, f * C1 + first, width))
+                    slot_words[f, s][:, first : first + width],
+                    xw[:, s * T : (s + 1) * T].bitcast(U32).indirect(entries(token_of, f * C1 + first, width)),
                 )
-                for start in range(0, width, P):
-                    slot_words[f, s, (first + start) // P] = words[:, start : start + P]
 
         def block_sums(f, b, bank):
             acc = psum.tile([P, H], F32, name="acc", tag=f"bank{bank}")
-            first = f * C1 + b * P
+            cols = slice(b * P, (b + 1) * P)
             for s in range(PASSES):
                 nc.tensor.matmul_mx(
                     acc[:],
-                    lhsT=slot_words[f, s, b].bitcast(FP8X4),
-                    lhsT_scale=lowered[:, first : first + P] if s else in_place[first],
+                    lhsT=slot_words[f, s][:, cols].bitcast(FP8X4),
+                    lhsT_scale=slot_scales[s][:, f * C1 + b * P : f * C1 + (b + 1) * P],
                     rhs=wgw[f][:, s * 2 * H : (s + 1) * 2 * H].bitcast(FP4X4),
                     rhs_scale=wgs[:, (f * PASSES + s) * H : (f * PASSES + s + 1) * H],
                     start=(s == 0),
@@ -170,21 +174,10 @@ def tile_moe_hie_silu_kernel(
                 )
 
 
-        cuts = [(0, 0, P), (1, 0, P), (0, P, P), (1, P, P), (0, PIECE, PIECE), (1, 2 * P, P), (1, 3 * P, P)]
-        gather_words(0, [(s, first, width, f"words{s}{first}") for s, first, width in cuts])
+        gather_words(0, [(0, 0, P), (1, 0, P), (0, P, P), (1, P, P), (0, PIECE, PIECE), (1, 2 * P, P), (1, 3 * P, P)])
+        gather_words(1, [(0, 0, C1), (1, 0, PIECE), (1, PIECE, PIECE)])
         for b in range(3):
             activate(0, b, block_sums(0, b, b))
-        gather_scales(2 * EARLY, T - 2 * EARLY, "words00", nc.sync)
-        weight = keep.tile([P, T], F32, name="weight", align_bytes=64)
-        nc.sync.dma_start(weight[:], gate)
-        load_scale_rows(wes, we_scales.rearrange("e s r n -> (e s) r n"), E, range(4))
-        wew = keep.tile([P, E * N], I32, name="wew", align_bytes=64)
-        nc.sync.dma_start(
-            wew[:].rearrange("p (e n) -> p e n", e=E),
-            we_words.rearrange("e s p n d -> p (e s) (n d)").bitcast(I32),
-        )
-        nc.sync.dma_start(column_of[:], dst)
-        gather_words(1, [(0, 0, C1, "words10"), (1, 0, PIECE, "words0128"), (1, PIECE, PIECE, "words1128")])
         last_sums = block_sums(0, 3, 3)
         for u in range(2):
             activate_plane(0, 3, u, last_sums)

@@ -233,11 +233,6 @@ def tile_moe_hie_silu_kernel(
             experts(y, first // C2, 2, *quantised)
             return y
 
-        def stage(y, tag):
-            staged = keep.tile([P, PIECE], F32, name="staged", tag=tag, align_bytes=64)
-            nc.scalar.copy(staged[:], y[:])
-            return staged
-
         def pick(picked, start, u, first):
             window = planes[:, start - C1 : start + C1].bitcast(U32)
             nc.vector.tensor_copy(picked[:, u, :], window.indirect(entries(slot_of, first, PIECE)))
@@ -248,31 +243,28 @@ def tile_moe_hie_silu_kernel(
             quantise(grouped[:], codes[:], scales[:])
             return codes, scales
 
-        def woven(picked, name):
-            grouped = keep.tile([P, PIECE, 2], U32, name=name, align_bytes=64)
-            nc.scalar.copy(grouped[:], picked[:].rearrange("p u j -> p j u"))
-            return grouped
+        def gate_and_place(y, first, width):
+            gated = keep.tile([P, width], F32, name=f"gated{first}", align_bytes=64)
+            nc.vector.tensor_tensor(gated[:], y[:, 0:width], weight[:, first : first + width], MULT)
+            return lambda: nc.scalar.activation(placed[:].indirect(entries(column_of, first, width)), gated[:], COPY)
 
-        gated = keep.tile([P, PIECE], F32, name="gated", align_bytes=64)
-        nc.vector.tensor_tensor(gated[:], results(0, (codes0[0], scales0[0]), 1)[:], weight[:, 0:PIECE], MULT)
-        waiting = results(PIECE, (codes0[1], scales0[1]), 2)
-        second = keep.tile([P, C2], F32, name="second", align_bytes=64)
-        nc.scalar.copy(second[:], waiting[:, 0:C2])
-        nc.scalar.activation(placed[:].indirect(entries(column_of, 0, PIECE)), gated[:], COPY)
-        early = keep.tile([P, 2, PIECE], U32, name="early", tag="codes00", align_bytes=64)
+        early = keep.tile([P, 2, PIECE], U32, name="early", align_bytes=64)
         pick(early, pair2, 0, C1)
+        gate_and_place(results(0, (codes0[0], scales0[0]), 4), 0, PIECE)()
         pick(early, pair3, 1, C1)
+        waiting = results(PIECE, (codes0[1], scales0[1]), 2)
+        scatter = gate_and_place(waiting, PIECE, C2)
+        held = keep.tile([P, C2], F32, name="held", align_bytes=64)
+        nc.scalar.copy(held[:], waiting[:, C2:PIECE])
+        scatter()
         late = keep.tile([P, 2, PIECE], U32, name="late", tag="codes01", align_bytes=64)
         pick(late, pair2, 0, C1 + PIECE)
         pick(late, pair3, 1, C1 + PIECE)
-        grouped = [woven(early, "grouped10")]
-        held = keep.tile([P, C2], F32, name="held", tag="codes00", align_bytes=64)
-        nc.scalar.copy(held[:], waiting[:, C2:PIECE])
-        grouped.append(woven(late, "grouped11"))
-        place(PIECE, C2, second[:])
-        third = stage(results(C1, quantised(grouped[0], "10"), 7), "third")
+        grouped = [weave(0, PIECE, early, "codes00"), weave(0, PIECE, late, "grouped11")]
+        last = keep.tile([P, C1], F32, name="last", align_bytes=64)
+        for h, bank in enumerate((7, 5)):
+            y = results(C1 + h * PIECE, quantised(grouped[h], f"1{h}"), bank)
+            nc.scalar.copy(last[:, h * PIECE : (h + 1) * PIECE], y[:])
         place(PIECE + C2, C2, held[:])
-        fourth = stage(results(C1 + PIECE, quantised(grouped[1], "11"), 5), "fourth")
-        place(C1, PIECE, third[:])
-        place(C1 + PIECE, PIECE, fourth[:])
+        place(C1, C1, last[:])
         nc.sync.dma_start(out, placed[:])

@@ -17,6 +17,7 @@ FP4X4 = mybir.dt.float4_e2m1fn_x4
 SILU = mybir.ActivationFunctionType.Silu
 COPY = mybir.ActivationFunctionType.Copy
 MULT = mybir.AluOpType.mult
+ADD = mybir.AluOpType.add
 
 P = 128
 PASSES = K // 512
@@ -25,6 +26,7 @@ LANES = 16
 SPARE = 192
 EARLY = 384
 DROP = 16
+STORES = 4
 
 
 def entries(offsets, first, count):
@@ -52,6 +54,9 @@ def tile_moe_hie_silu_kernel(
         nc.vector.memset(wgs[:].bitcast(I32), 0)
         nc.vector.memset(lowered[:].bitcast(I32), 0)
         nc.vector.memset(wes[:].bitcast(I32), 0)
+        by_scalar = keep.tile([P, T], F32, name="by_scalar", align_bytes=64)
+        by_vector = keep.tile([P, T], F32, name="by_vector", align_bytes=64)
+        nc.vector.memset(by_scalar[:], 0.0)
 
         def load_scale_rows(plane, rows, count, quadrants):
             for q in quadrants:
@@ -105,6 +110,7 @@ def tile_moe_hie_silu_kernel(
             we_words.rearrange("e s p n d -> p (e s) (n d)").bitcast(I32),
         )
 
+        nc.gpsimd.memset(by_vector[:], 0.0)
         identity = keep.tile([P, P], F32, name="identity")
         make_identity(nc, identity[:])
 
@@ -203,11 +209,6 @@ def tile_moe_hie_silu_kernel(
         def quantise(grouped, codes, scales):
             nc.vector.quantize_mx(codes.bitcast(FP8X4), scales, grouped.rearrange("p j u -> p (j u)").bitcast(BF16))
 
-        def place(first, width, staged):
-            nc.vector.tensor_tensor(
-                placed[:].indirect(entries(column_of, first, width)), staged, weight[:, first : first + width], MULT
-            )
-
         picked0 = keep.tile([P, 2, C1], U32, name="picked0", align_bytes=64)
         for u, start, first, width in ((0, pair0, 0, C1), (1, pair1, 0, PIECE), (1, pair1, PIECE, PIECE)):
             window = planes[:, start : start + C1 + SPARE].bitcast(U32)
@@ -226,7 +227,6 @@ def tile_moe_hie_silu_kernel(
             quantise(grouped0[h][:], codes0[h][:], scales0[h][:])
         turn_plane(1, pair2, 0, range(3, 4), 4)
         turn_plane(1, pair3, 1, range(4), 2)
-        placed = keep.tile([P, T], F32, name="placed", tag="hidden131", align_bytes=64)
 
         def results(first, quantised, bank):
             y = psum.tile([P, PIECE], F32, name="y", tag=f"bank{bank}")
@@ -243,28 +243,40 @@ def tile_moe_hie_silu_kernel(
             quantise(grouped[:], codes[:], scales[:])
             return codes, scales
 
-        def gate_and_place(y, first, width):
-            gated = keep.tile([P, width], F32, name=f"gated{first}", align_bytes=64)
-            nc.vector.tensor_tensor(gated[:], y[:, 0:width], weight[:, first : first + width], MULT)
-            return lambda: nc.scalar.activation(placed[:].indirect(entries(column_of, first, width)), gated[:], COPY)
+        def apply_gate(gated, y, first):
+            nc.vector.tensor_tensor(gated, y[:], weight[:, first : first + PIECE], MULT)
+
+        def scalar_places(first, width, gated):
+            nc.scalar.activation(by_scalar[:].indirect(entries(column_of, first, width)), gated, COPY)
+
+        def vector_places(first, width, gated):
+            nc.vector.tensor_copy(by_vector[:].indirect(entries(column_of, first, width)), gated)
 
         early = keep.tile([P, 2, PIECE], U32, name="early", align_bytes=64)
         pick(early, pair2, 0, C1)
-        gate_and_place(results(0, (codes0[0], scales0[0]), 4), 0, PIECE)()
+        gated0 = keep.tile([P, PIECE], F32, name="gated0", tag="hidden131", align_bytes=64)
+        apply_gate(gated0[:], results(0, (codes0[0], scales0[0]), 4), 0)
+        scalar_places(0, PIECE, gated0[:])
         pick(early, pair3, 1, C1)
-        waiting = results(PIECE, (codes0[1], scales0[1]), 2)
-        scatter = gate_and_place(waiting, PIECE, C2)
-        held = keep.tile([P, C2], F32, name="held", align_bytes=64)
-        nc.scalar.copy(held[:], waiting[:, C2:PIECE])
-        scatter()
+        gated1 = keep.tile([P, PIECE], F32, name="gated1", align_bytes=64)
+        apply_gate(gated1[:], results(PIECE, (codes0[1], scales0[1]), 2), PIECE)
+        scalar_places(PIECE, PIECE, gated1[:])
         late = keep.tile([P, 2, PIECE], U32, name="late", tag="codes01", align_bytes=64)
         pick(late, pair2, 0, C1 + PIECE)
+        grouped_early = weave(0, PIECE, early, "scales01")
         pick(late, pair3, 1, C1 + PIECE)
-        grouped = [weave(0, PIECE, early, "codes00"), weave(0, PIECE, late, "grouped11")]
+        quantised_early = quantised(grouped_early, "10")
+        quantised_late = quantised(weave(0, PIECE, late, "grouped11"), "11")
         last = keep.tile([P, C1], F32, name="last", align_bytes=64)
-        for h, bank in enumerate((7, 5)):
-            y = results(C1 + h * PIECE, quantised(grouped[h], f"1{h}"), bank)
-            nc.scalar.copy(last[:, h * PIECE : (h + 1) * PIECE], y[:])
-        place(PIECE + C2, C2, held[:])
-        place(C1, C1, last[:])
-        nc.sync.dma_start(out, placed[:])
+        apply_gate(last[:, 0:PIECE], results(C1, quantised_early, 7), C1)
+        vector_places(C1, C2, last[:, 0:C2])
+        scalar_places(C1 + C2, C2, last[:, C2:PIECE])
+        apply_gate(last[:, PIECE:C1], results(C1 + PIECE, quantised_late, 5), C1 + PIECE)
+        scalar_places(C1 + PIECE, C2, last[:, PIECE : PIECE + C2])
+        vector_places(T - C2, C2, last[:, C1 - C2 : C1])
+        width = T // STORES
+        for c in range(STORES):
+            cols = slice(c * width, (c + 1) * width)
+            total = keep.tile([P, width], F32, name=f"total{c}", align_bytes=64)
+            nc.vector.tensor_tensor(total[:], by_scalar[:, cols], by_vector[:, cols], ADD)
+            nc.sync.dma_start(out[:, cols], total[:])

@@ -50,13 +50,20 @@ def tile_moe_hie_silu_kernel(
         lowered = keep.tile([P, T], U8, name="lowered", align_bytes=64)
         wgs = keep.tile([P, G * PASSES * H], U8, name="wgs", align_bytes=64)
         wes = keep.tile([P, E * N], U8, name="wes", align_bytes=64)
-        nc.gpsimd.memset(xs[:].bitcast(I32), 0)
+        nc.vector.memset(xs[:].bitcast(I32), 0)
         nc.vector.memset(wgs[:].bitcast(I32), 0)
         nc.vector.memset(lowered[:].bitcast(I32), 0)
+        pair0, pair1, pair2 = 0, C1 + SPARE, 2 * (C1 + SPARE)
+        pair3 = pair2 + C1
+        planes = keep.tile([P, pair3 + C1], F32, name="planes", align_bytes=64)
+        for start in (pair0, pair1):
+            nc.vector.memset(planes[:, start + C1 : start + C1 + SPARE], 0.0)
+        identity = keep.tile([P, P], F32, name="identity")
+        nc.vector.memset(identity[:], 0.0)
+        make_identity(nc, identity[:], nomemset=True)
         nc.vector.memset(wes[:].bitcast(I32), 0)
         by_scalar = keep.tile([P, T], F32, name="by_scalar", align_bytes=64)
         by_vector = keep.tile([P, T], F32, name="by_vector", align_bytes=64)
-        nc.vector.memset(by_scalar[:], 0.0)
 
         def load_scale_rows(plane, rows, count, quadrants):
             for q in quadrants:
@@ -79,6 +86,9 @@ def tile_moe_hie_silu_kernel(
         for r in range(4):
             queue = nc.sync if r % 2 else nc.scalar
             queue.dma_start(xs[r:P:DROP, :].bitcast(I32), token_rows[r])
+        zeros = planes[:, C1 : C1 + P].unsqueeze(1).to_broadcast([P, T // P, P])
+        for window in (by_scalar, by_vector):
+            nc.scalar.copy(window[:].rearrange("p (c j) -> p c j", j=P), zeros)
         group_rows = wg_scales.rearrange("f s r i -> (f s) r i")
         load_scale_rows(wgs, group_rows, G * PASSES, range(1))
         xw = keep.tile([P, PASSES * T], I32, name="xw", align_bytes=64)
@@ -110,15 +120,6 @@ def tile_moe_hie_silu_kernel(
             we_words.rearrange("e s p n d -> p (e s) (n d)").bitcast(I32),
         )
 
-        nc.gpsimd.memset(by_vector[:], 0.0)
-        identity = keep.tile([P, P], F32, name="identity")
-        make_identity(nc, identity[:])
-
-        pair0, pair1, pair2 = 0, C1 + SPARE, 2 * (C1 + SPARE)
-        pair3 = pair2 + C1
-        planes = keep.tile([P, pair3 + C1], F32, name="planes", align_bytes=64)
-        for start in (pair0, pair1):
-            nc.gpsimd.memset(planes[:, start + C1 : start + C1 + SPARE], 0.0)
 
         def gather_words(f, cuts):
             for s in range(PASSES):
@@ -244,22 +245,24 @@ def tile_moe_hie_silu_kernel(
             return codes, scales
 
         def apply_gate(gated, y, first):
-            nc.vector.tensor_tensor(gated, y[:], weight[:, first : first + PIECE], MULT)
+            nc.vector.tensor_tensor(gated, y, weight[:, first : first + y.shape[1]], MULT)
 
         def scalar_places(first, width, gated):
             nc.scalar.activation(by_scalar[:].indirect(entries(column_of, first, width)), gated, COPY)
 
         def vector_places(first, width, gated):
-            nc.vector.tensor_copy(by_vector[:].indirect(entries(column_of, first, width)), gated)
+            nc.vector.tensor_tensor(
+                by_vector[:].indirect(entries(column_of, first, width)), gated, weight[:, first : first + width], MULT
+            )
 
         early = keep.tile([P, 2, PIECE], U32, name="early", align_bytes=64)
         pick(early, pair2, 0, C1)
         gated0 = keep.tile([P, PIECE], F32, name="gated0", tag="hidden131", align_bytes=64)
-        apply_gate(gated0[:], results(0, (codes0[0], scales0[0]), 4), 0)
+        apply_gate(gated0[:], results(0, (codes0[0], scales0[0]), 4)[:], 0)
         scalar_places(0, PIECE, gated0[:])
         pick(early, pair3, 1, C1)
         gated1 = keep.tile([P, PIECE], F32, name="gated1", align_bytes=64)
-        apply_gate(gated1[:], results(PIECE, (codes0[1], scales0[1]), 2), PIECE)
+        apply_gate(gated1[:], results(PIECE, (codes0[1], scales0[1]), 2)[:], PIECE)
         scalar_places(PIECE, PIECE, gated1[:])
         late = keep.tile([P, 2, PIECE], U32, name="late", tag="codes01", align_bytes=64)
         pick(late, pair2, 0, C1 + PIECE)
@@ -268,10 +271,14 @@ def tile_moe_hie_silu_kernel(
         quantised_early = quantised(grouped_early, "10")
         quantised_late = quantised(weave(0, PIECE, late, "grouped11"), "11")
         last = keep.tile([P, C1], F32, name="last", align_bytes=64)
-        apply_gate(last[:, 0:PIECE], results(C1, quantised_early, 7), C1)
+        y = results(C1, quantised_early, 7)
+        nc.vector.tensor_copy(last[:, 0:C2], y[:, 0:C2])
+        apply_gate(last[:, C2:PIECE], y[:, C2:PIECE], C1 + C2)
         vector_places(C1, C2, last[:, 0:C2])
         scalar_places(C1 + C2, C2, last[:, C2:PIECE])
-        apply_gate(last[:, PIECE:C1], results(C1 + PIECE, quantised_late, 5), C1 + PIECE)
+        y = results(C1 + PIECE, quantised_late, 5)
+        apply_gate(last[:, PIECE : PIECE + C2], y[:, 0:C2], C1 + PIECE)
+        nc.vector.tensor_copy(last[:, C1 - C2 : C1], y[:, C2:PIECE])
         scalar_places(C1 + PIECE, C2, last[:, PIECE : PIECE + C2])
         vector_places(T - C2, C2, last[:, C1 - C2 : C1])
         width = T // STORES

@@ -26,7 +26,8 @@ LANES = 16
 SPARE = 192
 EARLY = 384
 DROP = 16
-STORES = 4
+STORES = (320, 320, 256, 128)
+SHARE = 224
 
 
 def entries(offsets, first, count):
@@ -181,7 +182,7 @@ def tile_moe_hie_silu_kernel(
                 )
 
 
-        gather_words(0, [(0, 0, P), (1, 0, P), (0, P, P), (1, P, P), (0, PIECE, PIECE), (1, 2 * P, P), (1, 3 * P, P)])
+        gather_words(0, [(0, 0, P), (1, 0, P), (0, P, 3 * P), (1, P, P), (1, PIECE, PIECE)])
         gather_words(1, [(0, 0, C1), (1, 0, PIECE), (1, PIECE, PIECE)])
         for b in range(3):
             activate(0, b, block_sums(0, b, b))
@@ -266,24 +267,18 @@ def tile_moe_hie_silu_kernel(
         scalar_places(PIECE, PIECE, gated1[:])
         late = keep.tile([P, 2, PIECE], U32, name="late", tag="codes01", align_bytes=64)
         pick(late, pair2, 0, C1 + PIECE)
-        grouped_early = weave(0, PIECE, early, "scales01")
         pick(late, pair3, 1, C1 + PIECE)
-        quantised_early = quantised(grouped_early, "10")
-        quantised_late = quantised(weave(0, PIECE, late, "grouped11"), "11")
+        grouped = [weave(0, PIECE, early, "scales01"), weave(0, PIECE, late, "grouped11")]
+        halves = [quantised(grouped[h], f"1{h}") for h in range(2)]
         last = keep.tile([P, C1], F32, name="last", align_bytes=64)
-        y = results(C1, quantised_early, 7)
-        nc.vector.tensor_copy(last[:, 0:C2], y[:, 0:C2])
-        apply_gate(last[:, C2:PIECE], y[:, C2:PIECE], C1 + C2)
-        vector_places(C1, C2, last[:, 0:C2])
-        scalar_places(C1 + C2, C2, last[:, C2:PIECE])
-        y = results(C1 + PIECE, quantised_late, 5)
-        apply_gate(last[:, PIECE : PIECE + C2], y[:, 0:C2], C1 + PIECE)
-        nc.vector.tensor_copy(last[:, C1 - C2 : C1], y[:, C2:PIECE])
-        scalar_places(C1 + PIECE, C2, last[:, PIECE : PIECE + C2])
-        vector_places(T - C2, C2, last[:, C1 - C2 : C1])
-        width = T // STORES
-        for c in range(STORES):
-            cols = slice(c * width, (c + 1) * width)
+        third, fourth = results(C1, halves[0], 7), results(C1 + PIECE, halves[1], 5)
+        apply_gate(last[:, 0:SHARE], third[:, 0:SHARE], C1)
+        scalar_places(C1, SHARE, last[:, 0:SHARE])
+        nc.vector.tensor_copy(last[:, SHARE:PIECE], third[:, SHARE:PIECE])
+        nc.vector.tensor_copy(last[:, PIECE:C1], fourth[:])
+        vector_places(C1 + SHARE, C1 - SHARE, last[:, SHARE:C1])
+        for c, width in enumerate(STORES):
+            cols = slice(sum(STORES[:c]), sum(STORES[: c + 1]))
             total = keep.tile([P, width], F32, name=f"total{c}", align_bytes=64)
             nc.vector.tensor_tensor(total[:], by_scalar[:, cols], by_vector[:, cols], ADD)
             nc.sync.dma_start(out[:, cols], total[:])

@@ -182,7 +182,7 @@ def tile_moe_hie_silu_kernel(
                 )
 
 
-        gather_words(0, [(0, 0, P), (1, 0, P), (0, P, 3 * P), (1, P, P), (1, PIECE, PIECE)])
+        gather_words(0, [(0, 0, P), (1, 0, P), (0, P, P), (1, P, P), (0, PIECE, PIECE), (1, 2 * P, P), (1, 3 * P, P)])
         gather_words(1, [(0, 0, C1), (1, 0, PIECE), (1, PIECE, PIECE)])
         for b in range(3):
             activate(0, b, block_sums(0, b, b))

@@ -182,7 +182,7 @@ def tile_moe_hie_silu_kernel(
                 )
 
 
-        gather_words(0, [(0, 0, P), (1, 0, P), (0, P, P), (1, P, P), (0, PIECE, PIECE), (1, 2 * P, P), (1, 3 * P, P)])
+        gather_words(0, [(s, b * P, P) for b in range(4) for s in range(PASSES)])
         gather_words(1, [(0, 0, C1), (1, 0, PIECE), (1, PIECE, PIECE)])
         for b in range(3):
             activate(0, b, block_sums(0, b, b))

@@ -217,7 +217,7 @@ def tile_moe_hie_silu_kernel(
             nc.vector.tensor_copy(picked0[:, u, first : first + width], window.indirect(entries(slot_of, first, width)))
         for b, bank in ((1, 1), (2, 2)):
             activate(1, b, block_sums(1, b, bank))
-        last_sums = block_sums(1, 3, 3)
+        last_sums = block_sums(1, 3, 5)
         activate_plane(1, 3, 0, last_sums)
         turn_plane(1, pair2, 0, range(3), 1)
         activate_plane(1, 3, 1, last_sums)

@@ -1,7 +1,6 @@
 from contextlib import ExitStack
 
 import concourse.mybir as mybir
-from concourse.masks import make_identity
 
 K, T, G, C1, E, C2, H, N = 1024, 1024, 2, 512, 8, 128, 512, 128
 FLOPS = 2 * K * H * T + 2 * H * N * T
@@ -21,13 +20,13 @@ ADD = mybir.AluOpType.add
 
 P = 128
 PASSES = K // 512
-PIECE = 256
+HALF = 256
 LANES = 16
-SPARE = 192
-EARLY = 384
+QUADRANTS = 4
 DROP = 16
+GATE_AT = 1216
+PAIRS_AT = ((0, 512), (256, 768), (0, 1024), (1280, 1728))
 STORES = (320, 320, 256, 128)
-SHARE = 224
 
 
 def entries(offsets, first, count):
@@ -48,131 +47,165 @@ def tile_moe_hie_silu_kernel(
         column_of = lists.tile([P, T // LANES], U16, name="column_of")
 
         xs = keep.tile([P, T], U8, name="xs", align_bytes=64)
-        lowered = keep.tile([P, T], U8, name="lowered", align_bytes=64)
-        wgs = keep.tile([P, G * PASSES * H], U8, name="wgs", align_bytes=64)
+        wg_rows = keep.tile([P, PASSES * H], U8, name="wg_rows", align_bytes=64)
+        wg_lowered = keep.tile([P, PASSES * H], U8, name="wg_lowered", align_bytes=64)
+        slot_scales = [keep.tile([P, PASSES * C1], U8, name=f"slot_scales{f}", align_bytes=64) for f in range(G)]
         wes = keep.tile([P, E * N], U8, name="wes", align_bytes=64)
-        nc.vector.memset(xs[:].bitcast(I32), 0)
-        nc.vector.memset(wgs[:].bitcast(I32), 0)
-        nc.vector.memset(lowered[:].bitcast(I32), 0)
-        pair0, pair1, pair2 = 0, C1 + SPARE, 2 * (C1 + SPARE)
-        pair3 = pair2 + C1
-        planes = keep.tile([P, pair3 + C1], F32, name="planes", align_bytes=64)
-        for start in (pair0, pair1):
-            nc.vector.memset(planes[:, start + C1 : start + C1 + SPARE], 0.0)
-        identity = keep.tile([P, P], F32, name="identity")
-        nc.vector.memset(identity[:], 0.0)
-        make_identity(nc, identity[:], nomemset=True)
-        nc.vector.memset(wes[:].bitcast(I32), 0)
-        by_scalar = keep.tile([P, T], F32, name="by_scalar", align_bytes=64)
-        by_vector = keep.tile([P, T], F32, name="by_vector", align_bytes=64)
-
-        def load_scale_rows(plane, rows, count, quadrants):
-            for q in quadrants:
-                nc.sync.dma_start(
-                    plane[32 * q : 32 * q + 4, :].bitcast(I32).rearrange("r (c w) -> r c w", c=count),
-                    rows[:, 4 * q : 4 * q + 4, :].bitcast(I32).rearrange("c r w -> r c w"),
-                )
+        nc.vector.memset(wg_rows[:].bitcast(I32), 0)
+        nc.vector.memset(xs[32:64, :].bitcast(I32), 0)
+        nc.vector.memset(xs[64:P, :].bitcast(I32), 0)
+        for plane in (*slot_scales, wg_lowered, wes):
+            nc.vector.memset(plane[:].bitcast(I32), 0)
+        zeros = keep.tile([P, P], F32, name="zeros", align_bytes=64)
+        nc.vector.memset(zeros[:], 0.0)
 
         def load_group_words(f):
-            words = keep.tile([P, PASSES * 2 * H], U8, name=f"wgw{f}", align_bytes=64)
+            words = keep.tile([P, PASSES * 2 * H], U8, name=f"wg_raw{f}", align_bytes=64)
             nc.sync.dma_start(
                 words[:].bitcast(I32).rearrange("p (s b) -> p s b", s=PASSES),
                 wg_words[f].bitcast(I32).rearrange("s p b -> p s b"),
             )
             return words
 
-        wgw = [load_group_words(0)]
+        xw = keep.tile([P, PASSES * T], I32, name="xw", align_bytes=64)
+
+        def load_token_words(s):
+            nc.sync.dma_start(xw[:, s * T : (s + 1) * T], x_words[s].rearrange("p t d -> p (t d)").bitcast(I32))
+
+        def sort_group_words(f, raw):
+            words = keep.tile([P, PASSES * 2 * H], U8, name=f"wgw{f}", align_bytes=64)
+            for s in range(PASSES):
+                cols = slice(s * 2 * H, (s + 1) * 2 * H)
+                nc.scalar.copy(
+                    words[:, cols].bitcast(U16).rearrange("p (t m) -> p t m", t=4),
+                    raw[:, cols].bitcast(U16).rearrange("p (m t) -> p t m", t=4),
+                )
+            return words
+
+        def gather_scales(f, queue):
+            picked = keep.tile([P, C1], U8, name=f"picked_scales{f}", align_bytes=64)
+            nc.vector.tensor_copy(picked[:], xs[:].indirect(entries(token_of, f * C1, C1)))
+            for q in range(QUADRANTS):
+                queue.dma_start(
+                    slot_scales[f][32 * q : 32 * q + 4, :].bitcast(I32).rearrange("r (s w) -> r s w", s=PASSES),
+                    picked[8 * q : 8 * (q + 1), :].bitcast(I32),
+                )
+
         nc.sync.dma_start(token_of[:], offs)
-        token_rows = x_scales.bitcast(I32).rearrange("s (q r) w -> r q s w", r=4)
+        nc.scalar.dma_start(xs[0:32, :].bitcast(I32), x_scales.bitcast(I32).rearrange("s b w -> b s w"))
+        raw0 = load_group_words(0)
+        group_rows = wg_scales.bitcast(I32).rearrange("f s (q r) w -> r q (f s) w", r=4)
         for r in range(4):
             queue = nc.sync if r % 2 else nc.scalar
-            queue.dma_start(xs[r:P:DROP, :].bitcast(I32), token_rows[r])
-        zeros = planes[:, C1 : C1 + P].unsqueeze(1).to_broadcast([P, T // P, P])
-        for window in (by_scalar, by_vector):
-            nc.scalar.copy(window[:].rearrange("p (c j) -> p c j", j=P), zeros)
-        group_rows = wg_scales.rearrange("f s r i -> (f s) r i")
-        load_scale_rows(wgs, group_rows, G * PASSES, range(1))
-        xw = keep.tile([P, PASSES * T], I32, name="xw", align_bytes=64)
-        nc.sync.dma_start(
-            xw[:].rearrange("p (s t) -> p s t", s=PASSES),
-            x_words.rearrange("s p t d -> p s (t d)").bitcast(I32),
+            queue.dma_start(wg_rows[r:P:DROP, :].bitcast(I32), group_rows[r])
+        load_token_words(0)
+        raw1 = load_group_words(1)
+        load_token_words(1)
+        wgw = [sort_group_words(0, raw0)]
+        gather_scales(0, nc.sync)
+        gather_scales(1, nc.sync)
+        wg_sorted = keep.tile([P, PASSES * H], U8, name="wg_sorted", align_bytes=64)
+        nc.vector.tensor_copy(
+            wg_sorted[:].rearrange("p (s t m) -> p s t m", s=PASSES, t=4),
+            wg_rows[:].rearrange("p (s m t) -> p s t m", s=PASSES, t=4),
         )
-        load_scale_rows(wgs, group_rows, G * PASSES, range(1, 4))
-        slot_words, hidden = {}, {}
-        in_place = keep.tile([P, T], U8, name="in_place", align_bytes=64)
-        for first, width, queue in ((0, EARLY, nc.scalar), (EARLY, T - EARLY, nc.sync)):
-            cols = slice(first, first + width)
-            nc.vector.tensor_copy(in_place[:, cols], xs[:].indirect(entries(token_of, first, width)))
-            for row, count in ((0, 64), (64, 32), (96, 4)):
-                queue.dma_start(
-                    lowered[row : row + count, cols].bitcast(I32),
-                    in_place[row + DROP : row + DROP + count, cols].bitcast(I32),
-                )
-        slot_scales = (in_place, lowered)
-        wgw.append(load_group_words(1))
+        for row, count in ((0, 64), (64, 32), (96, 4)):
+            nc.sync.dma_start(
+                wg_lowered[row : row + count, :].bitcast(I32),
+                wg_sorted[row + DROP : row + DROP + count, :].bitcast(I32),
+            )
+        wgs = (wg_sorted, wg_lowered)
+        wgw.append(sort_group_words(1, raw1))
         nc.sync.dma_start(slot_of[:], offs2)
         nc.sync.dma_start(column_of[:], dst)
-        weight = keep.tile([P, T], F32, name="weight", align_bytes=64)
-        nc.sync.dma_start(weight[:], gate)
-        load_scale_rows(wes, we_scales.rearrange("e s r n -> (e s) r n"), E, range(4))
+        ring = keep.tile([P, GATE_AT + 2 * T], F32, name="ring", align_bytes=64)
+        weight = ring[:, GATE_AT:].rearrange("p (c j) -> p c j", j=2 * HALF)[:, :, 0:HALF]
+        nc.sync.dma_start(weight, gate.rearrange("p (c j) -> p c j", j=HALF))
+
+        def gate_of(first, width):
+            return weight[:, first // HALF, first % HALF : first % HALF + width]
+
+        expert_rows = we_scales.rearrange("e s r n -> (e s) r n")
+        for q in range(QUADRANTS):
+            nc.sync.dma_start(
+                wes[32 * q : 32 * q + 4, :].bitcast(I32).rearrange("r (c w) -> r c w", c=E),
+                expert_rows[:, 4 * q : 4 * q + 4, :].bitcast(I32).rearrange("c r w -> r c w"),
+            )
         wew = keep.tile([P, E * N], I32, name="wew", align_bytes=64)
         nc.sync.dma_start(
             wew[:].rearrange("p (e n) -> p e n", e=E),
             we_words.rearrange("e s p n d -> p (e s) (n d)").bitcast(I32),
         )
 
+        planes = [keep.tile([P, T], U32, name=f"plane{u}", align_bytes=64) for u in range(2)]
+        slot_words = {}
 
-        def gather_words(f, cuts):
+        def gather_words(f, h, s):
+            words = keep.tile([P, HALF], U32, name=f"slot_words{f}{h}{s}", align_bytes=64)
+            window = xw[:, s * T : (s + 1 if f == h == 0 else PASSES) * T].bitcast(U32)
+            nc.vector.tensor_copy(words[:], window.indirect(entries(token_of, f * C1 + h * HALF, HALF)))
+            slot_words[f, h, s] = words
+
+        def hidden_pairs(f, h, u, bank):
+            acc = psum.tile([P, 2, HALF], F32, name="acc", tag=f"bank{bank}")
             for s in range(PASSES):
-                slot_words[f, s] = keep.tile([P, C1], U32, name="words", tag=f"slot_words{f}{s}", align_bytes=64)
-            for s, first, width in cuts:
-                nc.vector.tensor_copy(
-                    slot_words[f, s][:, first : first + width],
-                    xw[:, s * T : (s + 1) * T].bitcast(U32).indirect(entries(token_of, f * C1 + first, width)),
-                )
-
-        def block_sums(f, b, bank):
-            acc = psum.tile([P, H], F32, name="acc", tag=f"bank{bank}")
-            cols = slice(b * P, (b + 1) * P)
-            for s in range(PASSES):
-                nc.tensor.matmul_mx(
-                    acc[:],
-                    lhsT=slot_words[f, s][:, cols].bitcast(FP8X4),
-                    lhsT_scale=slot_scales[s][:, f * C1 + b * P : f * C1 + (b + 1) * P],
-                    rhs=wgw[f][:, s * 2 * H : (s + 1) * 2 * H].bitcast(FP4X4),
-                    rhs_scale=wgs[:, (f * PASSES + s) * H : (f * PASSES + s + 1) * H],
-                    start=(s == 0),
-                    stop=(s == PASSES - 1),
-                )
-            return acc
-
-        def activate(f, b, acc):
-            h = keep.tile([P, H], BF16, name="h", tag=f"hidden{f}{b}", align_bytes=64)
+                for e in range(2):
+                    col = s * H + (2 * u + e) * P
+                    nc.tensor.matmul_mx(
+                        acc[:, e, :],
+                        lhsT=wgw[f][:, 2 * col : 2 * (col + P)].bitcast(FP4X4),
+                        lhsT_scale=wgs[f][:, col : col + P],
+                        rhs=slot_words[f, h, s][:].bitcast(FP8X4),
+                        rhs_scale=slot_scales[f][:, s * C1 + h * HALF : s * C1 + (h + 1) * HALF],
+                        start=(s == 0 and e == 0),
+                        stop=(s == PASSES - 1 and e == 1),
+                    )
+            first = f * C1 + h * HALF
             nc.scalar.activation(
-                h[:].rearrange("j (u p e) -> j u p e", u=2, e=2),
-                acc[:].rearrange("j (p u e) -> j u p e", u=2, e=2),
+                planes[u][:, first : first + HALF].bitcast(BF16).rearrange("p (j e) -> p j e", e=2),
+                acc[:].rearrange("p e j -> p j e"),
                 SILU,
             )
-            for u in range(2):
-                hidden[f, b, u] = h[:].bitcast(F32)[:, u * P : (u + 1) * P]
 
-        def activate_plane(f, b, u, acc):
-            h = keep.tile([P, H // 2], BF16, name="h", tag=f"hidden{f}{b}{u}", align_bytes=64)
-            nc.scalar.activation(
-                h[:].rearrange("j (p e) -> j p e", e=2),
-                acc[:].rearrange("j (p u e) -> j u p e", u=2, e=2)[:, u],
-                SILU,
+        for f in range(G):
+            for h in range(2):
+                for s in range(PASSES):
+                    gather_words(f, h, s)
+        for f in range(G):
+            for h in range(2):
+                for u in range(2):
+                    hidden_pairs(f, h, u, (4 * f + 2 * h + u) % 6)
+
+        windows = [keep.tile([P, T], F32, name=f"window{w}", align_bytes=64) for w in range(2)]
+        for window in windows:
+            nc.sync.dma_start(
+                window[:].rearrange("p (c j) -> p c j", j=P), zeros[:].unsqueeze(1).to_broadcast([P, T // P, P])
             )
-            hidden[f, b, u] = h[:].bitcast(F32)
+        picked, grouped = {}, {}
 
-        def turn_pairs(into, f, b, u):
-            nc.tensor.transpose(into, hidden[f, b, u], identity[:])
+        def pick(c, u):
+            low, high = PAIRS_AT[c]
+            picked[c] = ring[:, low : 2 * high - low].bitcast(U32).rearrange("p (u j) -> p u j", u=2)[:, :, 0:HALF]
+            window = planes[u][:, 0 : C1 if (c + 1) * HALF <= C1 else T]
+            nc.vector.tensor_copy(picked[c][:, u, :], window.indirect(entries(slot_of, c * HALF, HALF)))
 
-        def experts(y, first_expert, count, codes, scales):
-            for b in range(count):
-                e = first_expert + b
+        def weave(c):
+            grouped[c] = keep.tile([P, HALF, 2], U32, name="grouped", align_bytes=64)
+            nc.vector.tensor_copy(grouped[c][:].bitcast(I32), picked[c].rearrange("p u j -> p j u").bitcast(I32))
+
+        def results(c, banks):
+            codes = keep.tile([P, HALF], U32, name="codes", align_bytes=64)
+            scales = keep.tile([P, HALF], U8, name=f"scales{c}", align_bytes=64)
+            nc.vector.quantize_mx(
+                codes[:].bitcast(FP8X4), scales[:], grouped[c][:].rearrange("p j u -> p (j u)").bitcast(BF16)
+            )
+            width = HALF // len(banks)
+            sums = [psum.tile([P, width], F32, name="y", tag=f"bank{bank}") for bank in banks]
+            for b in range(HALF // C2):
+                e = c * HALF // C2 + b
+                at = b * C2 % width
                 nc.tensor.matmul_mx(
-                    y[:, b * C2 : (b + 1) * C2],
+                    sums[b * C2 // width][:, at : at + C2],
                     lhsT=wew[:, e * N : (e + 1) * N].bitcast(FP8X4),
                     lhsT_scale=wes[:, e * N : (e + 1) * N],
                     rhs=codes[:, b * C2 : (b + 1) * C2].bitcast(FP8X4),
@@ -180,105 +213,47 @@ def tile_moe_hie_silu_kernel(
                     start=True,
                     stop=True,
                 )
+            return sums
 
+        def scalar_places(first, y, window):
+            width = y.shape[1]
+            gated = keep.tile([P, width], F32, name=f"gated{first}", align_bytes=64)
+            nc.vector.tensor_tensor(gated[:], y, gate_of(first, width), MULT)
+            nc.scalar.activation(window[:].indirect(entries(column_of, first, width)), gated[:], COPY)
 
-        gather_words(0, [(s, b * P, P) for b in range(4) for s in range(PASSES)])
-        gather_words(1, [(0, 0, C1), (1, 0, PIECE), (1, PIECE, PIECE)])
-        for b in range(3):
-            activate(0, b, block_sums(0, b, b))
-        last_sums = block_sums(0, 3, 3)
-        for u in range(2):
-            activate_plane(0, 3, u, last_sums)
-
-        def turn_plane(f, start, u, blocks, bank):
-            turned = psum.tile([P, len(blocks) * P], F32, name="turned", tag=f"bank{bank}")
-            for n, b in enumerate(blocks):
-                turn_pairs(turned[:, n * P : (n + 1) * P], f, b, u)
-            nc.scalar.copy(planes[:, start + blocks[0] * P : start + (blocks[-1] + 1) * P], turned[:])
-
-        turn_plane(0, pair0, 0, range(3), 1)
-        turn_plane(0, pair0, 0, range(3, 4), 5)
-        turn_plane(0, pair1, 1, range(4), 2)
-        activate(1, 0, block_sums(1, 0, 3))
-
-        def weave(first, width, pairs, tag):
-            grouped = keep.tile([P, width, 2], U32, name="grouped", tag=tag, align_bytes=64)
-            nc.vector.tensor_copy(
-                grouped[:].bitcast(I32), pairs[:, :, first : first + width].rearrange("p u j -> p j u").bitcast(I32)
-            )
-            return grouped
-
-        def quantise(grouped, codes, scales):
-            nc.vector.quantize_mx(codes.bitcast(FP8X4), scales, grouped.rearrange("p j u -> p (j u)").bitcast(BF16))
-
-        picked0 = keep.tile([P, 2, C1], U32, name="picked0", align_bytes=64)
-        for u, start, first, width in ((0, pair0, 0, C1), (1, pair1, 0, PIECE), (1, pair1, PIECE, PIECE)):
-            window = planes[:, start : start + C1 + SPARE].bitcast(U32)
-            nc.vector.tensor_copy(picked0[:, u, first : first + width], window.indirect(entries(slot_of, first, width)))
-        for b, bank in ((1, 1), (2, 2)):
-            activate(1, b, block_sums(1, b, bank))
-        last_sums = block_sums(1, 3, 5)
-        activate_plane(1, 3, 0, last_sums)
-        turn_plane(1, pair2, 0, range(3), 1)
-        activate_plane(1, 3, 1, last_sums)
-
-        grouped0 = [weave(first, PIECE, picked0, f"grouped{first}") for first in (0, PIECE)]
-        codes0 = [keep.tile([P, PIECE], U32, name=f"codes0{h}", align_bytes=64) for h in range(2)]
-        scales0 = [keep.tile([P, PIECE], U8, name=f"scales0{h}", align_bytes=64) for h in range(2)]
-        for h in range(2):
-            quantise(grouped0[h][:], codes0[h][:], scales0[h][:])
-        turn_plane(1, pair2, 0, range(3, 4), 4)
-        turn_plane(1, pair3, 1, range(4), 2)
-
-        def results(first, quantised, bank):
-            y = psum.tile([P, PIECE], F32, name="y", tag=f"bank{bank}")
-            experts(y, first // C2, 2, *quantised)
-            return y
-
-        def pick(picked, start, u, first):
-            window = planes[:, start - C1 : start + C1].bitcast(U32)
-            nc.vector.tensor_copy(picked[:, u, :], window.indirect(entries(slot_of, first, PIECE)))
-
-        def quantised(grouped, name):
-            codes = keep.tile([P, PIECE], U32, name=f"codes{name}", align_bytes=64)
-            scales = keep.tile([P, PIECE], U8, name=f"scales{name}", align_bytes=64)
-            quantise(grouped[:], codes[:], scales[:])
-            return codes, scales
-
-        def apply_gate(gated, y, first):
-            nc.vector.tensor_tensor(gated, y, weight[:, first : first + y.shape[1]], MULT)
-
-        def scalar_places(first, width, gated):
-            nc.scalar.activation(by_scalar[:].indirect(entries(column_of, first, width)), gated, COPY)
-
-        def vector_places(first, width, gated):
+        def vector_places(first, staged):
+            width = staged.shape[1]
             nc.vector.tensor_tensor(
-                by_vector[:].indirect(entries(column_of, first, width)), gated, weight[:, first : first + width], MULT
+                windows[1][:].indirect(entries(column_of, first, width)), staged, gate_of(first, width), MULT
             )
 
-        early = keep.tile([P, 2, PIECE], U32, name="early", align_bytes=64)
-        pick(early, pair2, 0, C1)
-        gated0 = keep.tile([P, PIECE], F32, name="gated0", tag="hidden131", align_bytes=64)
-        apply_gate(gated0[:], results(0, (codes0[0], scales0[0]), 4)[:], 0)
-        scalar_places(0, PIECE, gated0[:])
-        pick(early, pair3, 1, C1)
-        gated1 = keep.tile([P, PIECE], F32, name="gated1", align_bytes=64)
-        apply_gate(gated1[:], results(PIECE, (codes0[1], scales0[1]), 2)[:], PIECE)
-        scalar_places(PIECE, PIECE, gated1[:])
-        late = keep.tile([P, 2, PIECE], U32, name="late", tag="codes01", align_bytes=64)
-        pick(late, pair2, 0, C1 + PIECE)
-        pick(late, pair3, 1, C1 + PIECE)
-        grouped = [weave(0, PIECE, early, "scales01"), weave(0, PIECE, late, "grouped11")]
-        halves = [quantised(grouped[h], f"1{h}") for h in range(2)]
-        last = keep.tile([P, C1], F32, name="last", align_bytes=64)
-        third, fourth = results(C1, halves[0], 7), results(C1 + PIECE, halves[1], 5)
-        apply_gate(last[:, 0:SHARE], third[:, 0:SHARE], C1)
-        scalar_places(C1, SHARE, last[:, 0:SHARE])
-        nc.vector.tensor_copy(last[:, SHARE:PIECE], third[:, SHARE:PIECE])
-        nc.vector.tensor_copy(last[:, PIECE:C1], fourth[:])
-        vector_places(C1 + SHARE, C1 - SHARE, last[:, SHARE:C1])
+        pick(0, 0)
+        pick(0, 1)
+        pick(1, 0)
+        weave(0)
+        pick(1, 1)
+        (y,) = results(0, (6,))
+        weave(1)
+        pick(2, 0)
+        scalar_places(0, y[:], windows[0])
+        (y,) = results(1, (7,))
+        pick(2, 1)
+        pick(3, 0)
+        weave(2)
+        scalar_places(HALF, y[:], windows[1])
+        (y,) = results(2, (6,))
+        pick(3, 1)
+        weave(3)
+        staged = keep.tile([P, HALF], F32, name="staged", align_bytes=64)
+        scalar_places(C1, y[:, 0:C2], windows[0])
+        nc.vector.tensor_copy(staged[:, 0:C2], y[:, C2:HALF])
+        seventh, eighth = results(3, (7, 5))
+        vector_places(C1 + C2, staged[:, 0:C2])
+        nc.scalar.copy(staged[:, C2:HALF], eighth[:])
+        scalar_places(C1 + HALF, seventh[:], windows[0])
+        vector_places(T - C2, staged[:, C2:HALF])
         for c, width in enumerate(STORES):
             cols = slice(sum(STORES[:c]), sum(STORES[: c + 1]))
             total = keep.tile([P, width], F32, name=f"total{c}", align_bytes=64)
-            nc.vector.tensor_tensor(total[:], by_scalar[:, cols], by_vector[:, cols], ADD)
+            nc.vector.tensor_tensor(total[:], windows[0][:, cols], windows[1][:, cols], ADD)
             nc.sync.dma_start(out[:, cols], total[:])

@@ -162,8 +162,8 @@ def tile_moe_hie_silu_kernel(
                     )
             first = f * C1 + h * HALF
             nc.scalar.activation(
-                planes[u][:, first : first + HALF].bitcast(BF16).rearrange("p (j e) -> p j e", e=2),
-                acc[:].rearrange("p e j -> p j e"),
+                planes[u][:, first : first + HALF].bitcast(BF16).rearrange("p (k i e) -> p k e i", i=4, e=2),
+                acc[:].rearrange("p e (k i) -> p k e i", i=4),
                 SILU,
             )
 

@@ -60,7 +60,7 @@ def tile_moe_hie_silu_kernel(
         nc.vector.memset(zeros[:], 0.0)
 
         def load_group_words(f):
-            words = keep.tile([P, PASSES * 2 * H], U8, name=f"wg_raw{f}", align_bytes=64)
+            words = keep.tile([P, PASSES * 2 * H], U8, name="wg_raw", tag=f"wg_raw{f}", align_bytes=64)
             nc.sync.dma_start(
                 words[:].bitcast(I32).rearrange("p (s b) -> p s b", s=PASSES),
                 wg_words[f].bitcast(I32).rearrange("s p b -> p s b"),
@@ -116,6 +116,10 @@ def tile_moe_hie_silu_kernel(
             )
         wgs = (wg_sorted, wg_lowered)
         wgw.append(sort_group_words(1, raw1))
+        windows = [keep.tile([P, T], F32, name="window", tag="wg_raw1", align_bytes=64)]
+        nc.scalar.copy(
+            windows[0][:].rearrange("p (c j) -> p c j", j=P), zeros[:].unsqueeze(1).to_broadcast([P, T // P, P])
+        )
         nc.sync.dma_start(slot_of[:], offs2)
         nc.sync.dma_start(column_of[:], dst)
         ring = keep.tile([P, GATE_AT + 2 * T], F32, name="ring", align_bytes=64)
@@ -141,7 +145,7 @@ def tile_moe_hie_silu_kernel(
         slot_words = {}
 
         def gather_words(f, h, s):
-            words = keep.tile([P, HALF], U32, name=f"slot_words{f}{h}{s}", align_bytes=64)
+            words = keep.tile([P, HALF], U32, name="slot_words", tag=f"slot_words{f}{h}{s}", align_bytes=64)
             window = xw[:, s * T : (s + 1 if f == h == 0 else PASSES) * T].bitcast(U32)
             nc.vector.tensor_copy(words[:], window.indirect(entries(token_of, f * C1 + h * HALF, HALF)))
             slot_words[f, h, s] = words
@@ -176,11 +180,8 @@ def tile_moe_hie_silu_kernel(
                 for u in range(2):
                     hidden_pairs(f, h, u, (4 * f + 2 * h + u) % 6)
 
-        windows = [keep.tile([P, T], F32, name=f"window{w}", align_bytes=64) for w in range(2)]
-        for window in windows:
-            nc.sync.dma_start(
-                window[:].rearrange("p (c j) -> p c j", j=P), zeros[:].unsqueeze(1).to_broadcast([P, T // P, P])
-            )
+        windows.append(keep.tile([P, T], F32, name="window", tag="slot_words111", align_bytes=64))
+        nc.scalar.copy(windows[1][:], windows[0][:])
         picked, grouped = {}, {}
 
         def pick(c, u):

@@ -77,8 +77,8 @@ def tile_moe_hie_silu_kernel(
             for s in range(PASSES):
                 cols = slice(s * 2 * H, (s + 1) * 2 * H)
                 nc.scalar.copy(
-                    words[:, cols].bitcast(U16).rearrange("p (t m) -> p t m", t=4),
-                    raw[:, cols].bitcast(U16).rearrange("p (m t) -> p t m", t=4),
+                    words[:, cols].bitcast(U16).rearrange("p (t k i) -> p k t i", t=4, i=8),
+                    raw[:, cols].bitcast(U16).rearrange("p (k i t) -> p k t i", t=4, i=8),
                 )
             return words
 
@@ -99,15 +99,19 @@ def tile_moe_hie_silu_kernel(
             queue = nc.sync if r % 2 else nc.scalar
             queue.dma_start(wg_rows[r:P:DROP, :].bitcast(I32), group_rows[r])
         load_token_words(0)
-        raw1 = load_group_words(1)
         load_token_words(1)
         wgw = [sort_group_words(0, raw0)]
+        windows = [keep.tile([P, T], F32, name="window", tag="wg_raw0", align_bytes=64)]
+        nc.scalar.copy(
+            windows[0][:].rearrange("p (c j) -> p c j", j=P), zeros[:].unsqueeze(1).to_broadcast([P, T // P, P])
+        )
         gather_scales(0, nc.sync)
+        raw1 = load_group_words(1)
         gather_scales(1, nc.sync)
         wg_sorted = keep.tile([P, PASSES * H], U8, name="wg_sorted", align_bytes=64)
         nc.vector.tensor_copy(
-            wg_sorted[:].rearrange("p (s t m) -> p s t m", s=PASSES, t=4),
-            wg_rows[:].rearrange("p (s m t) -> p s t m", s=PASSES, t=4),
+            wg_sorted[:].rearrange("p (s t k i) -> p s k t i", s=PASSES, t=4, i=16),
+            wg_rows[:].rearrange("p (s k i t) -> p s k t i", s=PASSES, t=4, i=16),
         )
         for row, count in ((0, 64), (64, 32), (96, 4)):
             nc.sync.dma_start(
@@ -116,10 +120,6 @@ def tile_moe_hie_silu_kernel(
             )
         wgs = (wg_sorted, wg_lowered)
         wgw.append(sort_group_words(1, raw1))
-        windows = [keep.tile([P, T], F32, name="window", tag="wg_raw1", align_bytes=64)]
-        nc.scalar.copy(
-            windows[0][:].rearrange("p (c j) -> p c j", j=P), zeros[:].unsqueeze(1).to_broadcast([P, T // P, P])
-        )
         nc.sync.dma_start(slot_of[:], offs2)
         nc.sync.dma_start(column_of[:], dst)
         ring = keep.tile([P, GATE_AT + 2 * T], F32, name="ring", align_bytes=64)

@@ -51,13 +51,13 @@ def tile_moe_hie_silu_kernel(
         wg_lowered = keep.tile([P, PASSES * H], U8, name="wg_lowered", align_bytes=64)
         slot_scales = [keep.tile([P, PASSES * C1], U8, name=f"slot_scales{f}", align_bytes=64) for f in range(G)]
         wes = keep.tile([P, E * N], U8, name="wes", align_bytes=64)
+        zeros = keep.tile([P, P], F32, name="zeros", align_bytes=64)
         nc.vector.memset(wg_rows[:].bitcast(I32), 0)
+        nc.vector.memset(zeros[:], 0.0)
         nc.vector.memset(xs[32:64, :].bitcast(I32), 0)
         nc.vector.memset(xs[64:P, :].bitcast(I32), 0)
         for plane in (*slot_scales, wg_lowered, wes):
             nc.vector.memset(plane[:].bitcast(I32), 0)
-        zeros = keep.tile([P, P], F32, name="zeros", align_bytes=64)
-        nc.vector.memset(zeros[:], 0.0)
 
         def load_group_words(f):
             words = keep.tile([P, PASSES * 2 * H], U8, name="wg_raw", tag=f"wg_raw{f}", align_bytes=64)
@@ -96,17 +96,18 @@ def tile_moe_hie_silu_kernel(
         raw0 = load_group_words(0)
         group_rows = wg_scales.bitcast(I32).rearrange("f s (q r) w -> r q (f s) w", r=4)
         for r in range(4):
-            queue = nc.sync if r % 2 else nc.scalar
-            queue.dma_start(wg_rows[r:P:DROP, :].bitcast(I32), group_rows[r])
+            nc.sync.dma_start(wg_rows[r:P:DROP, :].bitcast(I32), group_rows[r])
         load_token_words(0)
-        load_token_words(1)
-        wgw = [sort_group_words(0, raw0)]
-        windows = [keep.tile([P, T], F32, name="window", tag="wg_raw0", align_bytes=64)]
-        nc.scalar.copy(
-            windows[0][:].rearrange("p (c j) -> p c j", j=P), zeros[:].unsqueeze(1).to_broadcast([P, T // P, P])
-        )
-        gather_scales(0, nc.sync)
         raw1 = load_group_words(1)
+        load_token_words(1)
+        windows = [keep.tile([P, T], F32, name="window", align_bytes=64)]
+        nc.scalar.activation(
+            windows[0][:].rearrange("p (c j) -> p c j", j=P), zeros[:].unsqueeze(1).to_broadcast([P, T // P, P]), SILU
+        )
+        wgw = [sort_group_words(0, raw0)]
+        windows.append(keep.tile([P, T], F32, name="window", tag="wg_raw0", align_bytes=64))
+        nc.scalar.copy(windows[1][:], windows[0][:])
+        gather_scales(0, nc.sync)
         gather_scales(1, nc.sync)
         wg_sorted = keep.tile([P, PASSES * H], U8, name="wg_sorted", align_bytes=64)
         nc.vector.tensor_copy(
@@ -141,7 +142,7 @@ def tile_moe_hie_silu_kernel(
             we_words.rearrange("e s p n d -> p (e s) (n d)").bitcast(I32),
         )
 
-        planes = [keep.tile([P, T], U32, name=f"plane{u}", align_bytes=64) for u in range(2)]
+        planes = [keep.tile([P, T], U32, name="plane", tag=tag, align_bytes=64) for tag in ("wg_raw1", "plane1")]
         slot_words = {}
 
         def gather_words(f, h, s):
@@ -180,8 +181,6 @@ def tile_moe_hie_silu_kernel(
                 for u in range(2):
                     hidden_pairs(f, h, u, (4 * f + 2 * h + u) % 6)
 
-        windows.append(keep.tile([P, T], F32, name="window", tag="slot_words111", align_bytes=64))
-        nc.scalar.copy(windows[1][:], windows[0][:])
         picked, grouped = {}, {}
 
         def pick(c, u):
@@ -191,8 +190,11 @@ def tile_moe_hie_silu_kernel(
             nc.vector.tensor_copy(picked[c][:, u, :], window.indirect(entries(slot_of, c * HALF, HALF)))
 
         def weave(c):
-            grouped[c] = keep.tile([P, HALF, 2], U32, name="grouped", align_bytes=64)
-            nc.vector.tensor_copy(grouped[c][:].bitcast(I32), picked[c].rearrange("p u j -> p j u").bitcast(I32))
+            grouped[c] = keep.tile([P, HALF, 2], U32, name="grouped", tag="slot_words111" if c == 1 else "grouped", align_bytes=64)
+            if c == 1:
+                nc.scalar.copy(grouped[c][:], picked[c].rearrange("p u j -> p j u"))
+            else:
+                nc.vector.tensor_copy(grouped[c][:].bitcast(I32), picked[c].rearrange("p u j -> p j u").bitcast(I32))
 
         def results(c, banks):
             codes = keep.tile([P, HALF], U32, name="codes", align_bytes=64)

@@ -96,18 +96,19 @@ def tile_moe_hie_silu_kernel(
         raw0 = load_group_words(0)
         group_rows = wg_scales.bitcast(I32).rearrange("f s (q r) w -> r q (f s) w", r=4)
         for r in range(4):
-            nc.sync.dma_start(wg_rows[r:P:DROP, :].bitcast(I32), group_rows[r])
+            queue = nc.sync if r % 2 else nc.scalar
+            queue.dma_start(wg_rows[r:P:DROP, :].bitcast(I32), group_rows[r])
         load_token_words(0)
-        raw1 = load_group_words(1)
         load_token_words(1)
+        raw1 = load_group_words(1)
         windows = [keep.tile([P, T], F32, name="window", align_bytes=64)]
         nc.scalar.activation(
             windows[0][:].rearrange("p (c j) -> p c j", j=P), zeros[:].unsqueeze(1).to_broadcast([P, T // P, P]), SILU
         )
+        gather_scales(0, nc.scalar)
         wgw = [sort_group_words(0, raw0)]
         windows.append(keep.tile([P, T], F32, name="window", tag="wg_raw0", align_bytes=64))
         nc.scalar.copy(windows[1][:], windows[0][:])
-        gather_scales(0, nc.sync)
         gather_scales(1, nc.sync)
         wg_sorted = keep.tile([P, PASSES * H], U8, name="wg_sorted", align_bytes=64)
         nc.vector.tensor_copy(

@@ -48,15 +48,14 @@ def tile_moe_hie_silu_kernel(
 
         xs = keep.tile([P, T], U8, name="xs", align_bytes=64)
         wg_rows = keep.tile([P, PASSES * H], U8, name="wg_rows", align_bytes=64)
-        wg_lowered = keep.tile([P, PASSES * H], U8, name="wg_lowered", align_bytes=64)
-        slot_scales = [keep.tile([P, PASSES * C1], U8, name=f"slot_scales{f}", align_bytes=64) for f in range(G)]
-        wes = keep.tile([P, E * N], U8, name="wes", align_bytes=64)
+        spread = keep.tile([P, G * PASSES * C1], U8, name="spread", align_bytes=64)
+        slot_scales = [spread[:, f * PASSES * C1 : (f + 1) * PASSES * C1] for f in range(G)]
         zeros = keep.tile([P, P], F32, name="zeros", align_bytes=64)
         nc.vector.memset(wg_rows[:].bitcast(I32), 0)
         nc.vector.memset(zeros[:], 0.0)
-        nc.vector.memset(xs[32:64, :].bitcast(I32), 0)
-        nc.vector.memset(xs[64:P, :].bitcast(I32), 0)
-        for plane in (*slot_scales, wg_lowered, wes):
+        nc.vector.memset(xs[0:96, :].bitcast(I32), 0)
+        wg_lowered = keep.tile([P, PASSES * H], U8, name="wg_lowered", align_bytes=64)
+        for plane in (spread, wg_lowered):
             nc.vector.memset(plane[:].bitcast(I32), 0)
 
         def load_group_words(f):
@@ -73,7 +72,7 @@ def tile_moe_hie_silu_kernel(
             nc.sync.dma_start(xw[:, s * T : (s + 1) * T], x_words[s].rearrange("p t d -> p (t d)").bitcast(I32))
 
         def sort_group_words(f, raw):
-            words = keep.tile([P, PASSES * 2 * H], U8, name=f"wgw{f}", align_bytes=64)
+            words = keep.tile([P, PASSES * 2 * H], U8, name="wgw", tag=f"wgw{f}", align_bytes=64)
             for s in range(PASSES):
                 cols = slice(s * 2 * H, (s + 1) * 2 * H)
                 nc.scalar.copy(
@@ -83,16 +82,16 @@ def tile_moe_hie_silu_kernel(
             return words
 
         def gather_scales(f, queue):
-            picked = keep.tile([P, C1], U8, name=f"picked_scales{f}", align_bytes=64)
+            picked = keep.tile([P, C1], U8, name="picked_scales", tag=f"picked_scales{f}", align_bytes=64)
             nc.vector.tensor_copy(picked[:], xs[:].indirect(entries(token_of, f * C1, C1)))
             for q in range(QUADRANTS):
                 queue.dma_start(
                     slot_scales[f][32 * q : 32 * q + 4, :].bitcast(I32).rearrange("r (s w) -> r s w", s=PASSES),
-                    picked[8 * q : 8 * (q + 1), :].bitcast(I32),
+                    picked[96 + 8 * q : 96 + 8 * (q + 1), :].bitcast(I32),
                 )
 
         nc.sync.dma_start(token_of[:], offs)
-        nc.scalar.dma_start(xs[0:32, :].bitcast(I32), x_scales.bitcast(I32).rearrange("s b w -> b s w"))
+        nc.scalar.dma_start(xs[96:P, :].bitcast(I32), x_scales.bitcast(I32).rearrange("s b w -> b s w"))
         raw0 = load_group_words(0)
         group_rows = wg_scales.bitcast(I32).rearrange("f s (q r) w -> r q (f s) w", r=4)
         for r in range(4):
@@ -102,13 +101,15 @@ def tile_moe_hie_silu_kernel(
         load_token_words(1)
         raw1 = load_group_words(1)
         windows = [keep.tile([P, T], F32, name="window", align_bytes=64)]
-        nc.scalar.activation(
-            windows[0][:].rearrange("p (c j) -> p c j", j=P), zeros[:].unsqueeze(1).to_broadcast([P, T // P, P]), SILU
-        )
+        nc.scalar.activation(windows[0][:, 0:P], zeros[:], SILU)
+        wes = keep.tile([P, E * N], U8, name="wes", tag="zeros", align_bytes=64)
+        nc.gpsimd.memset(wes[:].bitcast(I32), 0)
         gather_scales(0, nc.scalar)
         wgw = [sort_group_words(0, raw0)]
-        windows.append(keep.tile([P, T], F32, name="window", tag="wg_raw0", align_bytes=64))
-        nc.scalar.copy(windows[1][:], windows[0][:])
+        nc.scalar.copy(
+            windows[0][:, P:T].rearrange("p (c j) -> p c j", j=P),
+            wes[:].bitcast(F32)[:, 0:P].unsqueeze(1).to_broadcast([P, T // P - 1, P]),
+        )
         gather_scales(1, nc.sync)
         wg_sorted = keep.tile([P, PASSES * H], U8, name="wg_sorted", align_bytes=64)
         nc.vector.tensor_copy(
@@ -182,6 +183,8 @@ def tile_moe_hie_silu_kernel(
                 for u in range(2):
                     hidden_pairs(f, h, u, (4 * f + 2 * h + u) % 6)
 
+        windows.append(keep.tile([P, T], F32, name="window", tag="wgw1", align_bytes=64))
+        nc.scalar.copy(windows[1][:], windows[0][:])
         picked, grouped = {}, {}
 
         def pick(c, u):

@@ -149,24 +149,24 @@ def tile_moe_hie_silu_kernel(
 
         def gather_words(f, h, s):
             words = keep.tile([P, HALF], U32, name="slot_words", tag=f"slot_words{f}{h}{s}", align_bytes=64)
-            window = xw[:, s * T : (s + 1 if f == h == 0 else PASSES) * T].bitcast(U32)
+            window = xw[:, s * T : (s + 1 if f == 0 else PASSES) * T].bitcast(U32)
             nc.vector.tensor_copy(words[:], window.indirect(entries(token_of, f * C1 + h * HALF, HALF)))
             slot_words[f, h, s] = words
 
-        def hidden_pairs(f, h, u, bank):
-            acc = psum.tile([P, 2, HALF], F32, name="acc", tag=f"bank{bank}")
-            for s in range(PASSES):
-                for e in range(2):
-                    col = s * H + (2 * u + e) * P
-                    nc.tensor.matmul_mx(
-                        acc[:, e, :],
-                        lhsT=wgw[f][:, 2 * col : 2 * (col + P)].bitcast(FP4X4),
-                        lhsT_scale=wgs[f][:, col : col + P],
-                        rhs=slot_words[f, h, s][:].bitcast(FP8X4),
-                        rhs_scale=slot_scales[f][:, s * C1 + h * HALF : s * C1 + (h + 1) * HALF],
-                        start=(s == 0 and e == 0),
-                        stop=(s == PASSES - 1 and e == 1),
-                    )
+        def products(acc, f, h, u, s):
+            for e in range(2):
+                col = s * H + (2 * u + e) * P
+                nc.tensor.matmul_mx(
+                    acc[:, e, :],
+                    lhsT=wgw[f][:, 2 * col : 2 * (col + P)].bitcast(FP4X4),
+                    lhsT_scale=wgs[f][:, col : col + P],
+                    rhs=slot_words[f, h, s][:].bitcast(FP8X4),
+                    rhs_scale=slot_scales[f][:, s * C1 + h * HALF : s * C1 + (h + 1) * HALF],
+                    start=(s == 0 and e == 0),
+                    stop=(s == PASSES - 1 and e == 1),
+                )
+
+        def activate(acc, f, h, u):
             first = f * C1 + h * HALF
             nc.scalar.activation(
                 planes[u][:, first : first + HALF].bitcast(BF16).rearrange("p (k i e) -> p k e i", i=4, e=2),
@@ -174,14 +174,23 @@ def tile_moe_hie_silu_kernel(
                 SILU,
             )
 
+        for s in range(PASSES):
+            for h in range(2):
+                gather_words(0, h, s)
+        for h in range(2):
+            for s in range(PASSES):
+                gather_words(1, h, s)
         for f in range(G):
             for h in range(2):
-                for s in range(PASSES):
-                    gather_words(f, h, s)
-        for f in range(G):
-            for h in range(2):
-                for u in range(2):
-                    hidden_pairs(f, h, u, (4 * f + 2 * h + u) % 6)
+                sums = [psum.tile([P, 2, HALF], F32, name="acc", tag=f"bank{(4 * f + 2 * h + u) % 6}") for u in range(2)]
+                if f == h == 0:
+                    steps = [(u, s) for s in range(PASSES) for u in range(2)]
+                else:
+                    steps = [(u, s) for u in range(2) for s in range(PASSES)]
+                for u, s in steps:
+                    products(sums[u], f, h, u, s)
+                    if s == PASSES - 1:
+                        activate(sums[u], f, h, u)
 
         windows.append(keep.tile([P, T], F32, name="window", tag="wgw1", align_bytes=64))
         nc.scalar.copy(windows[1][:], windows[0][:])

@@ -192,8 +192,6 @@ def tile_moe_hie_silu_kernel(
                     if s == PASSES - 1:
                         activate(sums[u], f, h, u)
 
-        windows.append(keep.tile([P, T], F32, name="window", tag="wgw1", align_bytes=64))
-        nc.scalar.copy(windows[1][:], windows[0][:])
         picked, grouped = {}, {}
 
         def pick(c, u):
@@ -250,6 +248,8 @@ def tile_moe_hie_silu_kernel(
         pick(1, 1)
         (y,) = results(0, (6,))
         weave(1)
+        windows.append(keep.tile([P, T], F32, name="window", tag="wgw1", align_bytes=64))
+        nc.scalar.copy(windows[1][:], windows[0][:])
         pick(2, 0)
         scalar_places(0, y[:], windows[0])
         (y,) = results(1, (7,))

from contextlib import ExitStack

import concourse.mybir as mybir

K, T, G, C1, E, C2, H, N = 1024, 1024, 2, 512, 8, 128, 512, 128
FLOPS = 2 * K * H * T + 2 * H * N * T

F32 = mybir.dt.float32
BF16 = mybir.dt.bfloat16
I32 = mybir.dt.int32
U32 = mybir.dt.uint32
U16 = mybir.dt.uint16
U8 = mybir.dt.uint8
FP8X4 = mybir.dt.float8_e4m3fn_x4
FP4X4 = mybir.dt.float4_e2m1fn_x4
SILU = mybir.ActivationFunctionType.Silu
COPY = mybir.ActivationFunctionType.Copy
MULT = mybir.AluOpType.mult
ADD = mybir.AluOpType.add

P = 128
PASSES = K // 512
HALF = 256
LANES = 16
QUADRANTS = 4
DROP = 16
GATE_AT = 1216
PAIRS_AT = ((0, 512), (256, 768), (0, 1024), (1280, 1728))
STORES = (320, 320, 256, 128)


def entries(offsets, first, count):
    return offsets[:, first // LANES : (first + count) // LANES]


def tile_moe_hie_silu_kernel(
    tc, x_words, x_scales, wg_words, wg_scales, we_words, we_scales, gate, offs, offs2, dst, out
):
    nc = tc.nc
    with ExitStack() as ctx:
        lists = ctx.enter_context(tc.tile_pool(name="lists", bufs=1))
        keep = ctx.enter_context(tc.tile_pool(name="keep", bufs=1))
        psum = ctx.enter_context(tc.psum_pool(name="psum", bufs=1))

        token_of = lists.tile([P, T // LANES], U16, name="token_of")
        slot_of = lists.tile([P, T // LANES], U16, name="slot_of")
        column_of = lists.tile([P, T // LANES], U16, name="column_of")

        xs = keep.tile([P, T], U8, name="xs", align_bytes=64)
        wg_rows = keep.tile([P, PASSES * H], U8, name="wg_rows", align_bytes=64)
        spread = keep.tile([P, G * PASSES * C1], U8, name="spread", align_bytes=64)
        slot_scales = [spread[:, f * PASSES * C1 : (f + 1) * PASSES * C1] for f in range(G)]
        zeros = keep.tile([P, P], F32, name="zeros", align_bytes=64)
        nc.vector.memset(wg_rows[:].bitcast(I32), 0)
        nc.vector.memset(zeros[:], 0.0)
        nc.vector.memset(xs[0:96, :].bitcast(I32), 0)
        wg_lowered = keep.tile([P, PASSES * H], U8, name="wg_lowered", align_bytes=64)
        for plane in (spread, wg_lowered):
            nc.vector.memset(plane[:].bitcast(I32), 0)

        def load_group_words(f):
            words = keep.tile([P, PASSES * 2 * H], U8, name="wg_raw", tag=f"wg_raw{f}", align_bytes=64)
            nc.sync.dma_start(
                words[:].bitcast(I32).rearrange("p (s b) -> p s b", s=PASSES),
                wg_words[f].bitcast(I32).rearrange("s p b -> p s b"),
            )
            return words

        xw = keep.tile([P, PASSES * T], I32, name="xw", align_bytes=64)

        def load_token_words(s):
            nc.sync.dma_start(xw[:, s * T : (s + 1) * T], x_words[s].rearrange("p t d -> p (t d)").bitcast(I32))

        def sort_group_words(f, raw):
            words = keep.tile([P, PASSES * 2 * H], U8, name="wgw", tag=f"wgw{f}", align_bytes=64)
            for s in range(PASSES):
                cols = slice(s * 2 * H, (s + 1) * 2 * H)
                nc.scalar.copy(
                    words[:, cols].bitcast(U16).rearrange("p (t k i) -> p k t i", t=4, i=8),
                    raw[:, cols].bitcast(U16).rearrange("p (k i t) -> p k t i", t=4, i=8),
                )
            return words

        def gather_scales(f, queue):
            picked = keep.tile([P, C1], U8, name="picked_scales", tag=f"picked_scales{f}", align_bytes=64)
            nc.vector.tensor_copy(picked[:], xs[:].indirect(entries(token_of, f * C1, C1)))
            for q in range(QUADRANTS):
                queue.dma_start(
                    slot_scales[f][32 * q : 32 * q + 4, :].bitcast(I32).rearrange("r (s w) -> r s w", s=PASSES),
                    picked[96 + 8 * q : 96 + 8 * (q + 1), :].bitcast(I32),
                )

        nc.sync.dma_start(token_of[:], offs)
        nc.scalar.dma_start(xs[96:P, :].bitcast(I32), x_scales.bitcast(I32).rearrange("s b w -> b s w"))
        raw0 = load_group_words(0)
        group_rows = wg_scales.bitcast(I32).rearrange("f s (q r) w -> r q (f s) w", r=4)
        for r in range(4):
            queue = nc.sync if r % 2 else nc.scalar
            queue.dma_start(wg_rows[r:P:DROP, :].bitcast(I32), group_rows[r])
        load_token_words(0)
        load_token_words(1)
        raw1 = load_group_words(1)
        windows = [keep.tile([P, T], F32, name="window", align_bytes=64)]
        nc.scalar.activation(windows[0][:, 0:P], zeros[:], SILU)
        wes = keep.tile([P, E * N], U8, name="wes", tag="zeros", align_bytes=64)
        nc.gpsimd.memset(wes[:].bitcast(I32), 0)
        gather_scales(0, nc.scalar)
        wgw = [sort_group_words(0, raw0)]
        nc.scalar.copy(
            windows[0][:, P:T].rearrange("p (c j) -> p c j", j=P),
            wes[:].bitcast(F32)[:, 0:P].unsqueeze(1).to_broadcast([P, T // P - 1, P]),
        )
        gather_scales(1, nc.sync)
        wg_sorted = keep.tile([P, PASSES * H], U8, name="wg_sorted", align_bytes=64)
        nc.vector.tensor_copy(
            wg_sorted[:].rearrange("p (s t k i) -> p s k t i", s=PASSES, t=4, i=16),
            wg_rows[:].rearrange("p (s k i t) -> p s k t i", s=PASSES, t=4, i=16),
        )
        for row, count in ((0, 64), (64, 32), (96, 4)):
            nc.sync.dma_start(
                wg_lowered[row : row + count, :].bitcast(I32),
                wg_sorted[row + DROP : row + DROP + count, :].bitcast(I32),
            )
        wgs = (wg_sorted, wg_lowered)
        wgw.append(sort_group_words(1, raw1))
        nc.sync.dma_start(slot_of[:], offs2)
        nc.sync.dma_start(column_of[:], dst)
        ring = keep.tile([P, GATE_AT + 2 * T], F32, name="ring", align_bytes=64)
        weight = ring[:, GATE_AT:].rearrange("p (c j) -> p c j", j=2 * HALF)[:, :, 0:HALF]
        nc.sync.dma_start(weight, gate.rearrange("p (c j) -> p c j", j=HALF))

        def gate_of(first, width):
            return weight[:, first // HALF, first % HALF : first % HALF + width]

        expert_rows = we_scales.rearrange("e s r n -> (e s) r n")
        for q in range(QUADRANTS):
            nc.sync.dma_start(
                wes[32 * q : 32 * q + 4, :].bitcast(I32).rearrange("r (c w) -> r c w", c=E),
                expert_rows[:, 4 * q : 4 * q + 4, :].bitcast(I32).rearrange("c r w -> r c w"),
            )
        wew = keep.tile([P, E * N], I32, name="wew", align_bytes=64)
        nc.sync.dma_start(
            wew[:].rearrange("p (e n) -> p e n", e=E),
            we_words.rearrange("e s p n d -> p (e s) (n d)").bitcast(I32),
        )

        planes = [keep.tile([P, T], U32, name="plane", tag=tag, align_bytes=64) for tag in ("wg_raw1", "plane1")]
        slot_words = {}

        def gather_words(f, h, s):
            words = keep.tile([P, HALF], U32, name="slot_words", tag=f"slot_words{f}{h}{s}", align_bytes=64)
            window = xw[:, s * T : (s + 1 if f == 0 else PASSES) * T].bitcast(U32)
            nc.vector.tensor_copy(words[:], window.indirect(entries(token_of, f * C1 + h * HALF, HALF)))
            slot_words[f, h, s] = words

        def products(acc, f, h, u, s):
            for e in range(2):
                col = s * H + (2 * u + e) * P
                nc.tensor.matmul_mx(
                    acc[:, e, :],
                    lhsT=wgw[f][:, 2 * col : 2 * (col + P)].bitcast(FP4X4),
                    lhsT_scale=wgs[f][:, col : col + P],
                    rhs=slot_words[f, h, s][:].bitcast(FP8X4),
                    rhs_scale=slot_scales[f][:, s * C1 + h * HALF : s * C1 + (h + 1) * HALF],
                    start=(s == 0 and e == 0),
                    stop=(s == PASSES - 1 and e == 1),
                )

        def activate(acc, f, h, u):
            first = f * C1 + h * HALF
            nc.scalar.activation(
                planes[u][:, first : first + HALF].bitcast(BF16).rearrange("p (k i e) -> p k e i", i=4, e=2),
                acc[:].rearrange("p e (k i) -> p k e i", i=4),
                SILU,
            )

        for s in range(PASSES):
            for h in range(2):
                gather_words(0, h, s)
        for h in range(2):
            for s in range(PASSES):
                gather_words(1, h, s)
        for f in range(G):
            for h in range(2):
                sums = [psum.tile([P, 2, HALF], F32, name="acc", tag=f"bank{(4 * f + 2 * h + u) % 6}") for u in range(2)]
                if f == h == 0:
                    steps = [(u, s) for s in range(PASSES) for u in range(2)]
                else:
                    steps = [(u, s) for u in range(2) for s in range(PASSES)]
                for u, s in steps:
                    products(sums[u], f, h, u, s)
                    if s == PASSES - 1:
                        activate(sums[u], f, h, u)

        picked, grouped = {}, {}

        def pick(c, u):
            low, high = PAIRS_AT[c]
            picked[c] = ring[:, low : 2 * high - low].bitcast(U32).rearrange("p (u j) -> p u j", u=2)[:, :, 0:HALF]
            window = planes[u][:, 0 : C1 if (c + 1) * HALF <= C1 else T]
            nc.vector.tensor_copy(picked[c][:, u, :], window.indirect(entries(slot_of, c * HALF, HALF)))

        def weave(c):
            grouped[c] = keep.tile([P, HALF, 2], U32, name="grouped", tag="slot_words111" if c == 1 else "grouped", align_bytes=64)
            if c == 1:
                nc.scalar.copy(grouped[c][:], picked[c].rearrange("p u j -> p j u"))
            else:
                nc.vector.tensor_copy(grouped[c][:].bitcast(I32), picked[c].rearrange("p u j -> p j u").bitcast(I32))

        def results(c, banks):
            codes = keep.tile([P, HALF], U32, name="codes", align_bytes=64)
            scales = keep.tile([P, HALF], U8, name=f"scales{c}", align_bytes=64)
            nc.vector.quantize_mx(
                codes[:].bitcast(FP8X4), scales[:], grouped[c][:].rearrange("p j u -> p (j u)").bitcast(BF16)
            )
            width = HALF // len(banks)
            sums = [psum.tile([P, width], F32, name="y", tag=f"bank{bank}") for bank in banks]
            for b in range(HALF // C2):
                e = c * HALF // C2 + b
                at = b * C2 % width
                nc.tensor.matmul_mx(
                    sums[b * C2 // width][:, at : at + C2],
                    lhsT=wew[:, e * N : (e + 1) * N].bitcast(FP8X4),
                    lhsT_scale=wes[:, e * N : (e + 1) * N],
                    rhs=codes[:, b * C2 : (b + 1) * C2].bitcast(FP8X4),
                    rhs_scale=scales[:, b * C2 : (b + 1) * C2],
                    start=True,
                    stop=True,
                )
            return sums

        def scalar_places(first, y, window):
            width = y.shape[1]
            gated = keep.tile([P, width], F32, name=f"gated{first}", align_bytes=64)
            nc.vector.tensor_tensor(gated[:], y, gate_of(first, width), MULT)
            nc.scalar.activation(window[:].indirect(entries(column_of, first, width)), gated[:], COPY)

        def vector_places(first, staged):
            width = staged.shape[1]
            nc.vector.tensor_tensor(
                windows[1][:].indirect(entries(column_of, first, width)), staged, gate_of(first, width), MULT
            )

        pick(0, 0)
        pick(0, 1)
        pick(1, 0)
        weave(0)
        pick(1, 1)
        (y,) = results(0, (6,))
        weave(1)
        windows.append(keep.tile([P, T], F32, name="window", tag="wgw1", align_bytes=64))
        nc.scalar.copy(windows[1][:], windows[0][:])
        pick(2, 0)
        scalar_places(0, y[:], windows[0])
        (y,) = results(1, (7,))
        pick(2, 1)
        pick(3, 0)
        weave(2)
        scalar_places(HALF, y[:], windows[1])
        (y,) = results(2, (6,))
        pick(3, 1)
        weave(3)
        staged = keep.tile([P, HALF], F32, name="staged", align_bytes=64)
        scalar_places(C1, y[:, 0:C2], windows[0])
        nc.vector.tensor_copy(staged[:, 0:C2], y[:, C2:HALF])
        seventh, eighth = results(3, (7, 5))
        vector_places(C1 + C2, staged[:, 0:C2])
        nc.scalar.copy(staged[:, C2:HALF], eighth[:])
        scalar_places(C1 + HALF, seventh[:], windows[0])
        vector_places(T - C2, staged[:, C2:HALF])
        for c, width in enumerate(STORES):
            cols = slice(sum(STORES[:c]), sum(STORES[: c + 1]))
            total = keep.tile([P, width], F32, name=f"total{c}", align_bytes=64)
            nc.vector.tensor_tensor(total[:], windows[0][:, cols], windows[1][:, cols], ADD)
            nc.sync.dma_start(out[:, cols], total[:])
